import numpy as np
import ml_dtypes


def mxq(x, axis, fmt="e4m3"):
    dtype, down = {"e4m3": (ml_dtypes.float8_e4m3fn, 7), "e5m2": (ml_dtypes.float8_e5m2, 14)}[fmt]
    v = np.moveaxis(np.asarray(x, np.float32).astype(ml_dtypes.bfloat16).astype(np.float64), axis, -1)
    blocks = v.reshape(v.shape[:-1] + (-1, 32))
    amax = np.abs(blocks).max(-1, keepdims=True)
    byte = np.maximum(np.where(amax > 0, np.frexp(amax)[1] - 1 + 127, 0) - down, 1)
    scale = np.exp2(byte - 127.0)
    codes = (blocks / scale).astype(np.float32).astype(dtype).astype(np.float64)
    return np.moveaxis((codes * scale).reshape(v.shape), -1, axis)


WIDE = False


def mx_kscale(k):
    if not WIDE:
        return np.ones(k)
    levels = np.array([10, -10, 5, -5, 0])
    if k % 512:
        return np.exp2(np.random.permutation(np.resize(levels, k // 32))).repeat(32)
    a = np.empty((k // 512, 16))
    for p in range(k // 512):
        a[p, :8] = np.random.permutation(np.resize(levels, 8))
        for g in range(8):
            far = levels[np.abs(levels - a[p, g]) >= 10]
            a[p, g + 8] = far[np.random.randint(len(far))]
    return np.exp2(a.ravel()).repeat(32)


def f64(x):
    return np.asarray(x).astype(np.float64)


def striped(idx):
    return np.tile(idx.reshape(-1, 16).T, (8, 1)).astype(np.uint16)


def unstriped(offs):
    return offs[:16].T.reshape(-1).astype(np.int64)


E2M1 = np.array([0.0, 0.5, 1.0, 1.5, 2.0, 3.0, 4.0, 6.0, -0.0, -0.5, -1.0, -1.5, -2.0, -3.0, -4.0, -6.0])


def pack_weight(w, fmt):
    k, n = w.shape
    w = f64(np.asarray(w, np.float32).astype(ml_dtypes.bfloat16)).reshape(k // 32, 32, n)
    amax = np.abs(w).max(1)
    if fmt == "e4m3":
        byte = np.frexp(amax)[1] - 1 + 127 - 7
    else:
        mant, ex = np.frexp(amax / 6.0)
        byte = np.where(mant > 0.5, ex, ex - 1) + 127
    byte = np.clip(np.where(amax > 0, byte, 1), 1, 254)
    scaled = (w * np.exp2(127.0 - byte)[:, None, :]).reshape(k, n).astype(np.float32)
    by_word = np.ascontiguousarray(scaled.reshape(k // 512, 128, 4, n).transpose(0, 1, 3, 2))
    if fmt == "e4m3":
        words = by_word.astype(ml_dtypes.float8_e4m3fn).view(np.uint8)
    else:
        c = by_word.astype(ml_dtypes.float4_e2m1fn).view(np.uint8) & 0xF
        words = (c[..., 0::2] | (c[..., 1::2] << 4)).reshape(k // 512, 128, 2 * n)
    return np.ascontiguousarray(words), np.ascontiguousarray(byte.astype(np.uint8).reshape(k // 512, 16, n))


def unpack_weight(words, scales, fmt):
    g, _, n = scales.shape
    words = np.ascontiguousarray(words).reshape(g, 128, n, -1)
    if fmt == "e4m3":
        vals = words.view(ml_dtypes.float8_e4m3fn).astype(np.float64)
    else:
        nib = np.empty((g, 128, n, 4), np.uint8)
        nib[..., 0::2] = words & 0xF
        nib[..., 1::2] = words >> 4
        vals = E2M1[nib]
    vals = vals * np.repeat(np.exp2(scales.astype(np.float64) - 127.0), 8, axis=1)[..., None]
    return vals.transpose(0, 1, 3, 2).reshape(g * 512, n)


def gelu(v):
    return 0.5 * v * (1.0 + np.tanh(np.sqrt(2.0 / np.pi) * (v + 0.044715 * v**3)))


K, T, S, P, P2, H, N = 1024, 2048, 1024, 512, 256, 1024, 512

def setup_inputs():
    n = np.random.standard_normal
    s = mx_kscale(K)[:, None]
    u = mx_kscale(H)[:, None]
    tab_words, tab_scales = pack_weight(n((K, T)) * s, "e4m3")
    w2_words, w2_scales = pack_weight(n((K, H)) / np.sqrt(K) / s, "e2m1")
    w3_words, w3_scales = pack_weight(n((H, N)) / np.sqrt(H) / u, "e4m3")
    return {
        "tab_words": tab_words, "tab_scales": tab_scales,
        "offs": striped(np.random.permutation(T)[:S]),
        "pos1": striped(np.random.permutation(S)[:P]),
        "pos2": striped(np.random.permutation(S)[:P]),
        "pos3": striped(np.random.permutation(P)[:P2]),
        "pos4": striped(np.random.permutation(P)[:P2]),
        "w1": (n((K, H)) / np.sqrt(K) / s * u.T).astype(np.float32),
        "w2_words": w2_words, "w2_scales": w2_scales,
        "w3_words": w3_words, "w3_scales": w3_scales,
        "bias": (0.5 * n(N)).astype(np.float32),
    }

def reference(tab_words, tab_scales, offs, pos1, pos2, pos3, pos4,
              w1, w2_words, w2_scales, w3_words, w3_scales, bias):
    v = unpack_weight(tab_words, tab_scales, "e4m3")[:, unstriped(offs)]
    w2 = unpack_weight(w2_words, w2_scales, "e2m1")
    w3 = unpack_weight(w3_words, w3_scales, "e4m3")
    left = mxq(f64(w1), 0, "e4m3").T @ v
    right = w2.T @ v
    z = left[:, unstriped(pos1)] * right[:, unstriped(pos2)]
    y = w3.T @ mxq(z, 0, "e4m3")
    term = np.maximum(y[:, unstriped(pos3)], y[:, unstriped(pos4)])
    return term + f64(bias)[:, None]

@@ -1,0 +1,292 @@
+from contextlib import ExitStack
+
+import concourse.mybir as mybir
+
+K, T, S, PICKS, TERMS, H, N = 1024, 2048, 1024, 512, 256, 1024, 512
+FLOPS = 2 * (2 * K * H * S + H * N * PICKS)
+
+F32 = mybir.dt.float32
+BF16 = mybir.dt.bfloat16
+I32 = mybir.dt.int32
+U32 = mybir.dt.uint32
+U16 = mybir.dt.uint16
+U8 = mybir.dt.uint8
+E4M3 = mybir.dt.float8_e4m3fn_x4
+E2M1 = mybir.dt.float4_e2m1fn_x4
+MULT = mybir.AluOpType.mult
+MAX = mybir.AluOpType.max
+COPY = mybir.ActivationFunctionType.Copy
+IDENTITY = mybir.ActivationFunctionType.Identity
+
+P = 128
+PACK = 4
+PASS = P * PACK
+BANK = 512
+PASSES = 2
+LAST_CHUNKS = ((0, 256), (256, 128), (384, 128))
+
+
+def tile_list_curriculum_merger_kernel(
+    tc, tab_words, tab_scales, offs, pos1, pos2, pos3, pos4,
+    w1, w2_words, w2_scales, w3_words, w3_scales, bias, out,
+):
+    nc = tc.nc
+    with ExitStack() as ctx:
+        lists = ctx.enter_context(tc.tile_pool(name="lists", bufs=1))
+        keep = ctx.enter_context(tc.tile_pool(name="keep", bufs=1))
+        stage = ctx.enter_context(tc.tile_pool(name="stage", bufs=2))
+        rows = ctx.enter_context(tc.tile_pool(name="rows", bufs=10))
+        psum = ctx.enter_context(tc.psum_pool(name="psum", bufs=1))
+        banks_taken = []
+
+        def next_bank():
+            banks_taken.append(psum.tile([P, BANK], F32, name="acc", tag=f"bank{len(banks_taken) % 4}"))
+            return banks_taken[-1]
+
+        def load_list(src, name):
+            tile = lists.tile(list(src.shape), U16, name=name)
+            nc.sync.dma_start(tile[:], src)
+            return tile
+
+        w2_rows = keep.tile([P, H], U8, name="w2_rows")
+        tab_rows = keep.tile([P, T], U8, name="tab_rows", tag="slot_c")
+        for tile in (w2_rows, tab_rows):
+            nc.vector.memset(tile[32:64, :].bitcast(I32), 0)
+            nc.vector.memset(tile[64:128, :].bitcast(I32), 0)
+        w2_planes = keep.tile([P, PASSES, H], U8, name="w2_planes", align_bytes=64)
+        v_planes = keep.tile([P, PASSES, S], U8, name="v_planes", align_bytes=64)
+        for tile in (w2_planes, v_planes):
+            nc.gpsimd.memset(tile[:].rearrange("p a c -> p (a c)").bitcast(I32), 0)
+
+        idx = load_list(offs, "idx")
+        nc.sync.dma_start(w2_rows[0:32, :].bitcast(I32), w2_scales.rearrange("a q c -> q a c").bitcast(I32))
+        nc.sync.dma_start(tab_rows[0:32, :].bitcast(I32), tab_scales.rearrange("a q t -> q a t").bitcast(I32))
+        tab = [keep.tile([P, T], I32, name=f"tab{a}", tag=("slot_a", "slot_b")[a]) for a in range(PASSES)]
+
+        def load_tab(a):
+            nc.sync.dma_start(tab[a][:], tab_words[a].rearrange("p t i -> p (t i)").bitcast(I32))
+
+        load_tab(0)
+        p1 = load_list(pos1, "p1")
+        p2 = load_list(pos2, "p2")
+        p3 = load_list(pos3, "p3")
+        p4 = load_list(pos4, "p4")
+        load_tab(1)
+        w2_raw = keep.tile([P, PASSES, 2 * H], U8, name="w2_raw", tag="packed", align_bytes=64)
+        nc.sync.dma_start(w2_raw[:].bitcast(I32), w2_words.rearrange("a p c -> p a c").bitcast(I32))
+        bias_cols = keep.tile([P, N // P], F32, name="bias_cols")
+        with nc.allow_non_contiguous_dma("one bias value for each partition"):
+            nc.gpsimd.dma_start(bias_cols[:], bias.rearrange("(n p) -> p n", p=P))
+
+        def spread_rows(planes, packed):
+            for q in range(4):
+                nc.scalar.dma_start(
+                    planes[32 * q : 32 * q + 4, :, :].bitcast(I32), packed[8 * q : 8 * q + 8, :].bitcast(I32)
+                )
+
+        w2_sorted = keep.tile([P, H], U8, name="w2_sorted")
+        nc.vector.tensor_copy(
+            w2_sorted[:].rearrange("p (b t g i) -> p b g t i", b=PASSES, t=PACK, i=16),
+            w2_rows[:].rearrange("p (b g i t) -> p b g t i", b=PASSES, t=PACK, i=16),
+        )
+        spread_rows(w2_planes, w2_sorted)
+
+        v_rows = keep.tile([P, S], U8, name="v_rows", tag="scale_rows", align_bytes=64)
+        nc.vector.tensor_copy(v_rows[:], tab_rows[:].indirect(idx[:]))
+        spread_rows(v_planes, v_rows)
+
+        w1_raw = {}
+
+        def load_w1(a, b, slot):
+            w1_raw[a, b] = keep.tile([P, PACK, PASS], F32, name=f"w1_raw{a}{b}", tag=slot)
+            nc.sync.dma_start(
+                w1_raw[a, b][:],
+                w1[PASS * a : PASS * (a + 1), PASS * b : PASS * (b + 1)].rearrange("(p j) c -> p j c", j=PACK),
+            )
+
+        v_words = {}
+
+        def gather_words(a, h):
+            v_words[a, h] = keep.tile([P, BANK], U32, name=f"v_words{a}{h}", align_bytes=64)
+            nc.vector.tensor_copy(v_words[a, h][:], tab[a][:].bitcast(U32).indirect(idx[:, 32 * h : 32 * (h + 1)]))
+
+        w2_codes = {}
+
+        def order_w2(b):
+            w2_codes[b] = keep.tile([P, PASSES, 2 * PASS], U8, name=f"w2_codes{b}", align_bytes=64)
+            nc.vector.tensor_copy(
+                w2_codes[b][:].bitcast(U16).rearrange("p a (t g i) -> p a g t i", t=PACK, i=8),
+                w2_raw[:].bitcast(U16)[:, :, PASS * b : PASS * (b + 1)].rearrange("p a (g i t) -> p a g t i", t=PACK, i=8),
+            )
+
+        w1_bf, w1_codes, w1_planes = {}, {}, {}
+
+        def round_w1(a, b, copy, part, parts):
+            if part == 0:
+                w1_bf[a, b] = stage.tile([P, PACK, P, PACK], BF16, name="w1_bf", align_bytes=64)
+            ms = slice(P // parts * part, P // parts * (part + 1))
+            copy(
+                w1_bf[a, b][:, :, ms, :].rearrange("p t m j -> p m j t"),
+                w1_raw[a, b][:].rearrange("p j (m t) -> p m j t", t=PACK)[:, ms, :, :],
+            )
+
+        def scalar_round(dst, src):
+            nc.scalar.activation(dst, src, COPY)
+
+        def quantize_w1(a, b):
+            w1_codes[a, b] = keep.tile([P, PASS], U32, name=f"w1_codes{a}{b}", align_bytes=64)
+            w1_planes[a, b] = keep.tile([P, PASS], U8, name=f"w1_planes{a}{b}", align_bytes=64)
+            nc.vector.quantize_mx(
+                out=w1_codes[a, b][:].bitcast(E4M3),
+                scales=w1_planes[a, b][:],
+                in_=w1_bf[a, b][:].rearrange("p t m j -> p (t m j)"),
+            )
+
+        def product_rows(codes, planes, window):
+            if window is None:
+                window = rows.tile([P, S], F32, name="window")[:]
+            for h in range(S // BANK):
+                acc = next_bank()
+                for a in range(PASSES):
+                    nc.tensor.matmul_mx(
+                        out=acc[:], lhsT=codes(a), lhsT_scale=planes(a),
+                        rhs=v_words[a, h][:].bitcast(E4M3), rhs_scale=v_planes[:, a, BANK * h : BANK * (h + 1)],
+                        start=(a == 0), stop=(a == PASSES - 1),
+                    )
+                nc.scalar.copy(window[:, BANK * h : BANK * (h + 1)], acc[:])
+            return window
+
+        picked = {}
+
+        def right(b, t, window=None):
+            window = product_rows(
+                lambda a: w2_codes[b][:, a, 2 * P * t : 2 * P * (t + 1)].bitcast(E2M1),
+                lambda a: w2_planes[:, a, PASS * b + P * t : PASS * b + P * (t + 1)],
+                window,
+            )
+            picked[b, t] = stage.tile([P, PICKS], F32, name="picked", bufs=8)
+            nc.vector.tensor_copy(picked[b, t][:], window.indirect(p2[:]))
+
+        z = [keep.tile([P, PACK, PICKS], F32, name=f"z{b}") for b in range(PASSES)]
+
+        def left_window(b, t):
+            return product_rows(
+                lambda a: w1_codes[a, b][:, P * t : P * (t + 1)].bitcast(E4M3),
+                lambda a: w1_planes[a, b][:, P * t : P * (t + 1)],
+                None,
+            )
+
+        def merge(window, b, t, m0, width):
+            nc.vector.tensor_tensor(
+                z[b][:, t, m0 : m0 + width],
+                window.indirect(p1[:, m0 // 16 : (m0 + width) // 16]),
+                picked[b, t][:, m0 : m0 + width],
+                MULT,
+            )
+
+        def left(b, t):
+            merge(left_window(b, t), b, t, 0, PICKS)
+
+        def quantize_z(b, m0, width, copy):
+            z_bf = keep.tile([P, width, PACK], BF16, name=f"z_bf{b}_{m0}", tag=f"z_bf{b}_{m0}", align_bytes=64)
+            copy(
+                z_bf[:].rearrange("p (c i) t -> p c t i", i=4),
+                z[b][:, :, m0 : m0 + width].rearrange("p t (c i) -> p c t i", i=4),
+            )
+            codes = keep.tile([P, width], U32, name=f"z_codes{b}_{m0}", align_bytes=64)
+            plane = keep.tile([P, width], U8, name=f"z_plane{b}_{m0}", align_bytes=64)
+            nc.vector.quantize_mx(
+                out=codes[:].bitcast(E4M3), scales=plane[:], in_=z_bf[:].rearrange("p c t -> p (c t)")
+            )
+            return codes, plane
+
+        load_w1(0, 0, "slot_c")
+        gather_words(0, 0)
+        gather_words(0, 1)
+        load_w1(1, 0, "slot_a")
+        gather_words(1, 0)
+        gather_words(1, 1)
+        load_w1(0, 1, "slot_b")
+        order_w2(0)
+        round_w1(0, 0, scalar_round, 0, 1)
+        order_w2(1)
+        round_w1(1, 0, nc.vector.tensor_copy, 0, 1)
+        load_w1(1, 1, "slot_a")
+        w3_codes = keep.tile([P, PASSES, 4 * N], U8, name="w3_codes", tag="packed", align_bytes=64)
+        nc.sync.dma_start(w3_codes[:].bitcast(I32), w3_words.rearrange("a p c i -> p a (c i)").bitcast(I32))
+        w3_planes = keep.tile([P, PASSES, N], U8, name="w3_planes", tag="scale_rows", align_bytes=64)
+        nc.gpsimd.memset(w3_planes[:].rearrange("p a c -> p (a c)").bitcast(I32), 0)
+        for q in range(4):
+            nc.sync.dma_start(
+                w3_planes[32 * q : 32 * q + 4, :, :].bitcast(I32),
+                w3_scales[:, 4 * q : 4 * q + 4, :].rearrange("a r c -> r a c").bitcast(I32),
+            )
+        quantize_w1(0, 0)
+        quantize_w1(1, 0)
+
+        first_rows = keep.tile([P, 2, S], F32, name="first_rows", tag="slot_c")
+        right(0, 0, first_rows[:, 0, :])
+        right(0, 1, first_rows[:, 1, :])
+        right(0, 2)
+        left(0, 0)
+        right(0, 3)
+        left(0, 1)
+        round_w1(0, 1, scalar_round, 0, 2)
+        right(1, 0)
+        left(0, 2)
+        round_w1(0, 1, scalar_round, 1, 2)
+        quantize_w1(0, 1)
+        right(1, 1)
+        left(0, 3)
+        round_w1(1, 1, scalar_round, 0, 2)
+        round_w1(1, 1, scalar_round, 1, 2)
+        quantize_w1(1, 1)
+        right(1, 2)
+        late_rows = keep.tile([P, S], F32, name="late_rows", tag="z_bf0_0", align_bytes=64)
+        right(1, 3, late_rows[:])
+        left(1, 0)
+        left(1, 1)
+        left(1, 2)
+        last_window = left_window(1, 3)
+        z0_codes, z0_plane = quantize_z(0, 0, PICKS, nc.scalar.copy)
+
+        y = [keep.tile([P, PICKS], F32, name=f"y{n}") for n in range(N // P)]
+
+        def modules(acc_cols, n, m0, width, z1):
+            for b in range(PASSES):
+                codes = z0_codes[:, m0 : m0 + width] if b == 0 else z1[0][:]
+                plane = z0_plane[:, m0 : m0 + width] if b == 0 else z1[1][:]
+                nc.tensor.matmul_mx(
+                    out=acc_cols,
+                    lhsT=w3_codes[:, b, 4 * P * n : 4 * P * (n + 1)].bitcast(E4M3),
+                    lhsT_scale=w3_planes[:, b, P * n : P * (n + 1)],
+                    rhs=codes.bitcast(E4M3), rhs_scale=plane,
+                    start=(b == 0), stop=(b == PASSES - 1),
+                )
+
+        def add_bias(n, m0, acc_cols):
+            nc.scalar.activation(y[n][:, m0 : m0 + 256], acc_cols, IDENTITY, bias=bias_cols[:, n : n + 1])
+
+        for m0, width in LAST_CHUNKS:
+            merge(last_window, 1, 3, m0, width)
+        z1_first = quantize_z(1, 0, 256, nc.scalar.copy)
+        z1_late = [quantize_z(1, m0, 128, nc.vector.tensor_copy) for m0 in (256, 384)]
+        early = [next_bank() for pair in range(2)]
+        late = [psum.tile([P, BANK], F32, name=f"late{n}") for n in range(N // P)]
+        for n in range(N // P):
+            modules(early[n // 2][:, 256 * (n % 2) : 256 * (n % 2 + 1)], n, 0, 256, z1_first)
+        for c in range(2):
+            for n in range(N // P):
+                modules(late[n][:, 128 * c : 128 * (c + 1)], n, 256 + 128 * c, 128, z1_late[c])
+        for n in range(N // P):
+            add_bias(n, 0, early[n // 2][:, 256 * (n % 2) : 256 * (n % 2 + 1)])
+            add_bias(n, 256, late[n][:, 0:256])
+
+        for n in range(N // P):
+            first = stage.tile([P, TERMS], F32, name="first", bufs=4)
+            second = stage.tile([P, TERMS], F32, name="second", bufs=4)
+            nc.vector.tensor_copy(first[:], y[n][:].indirect(p3[:]))
+            nc.vector.tensor_copy(second[:], y[n][:].indirect(p4[:]))
+            term = stage.tile([P, TERMS], F32, name="term", bufs=4)
+            nc.vector.tensor_tensor(term[:], first[:], second[:], MAX)
+            nc.sync.dma_start(out[P * n : P * (n + 1), :], term[:])

@@ -2,8 +2,8 @@ from contextlib import ExitStack
 
 import concourse.mybir as mybir
 
-K, T, S, PICKS, TERMS, H, N = 1024, 2048, 1024, 512, 256, 1024, 512
-FLOPS = 2 * (2 * K * H * S + H * N * PICKS)
+K, T, S, MERGED, TERMS, H, N = 1024, 2048, 1024, 512, 256, 1024, 512
+FLOPS = 2 * (2 * K * H * S + H * N * MERGED)
 
 F32 = mybir.dt.float32
 BF16 = mybir.dt.bfloat16
@@ -23,7 +23,6 @@ PACK = 4
 PASS = P * PACK
 BANK = 512
 PASSES = 2
-LAST_CHUNKS = ((0, 256), (256, 128), (384, 128))
 
 
 def tile_list_curriculum_merger_kernel(
@@ -34,259 +33,245 @@ def tile_list_curriculum_merger_kernel(
     with ExitStack() as ctx:
         lists = ctx.enter_context(tc.tile_pool(name="lists", bufs=1))
         keep = ctx.enter_context(tc.tile_pool(name="keep", bufs=1))
-        stage = ctx.enter_context(tc.tile_pool(name="stage", bufs=2))
-        rows = ctx.enter_context(tc.tile_pool(name="rows", bufs=10))
+        rows = ctx.enter_context(tc.tile_pool(name="rows", bufs=8))
         psum = ctx.enter_context(tc.psum_pool(name="psum", bufs=1))
-        banks_taken = []
 
-        def next_bank():
-            banks_taken.append(psum.tile([P, BANK], F32, name="acc", tag=f"bank{len(banks_taken) % 4}"))
-            return banks_taken[-1]
+        def tile(shape, dtype, name, slot=None):
+            return keep.tile(shape, dtype, name=name, tag=slot or name, align_bytes=64)[:]
 
         def load_list(src, name):
-            tile = lists.tile(list(src.shape), U16, name=name)
-            nc.sync.dma_start(tile[:], src)
-            return tile
+            offsets = lists.tile(list(src.shape), U16, name=name)
+            nc.sync.dma_start(offsets[:], src)
+            return offsets
 
-        w2_rows = keep.tile([P, H], U8, name="w2_rows")
-        tab_rows = keep.tile([P, T], U8, name="tab_rows", tag="slot_c")
-        for tile in (w2_rows, tab_rows):
-            nc.vector.memset(tile[32:64, :].bitcast(I32), 0)
-            nc.vector.memset(tile[64:128, :].bitcast(I32), 0)
-        w2_planes = keep.tile([P, PASSES, H], U8, name="w2_planes", align_bytes=64)
-        v_planes = keep.tile([P, PASSES, S], U8, name="v_planes", align_bytes=64)
-        for tile in (w2_planes, v_planes):
-            nc.gpsimd.memset(tile[:].rearrange("p a c -> p (a c)").bitcast(I32), 0)
+        w2_rows = tile([P, H], U8, "w2_rows", "slot_w1")
+        tab_rows = tile([P, T], U8, "tab_rows", "slot_w2")
+        for packed in (w2_rows, tab_rows):
+            nc.vector.memset(packed[32:64, :].bitcast(I32), 0)
+            nc.vector.memset(packed[64:128, :].bitcast(I32), 0)
+        w2_planes = tile([P, PASSES, H], U8, "w2_planes")
+        v_planes = tile([P, PASSES, S], U8, "v_planes")
+        for planes in (w2_planes, v_planes):
+            nc.gpsimd.memset(planes.rearrange("p a c -> p (a c)").bitcast(I32), 0)
 
         idx = load_list(offs, "idx")
         nc.sync.dma_start(w2_rows[0:32, :].bitcast(I32), w2_scales.rearrange("a q c -> q a c").bitcast(I32))
         nc.sync.dma_start(tab_rows[0:32, :].bitcast(I32), tab_scales.rearrange("a q t -> q a t").bitcast(I32))
-        tab = [keep.tile([P, T], I32, name=f"tab{a}", tag=("slot_a", "slot_b")[a]) for a in range(PASSES)]
-
-        def load_tab(a):
-            nc.sync.dma_start(tab[a][:], tab_words[a].rearrange("p t i -> p (t i)").bitcast(I32))
-
-        load_tab(0)
         p1 = load_list(pos1, "p1")
         p2 = load_list(pos2, "p2")
         p3 = load_list(pos3, "p3")
         p4 = load_list(pos4, "p4")
-        load_tab(1)
-        w2_raw = keep.tile([P, PASSES, 2 * H], U8, name="w2_raw", tag="packed", align_bytes=64)
-        nc.sync.dma_start(w2_raw[:].bitcast(I32), w2_words.rearrange("a p c -> p a c").bitcast(I32))
-        bias_cols = keep.tile([P, N // P], F32, name="bias_cols")
-        with nc.allow_non_contiguous_dma("one bias value for each partition"):
-            nc.gpsimd.dma_start(bias_cols[:], bias.rearrange("(n p) -> p n", p=P))
 
-        def spread_rows(planes, packed):
-            for q in range(4):
-                nc.scalar.dma_start(
-                    planes[32 * q : 32 * q + 4, :, :].bitcast(I32), packed[8 * q : 8 * q + 8, :].bitcast(I32)
-                )
+        tab, w2_raw, w1_raw = {}, {}, {}
 
-        w2_sorted = keep.tile([P, H], U8, name="w2_sorted")
-        nc.vector.tensor_copy(
-            w2_sorted[:].rearrange("p (b t g i) -> p b g t i", b=PASSES, t=PACK, i=16),
-            w2_rows[:].rearrange("p (b g i t) -> p b g t i", b=PASSES, t=PACK, i=16),
-        )
-        spread_rows(w2_planes, w2_sorted)
+        def load_tab(a):
+            tab[a] = tile([P, T], I32, f"tab{a}", f"slot_tab{a}")
+            nc.sync.dma_start(tab[a], tab_words[a].rearrange("p t i -> p (t i)").bitcast(I32))
 
-        v_rows = keep.tile([P, S], U8, name="v_rows", tag="scale_rows", align_bytes=64)
-        nc.vector.tensor_copy(v_rows[:], tab_rows[:].indirect(idx[:]))
-        spread_rows(v_planes, v_rows)
-
-        w1_raw = {}
+        def load_w2(b, slot=None):
+            w2_raw[b] = tile([P, PASSES, 2 * PASS], U8, f"w2_raw{b}", slot)
+            nc.sync.dma_start(
+                w2_raw[b].bitcast(I32),
+                w2_words[:, :, 2 * PASS * b : 2 * PASS * (b + 1)].rearrange("a p c -> p a c").bitcast(I32),
+            )
 
         def load_w1(a, b, slot):
-            w1_raw[a, b] = keep.tile([P, PACK, PASS], F32, name=f"w1_raw{a}{b}", tag=slot)
+            w1_raw[a, b] = tile([P, PACK, PASS], F32, f"w1_raw{a}{b}", slot)
             nc.sync.dma_start(
-                w1_raw[a, b][:],
+                w1_raw[a, b],
                 w1[PASS * a : PASS * (a + 1), PASS * b : PASS * (b + 1)].rearrange("(p j) c -> p j c", j=PACK),
             )
 
-        v_words = {}
+        def spread_rows(planes, packed):
+            for q in range(4):
+                nc.sync.dma_start(
+                    planes[32 * q : 32 * q + 4, :, :].bitcast(I32), packed[8 * q : 8 * q + 8, :].bitcast(I32)
+                )
+
+        load_tab(0)
+        load_w2(0)
+        load_tab(1)
+
+        w2_sorted = tile([P, H], U8, "w2_sorted")
+        nc.vector.tensor_copy(
+            w2_sorted.rearrange("p (b t g i) -> p b g t i", b=PASSES, t=PACK, i=16),
+            w2_rows.rearrange("p (b g i t) -> p b g t i", b=PASSES, t=PACK, i=16),
+        )
+        spread_rows(w2_planes, w2_sorted)
+        load_w1(0, 0, "slot_w1")
+
+        v_rows = tile([P, S], U8, "v_rows")
+        nc.vector.tensor_copy(v_rows, tab_rows.indirect(idx[:]))
+        spread_rows(v_planes, v_rows)
+        load_w2(1, "slot_w2")
+
+        v_words, w2_codes, w1_bf, w1_codes, w1_planes, picked, z_bf, z_mx = {}, {}, {}, {}, {}, {}, {}, {}
 
         def gather_words(a, h):
-            v_words[a, h] = keep.tile([P, BANK], U32, name=f"v_words{a}{h}", align_bytes=64)
-            nc.vector.tensor_copy(v_words[a, h][:], tab[a][:].bitcast(U32).indirect(idx[:, 32 * h : 32 * (h + 1)]))
-
-        w2_codes = {}
+            v_words[a, h] = tile([P, BANK], U32, f"v_words{a}{h}")
+            nc.vector.tensor_copy(v_words[a, h], tab[a].bitcast(U32).indirect(idx[:, 32 * h : 32 * (h + 1)]))
 
         def order_w2(b):
-            w2_codes[b] = keep.tile([P, PASSES, 2 * PASS], U8, name=f"w2_codes{b}", align_bytes=64)
+            w2_codes[b] = tile([P, PASSES, 2 * PASS], U8, f"w2_codes{b}")
             nc.vector.tensor_copy(
-                w2_codes[b][:].bitcast(U16).rearrange("p a (t g i) -> p a g t i", t=PACK, i=8),
-                w2_raw[:].bitcast(U16)[:, :, PASS * b : PASS * (b + 1)].rearrange("p a (g i t) -> p a g t i", t=PACK, i=8),
-            )
-
-        w1_bf, w1_codes, w1_planes = {}, {}, {}
-
-        def round_w1(a, b, copy, part, parts):
-            if part == 0:
-                w1_bf[a, b] = stage.tile([P, PACK, P, PACK], BF16, name="w1_bf", align_bytes=64)
-            ms = slice(P // parts * part, P // parts * (part + 1))
-            copy(
-                w1_bf[a, b][:, :, ms, :].rearrange("p t m j -> p m j t"),
-                w1_raw[a, b][:].rearrange("p j (m t) -> p m j t", t=PACK)[:, ms, :, :],
+                w2_codes[b].bitcast(U16).rearrange("p a (t g i) -> p a g t i", t=PACK, i=8),
+                w2_raw[b].bitcast(U16).rearrange("p a (g i t) -> p a g t i", t=PACK, i=8),
             )
 
         def scalar_round(dst, src):
             nc.scalar.activation(dst, src, COPY)
 
-        def quantize_w1(a, b):
-            w1_codes[a, b] = keep.tile([P, PASS], U32, name=f"w1_codes{a}{b}", align_bytes=64)
-            w1_planes[a, b] = keep.tile([P, PASS], U8, name=f"w1_planes{a}{b}", align_bytes=64)
-            nc.vector.quantize_mx(
-                out=w1_codes[a, b][:].bitcast(E4M3),
-                scales=w1_planes[a, b][:],
-                in_=w1_bf[a, b][:].rearrange("p t m j -> p (t m j)"),
+        def round_w1(a, b, copy, m0, m1, slot=None):
+            if (a, b) not in w1_bf:
+                w1_bf[a, b] = tile([P, PACK, P, PACK], BF16, f"w1_bf{a}{b}", slot)
+            copy(
+                w1_bf[a, b][:, :, m0:m1, :].rearrange("p t m j -> p m j t"),
+                w1_raw[a, b].rearrange("p j (m t) -> p m j t", t=PACK)[:, m0:m1, :, :],
             )
 
-        def product_rows(codes, planes, window):
+        def quantize_w1(a, b):
+            w1_codes[a, b] = tile([P, PASS], U32, f"w1_codes{a}{b}")
+            w1_planes[a, b] = tile([P, PASS], U8, f"w1_planes{a}{b}")
+            nc.vector.quantize_mx(
+                out=w1_codes[a, b].bitcast(E4M3),
+                scales=w1_planes[a, b],
+                in_=w1_bf[a, b].rearrange("p t m j -> p (t m j)"),
+            )
+
+        banks_taken = []
+
+        def first_stage(codes, planes, window):
             if window is None:
                 window = rows.tile([P, S], F32, name="window")[:]
             for h in range(S // BANK):
-                acc = next_bank()
+                acc = psum.tile([P, BANK], F32, name="acc", tag=f"bank{len(banks_taken) % 4}")
+                banks_taken.append(acc)
                 for a in range(PASSES):
                     nc.tensor.matmul_mx(
                         out=acc[:], lhsT=codes(a), lhsT_scale=planes(a),
-                        rhs=v_words[a, h][:].bitcast(E4M3), rhs_scale=v_planes[:, a, BANK * h : BANK * (h + 1)],
+                        rhs=v_words[a, h].bitcast(E4M3), rhs_scale=v_planes[:, a, BANK * h : BANK * (h + 1)],
                         start=(a == 0), stop=(a == PASSES - 1),
                     )
                 nc.scalar.copy(window[:, BANK * h : BANK * (h + 1)], acc[:])
             return window
 
-        picked = {}
-
         def right(b, t, window=None):
-            window = product_rows(
+            window = first_stage(
                 lambda a: w2_codes[b][:, a, 2 * P * t : 2 * P * (t + 1)].bitcast(E2M1),
                 lambda a: w2_planes[:, a, PASS * b + P * t : PASS * b + P * (t + 1)],
                 window,
             )
-            picked[b, t] = stage.tile([P, PICKS], F32, name="picked", bufs=8)
-            nc.vector.tensor_copy(picked[b, t][:], window.indirect(p2[:]))
+            picked[b, t] = tile([P, MERGED], F32, f"picked{b}{t}")
+            nc.vector.tensor_copy(picked[b, t], window.indirect(p2[:]))
 
-        z = [keep.tile([P, PACK, PICKS], F32, name=f"z{b}") for b in range(PASSES)]
+        z = [tile([P, PACK, MERGED], F32, f"z{b}") for b in range(PASSES)]
 
-        def left_window(b, t):
-            return product_rows(
+        def left(b, t, window=None, parts=((0, MERGED),)):
+            window = first_stage(
                 lambda a: w1_codes[a, b][:, P * t : P * (t + 1)].bitcast(E4M3),
                 lambda a: w1_planes[a, b][:, P * t : P * (t + 1)],
-                None,
+                window,
             )
+            for m0, m1 in parts:
+                nc.vector.tensor_tensor(
+                    z[b][:, t, m0:m1], window.indirect(p1[:, m0 // 16 : m1 // 16]), picked[b, t][:, m0:m1], MULT
+                )
 
-        def merge(window, b, t, m0, width):
-            nc.vector.tensor_tensor(
-                z[b][:, t, m0 : m0 + width],
-                window.indirect(p1[:, m0 // 16 : (m0 + width) // 16]),
-                picked[b, t][:, m0 : m0 + width],
-                MULT,
-            )
-
-        def left(b, t):
-            merge(left_window(b, t), b, t, 0, PICKS)
-
-        def quantize_z(b, m0, width, copy):
-            z_bf = keep.tile([P, width, PACK], BF16, name=f"z_bf{b}_{m0}", tag=f"z_bf{b}_{m0}", align_bytes=64)
+        def round_z(b, m0, m1, copy, slot=None):
+            z_bf[b, m0] = slot if slot is not None else tile([P, m1 - m0, PACK], BF16, f"z_bf{b}_{m0}")
             copy(
-                z_bf[:].rearrange("p (c i) t -> p c t i", i=4),
-                z[b][:, :, m0 : m0 + width].rearrange("p t (c i) -> p c t i", i=4),
+                z_bf[b, m0].rearrange("p (c i) t -> p c t i", i=4),
+                z[b][:, :, m0:m1].rearrange("p t (c i) -> p c t i", i=4),
             )
-            codes = keep.tile([P, width], U32, name=f"z_codes{b}_{m0}", align_bytes=64)
-            plane = keep.tile([P, width], U8, name=f"z_plane{b}_{m0}", align_bytes=64)
-            nc.vector.quantize_mx(
-                out=codes[:].bitcast(E4M3), scales=plane[:], in_=z_bf[:].rearrange("p c t -> p (c t)")
-            )
-            return codes, plane
 
-        load_w1(0, 0, "slot_c")
+        def quantize_z(b, m0, m1):
+            codes = tile([P, m1 - m0], U32, f"z_codes{b}_{m0}")
+            plane = tile([P, m1 - m0], U8, f"z_plane{b}_{m0}")
+            nc.vector.quantize_mx(out=codes.bitcast(E4M3), scales=plane, in_=z_bf[b, m0].rearrange("p c t -> p (c t)"))
+            z_mx[b, m0, m1] = (codes, plane)
+
         gather_words(0, 0)
         gather_words(0, 1)
-        load_w1(1, 0, "slot_a")
+        load_w1(1, 0, "slot_tab0")
+        order_w2(0)
         gather_words(1, 0)
         gather_words(1, 1)
-        load_w1(0, 1, "slot_b")
-        order_w2(0)
-        round_w1(0, 0, scalar_round, 0, 1)
+        load_w1(0, 1, "slot_tab1")
         order_w2(1)
-        round_w1(1, 0, nc.vector.tensor_copy, 0, 1)
-        load_w1(1, 1, "slot_a")
-        w3_codes = keep.tile([P, PASSES, 4 * N], U8, name="w3_codes", tag="packed", align_bytes=64)
-        nc.sync.dma_start(w3_codes[:].bitcast(I32), w3_words.rearrange("a p c i -> p a (c i)").bitcast(I32))
-        w3_planes = keep.tile([P, PASSES, N], U8, name="w3_planes", tag="scale_rows", align_bytes=64)
-        nc.gpsimd.memset(w3_planes[:].rearrange("p a c -> p (a c)").bitcast(I32), 0)
+        round_w1(0, 0, scalar_round, 0, 96)
+        round_w1(0, 0, nc.vector.tensor_copy, 96, P)
+        quantize_w1(0, 0)
+        round_w1(1, 0, nc.vector.tensor_copy, 0, P)
+        first_rows = tile([P, 2, S], F32, "first_rows", "slot_w1")
+        right(0, 0, first_rows[:, 0, :])
+        quantize_w1(1, 0)
+        right(0, 1, first_rows[:, 1, :])
+        load_w1(1, 1, "slot_w1")
+        right(0, 2)
+        left(0, 0, tile([P, S], F32, "left00_rows", "w1_bf01"))
+        right(0, 3)
+        left(0, 1)
+        round_w1(0, 1, scalar_round, 0, 64)
+        right(1, 0)
+        left(0, 2)
+        round_w1(0, 1, scalar_round, 64, P)
+        quantize_w1(0, 1)
+        right(1, 1)
+        left(0, 3)
+        round_w1(1, 1, nc.vector.tensor_copy, 0, P)
+        quantize_w1(1, 1)
+        right(1, 2)
+
+        w3_codes = tile([P, PASSES, 4 * N], U8, "w3_codes", "w1_bf00")
+        nc.sync.dma_start(w3_codes.bitcast(I32), w3_words.rearrange("a p c i -> p a (c i)").bitcast(I32))
+        w3_planes = tile([P, PASSES, N], U8, "w3_planes", "picked02")
+        nc.gpsimd.memset(w3_planes.rearrange("p a c -> p (a c)").bitcast(I32), 0)
         for q in range(4):
             nc.sync.dma_start(
                 w3_planes[32 * q : 32 * q + 4, :, :].bitcast(I32),
                 w3_scales[:, 4 * q : 4 * q + 4, :].rearrange("a r c -> r a c").bitcast(I32),
             )
-        quantize_w1(0, 0)
-        quantize_w1(1, 0)
+        bias_cols = tile([P, N // P], F32, "bias_cols", "w1_bf10")
+        with nc.allow_non_contiguous_dma("one bias value for each partition"):
+            nc.sync.dma_start(bias_cols, bias.rearrange("(n p) -> p n", p=P))
 
-        first_rows = keep.tile([P, 2, S], F32, name="first_rows", tag="slot_c")
-        right(0, 0, first_rows[:, 0, :])
-        right(0, 1, first_rows[:, 1, :])
-        right(0, 2)
-        left(0, 0)
-        right(0, 3)
-        left(0, 1)
-        round_w1(0, 1, scalar_round, 0, 2)
-        right(1, 0)
-        left(0, 2)
-        round_w1(0, 1, scalar_round, 1, 2)
-        quantize_w1(0, 1)
-        right(1, 1)
-        left(0, 3)
-        round_w1(1, 1, scalar_round, 0, 2)
-        round_w1(1, 1, scalar_round, 1, 2)
-        quantize_w1(1, 1)
-        right(1, 2)
-        late_rows = keep.tile([P, S], F32, name="late_rows", tag="z_bf0_0", align_bytes=64)
-        right(1, 3, late_rows[:])
         left(1, 0)
+        right(1, 3)
         left(1, 1)
+        round_z(0, 0, 256, nc.scalar.copy)
+        quantize_z(0, 0, 256)
         left(1, 2)
-        last_window = left_window(1, 3)
-        z0_codes, z0_plane = quantize_z(0, 0, PICKS, nc.scalar.copy)
+        round_z(0, 256, 512, nc.scalar.copy)
+        quantize_z(0, 256, 512)
+        left(1, 3, parts=((0, 256), (256, 384), (384, 512)))
+        round_z(1, 0, 256, nc.scalar.copy)
+        round_z(1, 256, 384, nc.vector.tensor_copy)
+        round_z(1, 384, 512, nc.vector.tensor_copy)
+        for m0, m1 in ((256, 384), (384, 512), (0, 256)):
+            quantize_z(1, m0, m1)
 
-        y = [keep.tile([P, PICKS], F32, name=f"y{n}") for n in range(N // P)]
-
-        def modules(acc_cols, n, m0, width, z1):
-            for b in range(PASSES):
-                codes = z0_codes[:, m0 : m0 + width] if b == 0 else z1[0][:]
-                plane = z0_plane[:, m0 : m0 + width] if b == 0 else z1[1][:]
+        y = [tile([P, MERGED], F32, f"y{n}") for n in range(N // P)]
+        parts = list(z_mx)
+        for n in range(N // P):
+            acc = psum.tile([P, BANK], F32, name="late", bufs=4)
+            for b, m0, m1 in parts:
+                codes, plane = z_mx[b, m0, m1]
                 nc.tensor.matmul_mx(
-                    out=acc_cols,
+                    out=acc[:, m0:m1],
                     lhsT=w3_codes[:, b, 4 * P * n : 4 * P * (n + 1)].bitcast(E4M3),
                     lhsT_scale=w3_planes[:, b, P * n : P * (n + 1)],
                     rhs=codes.bitcast(E4M3), rhs_scale=plane,
-                    start=(b == 0), stop=(b == PASSES - 1),
+                    start=((b, m0, m1) == parts[0]), stop=((b, m0, m1) == parts[-1]),
                 )
+            nc.scalar.activation(y[n], acc[:], IDENTITY, bias=bias_cols[:, n : n + 1])
 
-        def add_bias(n, m0, acc_cols):
-            nc.scalar.activation(y[n][:, m0 : m0 + 256], acc_cols, IDENTITY, bias=bias_cols[:, n : n + 1])
-
-        for m0, width in LAST_CHUNKS:
-            merge(last_window, 1, 3, m0, width)
-        z1_first = quantize_z(1, 0, 256, nc.scalar.copy)
-        z1_late = [quantize_z(1, m0, 128, nc.vector.tensor_copy) for m0 in (256, 384)]
-        early = [next_bank() for pair in range(2)]
-        late = [psum.tile([P, BANK], F32, name=f"late{n}") for n in range(N // P)]
-        for n in range(N // P):
-            modules(early[n // 2][:, 256 * (n % 2) : 256 * (n % 2 + 1)], n, 0, 256, z1_first)
-        for c in range(2):
-            for n in range(N // P):
-                modules(late[n][:, 128 * c : 128 * (c + 1)], n, 256 + 128 * c, 128, z1_late[c])
-        for n in range(N // P):
-            add_bias(n, 0, early[n // 2][:, 256 * (n % 2) : 256 * (n % 2 + 1)])
-            add_bias(n, 256, late[n][:, 0:256])
-
-        for n in range(N // P):
-            first = stage.tile([P, TERMS], F32, name="first", bufs=4)
-            second = stage.tile([P, TERMS], F32, name="second", bufs=4)
-            nc.vector.tensor_copy(first[:], y[n][:].indirect(p3[:]))
-            nc.vector.tensor_copy(second[:], y[n][:].indirect(p4[:]))
-            term = stage.tile([P, TERMS], F32, name="term", bufs=4)
-            nc.vector.tensor_tensor(term[:], first[:], second[:], MAX)
-            nc.sync.dma_start(out[P * n : P * (n + 1), :], term[:])
+        first = tile([P, N // P, TERMS], F32, "first")
+        second = tile([P, N // P, TERMS], F32, "second")
+        term = tile([P, N // P, TERMS], F32, "term")
+        out_rows = out.rearrange("(n p) t -> p n t", p=P)
+        for n0, n1 in ((0, 2), (2, 3), (3, 4)):
+            for n in range(n0, n1):
+                nc.vector.tensor_copy(first[:, n, :], y[n].indirect(p3[:]))
+                nc.vector.tensor_copy(second[:, n, :], y[n].indirect(p4[:]))
+            nc.vector.tensor_tensor(term[:, n0:n1, :], first[:, n0:n1, :], second[:, n0:n1, :], MAX)
+            nc.sync.dma_start(out_rows[:, n0:n1, :], term[:, n0:n1, :])

@@ -201,7 +201,8 @@ def tile_list_curriculum_merger_kernel(
         round_w1(0, 0, scalar_round, 0, 96)
         round_w1(0, 0, nc.vector.tensor_copy, 96, P)
         quantize_w1(0, 0)
-        round_w1(1, 0, nc.vector.tensor_copy, 0, P)
+        round_w1(1, 0, scalar_round, 0, 64)
+        round_w1(1, 0, nc.vector.tensor_copy, 64, P)
         first_rows = tile([P, 2, S], F32, "first_rows", "slot_w1")
         right(0, 0, first_rows[:, 0, :])
         quantize_w1(1, 0)
@@ -217,8 +218,9 @@ def tile_list_curriculum_merger_kernel(
         round_w1(0, 1, scalar_round, 64, P)
         quantize_w1(0, 1)
         right(1, 1)
+        round_w1(1, 1, scalar_round, 0, 64)
         left(0, 3)
-        round_w1(1, 1, nc.vector.tensor_copy, 0, P)
+        round_w1(1, 1, nc.vector.tensor_copy, 64, P)
         quantize_w1(1, 1)
         right(1, 2)
 
@@ -253,7 +255,7 @@ def tile_list_curriculum_merger_kernel(
         y = [tile([P, MERGED], F32, f"y{n}") for n in range(N // P)]
         parts = list(z_mx)
         for n in range(N // P):
-            acc = psum.tile([P, BANK], F32, name="late", bufs=4)
+            acc = psum.tile([P, BANK], F32, name="late", bufs=2)
             for b, m0, m1 in parts:
                 codes, plane = z_mx[b, m0, m1]
                 nc.tensor.matmul_mx(

@@ -21,8 +21,20 @@ IDENTITY = mybir.ActivationFunctionType.Identity
 P = 128
 PACK = 4
 PASS = P * PACK
-BANK = 512
 PASSES = 2
+BANK = 512
+QUADRANTS = 4
+PER_COLUMN = 16
+LINE = 16
+
+STAGE1_BANKS = 4
+STAGE2_BANKS = 2
+WINDOWS = 8
+
+SCALAR_SHARE = {(0, 0): 96, (1, 0): 0, (0, 1): P, (1, 1): 64}
+FIRST_PART = (0, 256)
+LATE_PARTS = ((256, 384), (384, 512))
+STORES = ((0, 2), (2, 3), (3, 4))
 
 
 def tile_list_curriculum_merger_kernel(
@@ -33,7 +45,7 @@ def tile_list_curriculum_merger_kernel(
     with ExitStack() as ctx:
         lists = ctx.enter_context(tc.tile_pool(name="lists", bufs=1))
         keep = ctx.enter_context(tc.tile_pool(name="keep", bufs=1))
-        rows = ctx.enter_context(tc.tile_pool(name="rows", bufs=8))
+        rows = ctx.enter_context(tc.tile_pool(name="rows", bufs=WINDOWS))
         psum = ctx.enter_context(tc.psum_pool(name="psum", bufs=1))
 
         def tile(shape, dtype, name, slot=None):
@@ -46,9 +58,9 @@ def tile_list_curriculum_merger_kernel(
 
         w2_rows = tile([P, H], U8, "w2_rows", "slot_w1")
         tab_rows = tile([P, T], U8, "tab_rows", "slot_w2")
-        for packed in (w2_rows, tab_rows):
-            nc.vector.memset(packed[32:64, :].bitcast(I32), 0)
-            nc.vector.memset(packed[64:128, :].bitcast(I32), 0)
+        for dense in (w2_rows, tab_rows):
+            nc.vector.memset(dense[32:64, :].bitcast(I32), 0)
+            nc.vector.memset(dense[64:128, :].bitcast(I32), 0)
         w2_planes = tile([P, PASSES, H], U8, "w2_planes")
         v_planes = tile([P, PASSES, S], U8, "v_planes")
         for planes in (w2_planes, v_planes):
@@ -82,10 +94,11 @@ def tile_list_curriculum_merger_kernel(
                 w1[PASS * a : PASS * (a + 1), PASS * b : PASS * (b + 1)].rearrange("(p j) c -> p j c", j=PACK),
             )
 
-        def spread_rows(planes, packed):
-            for q in range(4):
+        def spread_rows(planes, dense):
+            for quad in range(QUADRANTS):
                 nc.sync.dma_start(
-                    planes[32 * q : 32 * q + 4, :, :].bitcast(I32), packed[8 * q : 8 * q + 8, :].bitcast(I32)
+                    planes[32 * quad : 32 * quad + 4, :, :].bitcast(I32),
+                    dense[8 * quad : 8 * quad + 8, :].bitcast(I32),
                 )
 
         load_tab(0)
@@ -94,8 +107,8 @@ def tile_list_curriculum_merger_kernel(
 
         w2_sorted = tile([P, H], U8, "w2_sorted")
         nc.vector.tensor_copy(
-            w2_sorted.rearrange("p (b t g i) -> p b g t i", b=PASSES, t=PACK, i=16),
-            w2_rows.rearrange("p (b g i t) -> p b g t i", b=PASSES, t=PACK, i=16),
+            w2_sorted.rearrange("p (b t g i) -> p b g t i", b=PASSES, t=PACK, i=LINE),
+            w2_rows.rearrange("p (b g i t) -> p b g t i", b=PASSES, t=PACK, i=LINE),
         )
         spread_rows(w2_planes, w2_sorted)
         load_w1(0, 0, "slot_w1")
@@ -109,25 +122,32 @@ def tile_list_curriculum_merger_kernel(
 
         def gather_words(a, h):
             v_words[a, h] = tile([P, BANK], U32, f"v_words{a}{h}")
-            nc.vector.tensor_copy(v_words[a, h], tab[a].bitcast(U32).indirect(idx[:, 32 * h : 32 * (h + 1)]))
+            cols = slice(BANK // PER_COLUMN * h, BANK // PER_COLUMN * (h + 1))
+            nc.vector.tensor_copy(v_words[a, h], tab[a].bitcast(U32).indirect(idx[:, cols]))
 
         def order_w2(b):
             w2_codes[b] = tile([P, PASSES, 2 * PASS], U8, f"w2_codes{b}")
             nc.vector.tensor_copy(
-                w2_codes[b].bitcast(U16).rearrange("p a (t g i) -> p a g t i", t=PACK, i=8),
-                w2_raw[b].bitcast(U16).rearrange("p a (g i t) -> p a g t i", t=PACK, i=8),
+                w2_codes[b].bitcast(U16).rearrange("p a (t g i) -> p a g t i", t=PACK, i=LINE // 2),
+                w2_raw[b].bitcast(U16).rearrange("p a (g i t) -> p a g t i", t=PACK, i=LINE // 2),
             )
 
         def scalar_round(dst, src):
             nc.scalar.activation(dst, src, COPY)
 
-        def round_w1(a, b, copy, m0, m1, slot=None):
+        def round_w1(a, b, copy, m0, m1):
             if (a, b) not in w1_bf:
-                w1_bf[a, b] = tile([P, PACK, P, PACK], BF16, f"w1_bf{a}{b}", slot)
+                w1_bf[a, b] = tile([P, PACK, P, PACK], BF16, f"w1_bf{a}{b}")
             copy(
                 w1_bf[a, b][:, :, m0:m1, :].rearrange("p t m j -> p m j t"),
                 w1_raw[a, b].rearrange("p j (m t) -> p m j t", t=PACK)[:, m0:m1, :, :],
             )
+
+        def round_w1_shared(a, b):
+            share = SCALAR_SHARE[a, b]
+            if share > 0:
+                round_w1(a, b, scalar_round, 0, share)
+            round_w1(a, b, nc.vector.tensor_copy, share, P)
 
         def quantize_w1(a, b):
             w1_codes[a, b] = tile([P, PASS], U32, f"w1_codes{a}{b}")
@@ -141,10 +161,8 @@ def tile_list_curriculum_merger_kernel(
         banks_taken = []
 
         def first_stage(codes, planes, window):
-            if window is None:
-                window = rows.tile([P, S], F32, name="window")[:]
             for h in range(S // BANK):
-                acc = psum.tile([P, BANK], F32, name="acc", tag=f"bank{len(banks_taken) % 4}")
+                acc = psum.tile([P, BANK], F32, name="acc", tag=f"bank{len(banks_taken) % STAGE1_BANKS}")
                 banks_taken.append(acc)
                 for a in range(PASSES):
                     nc.tensor.matmul_mx(
@@ -153,10 +171,11 @@ def tile_list_curriculum_merger_kernel(
                         start=(a == 0), stop=(a == PASSES - 1),
                     )
                 nc.scalar.copy(window[:, BANK * h : BANK * (h + 1)], acc[:])
-            return window
 
         def right(b, t, window=None):
-            window = first_stage(
+            if window is None:
+                window = rows.tile([P, S], F32, name="window")[:]
+            first_stage(
                 lambda a: w2_codes[b][:, a, 2 * P * t : 2 * P * (t + 1)].bitcast(E2M1),
                 lambda a: w2_planes[:, a, PASS * b + P * t : PASS * b + P * (t + 1)],
                 window,
@@ -166,29 +185,29 @@ def tile_list_curriculum_merger_kernel(
 
         z = [tile([P, PACK, MERGED], F32, f"z{b}") for b in range(PASSES)]
 
-        def left(b, t, window=None, parts=((0, MERGED),)):
-            window = first_stage(
+        def left(b, t, parts=((0, MERGED),)):
+            window = rows.tile([P, S], F32, name="window")[:]
+            first_stage(
                 lambda a: w1_codes[a, b][:, P * t : P * (t + 1)].bitcast(E4M3),
                 lambda a: w1_planes[a, b][:, P * t : P * (t + 1)],
                 window,
             )
-            for m0, m1 in parts:
-                nc.vector.tensor_tensor(
-                    z[b][:, t, m0:m1], window.indirect(p1[:, m0 // 16 : m1 // 16]), picked[b, t][:, m0:m1], MULT
-                )
+            for c0, c1 in parts:
+                offsets = p1[:, c0 // PER_COLUMN : c1 // PER_COLUMN]
+                nc.vector.tensor_tensor(z[b][:, t, c0:c1], window.indirect(offsets), picked[b, t][:, c0:c1], MULT)
 
-        def round_z(b, m0, m1, copy, slot=None):
-            z_bf[b, m0] = slot if slot is not None else tile([P, m1 - m0, PACK], BF16, f"z_bf{b}_{m0}")
+        def round_z(b, c0, c1, copy):
+            z_bf[b, c0] = tile([P, c1 - c0, PACK], BF16, f"z_bf{b}_{c0}")
             copy(
-                z_bf[b, m0].rearrange("p (c i) t -> p c t i", i=4),
-                z[b][:, :, m0:m1].rearrange("p t (c i) -> p c t i", i=4),
+                z_bf[b, c0].rearrange("p (g i) t -> p g t i", i=LINE // 4),
+                z[b][:, :, c0:c1].rearrange("p t (g i) -> p g t i", i=LINE // 4),
             )
 
-        def quantize_z(b, m0, m1):
-            codes = tile([P, m1 - m0], U32, f"z_codes{b}_{m0}")
-            plane = tile([P, m1 - m0], U8, f"z_plane{b}_{m0}")
-            nc.vector.quantize_mx(out=codes.bitcast(E4M3), scales=plane, in_=z_bf[b, m0].rearrange("p c t -> p (c t)"))
-            z_mx[b, m0, m1] = (codes, plane)
+        def quantize_z(b, c0, c1):
+            codes = tile([P, c1 - c0], U32, f"z_codes{b}_{c0}")
+            plane = tile([P, c1 - c0], U8, f"z_plane{b}_{c0}")
+            nc.vector.quantize_mx(out=codes.bitcast(E4M3), scales=plane, in_=z_bf[b, c0].rearrange("p c t -> p (c t)"))
+            z_mx[b, c0, c1] = (codes, plane)
 
         gather_words(0, 0)
         gather_words(0, 1)
@@ -198,72 +217,67 @@ def tile_list_curriculum_merger_kernel(
         gather_words(1, 1)
         load_w1(0, 1, "slot_tab1")
         order_w2(1)
-        round_w1(0, 0, scalar_round, 0, 96)
-        round_w1(0, 0, nc.vector.tensor_copy, 96, P)
+        load_w1(1, 1, "slot_w2")
+
+        round_w1_shared(0, 0)
         quantize_w1(0, 0)
-        round_w1(1, 0, scalar_round, 0, 64)
-        round_w1(1, 0, nc.vector.tensor_copy, 64, P)
+        round_w1_shared(1, 0)
         first_rows = tile([P, 2, S], F32, "first_rows", "slot_w1")
         right(0, 0, first_rows[:, 0, :])
         quantize_w1(1, 0)
         right(0, 1, first_rows[:, 1, :])
-        load_w1(1, 1, "slot_w1")
-        right(0, 2)
-        left(0, 0, tile([P, S], F32, "left00_rows", "w1_bf01"))
-        right(0, 3)
-        left(0, 1)
-        round_w1(0, 1, scalar_round, 0, 64)
-        right(1, 0)
-        left(0, 2)
-        round_w1(0, 1, scalar_round, 64, P)
-        quantize_w1(0, 1)
-        right(1, 1)
-        round_w1(1, 1, scalar_round, 0, 64)
-        left(0, 3)
-        round_w1(1, 1, nc.vector.tensor_copy, 64, P)
-        quantize_w1(1, 1)
-        right(1, 2)
+        for b, t in ((0, 2), (0, 3), (1, 0), (1, 1), (1, 2)):
+            right(b, t)
 
-        w3_codes = tile([P, PASSES, 4 * N], U8, "w3_codes", "w1_bf00")
-        nc.sync.dma_start(w3_codes.bitcast(I32), w3_words.rearrange("a p c i -> p a (c i)").bitcast(I32))
-        w3_planes = tile([P, PASSES, N], U8, "w3_planes", "picked02")
-        nc.gpsimd.memset(w3_planes.rearrange("p a c -> p (a c)").bitcast(I32), 0)
-        for q in range(4):
+        round_w1(0, 1, scalar_round, 0, SCALAR_SHARE[0, 1] // 2)
+        right(1, 3)
+        round_w1(0, 1, scalar_round, SCALAR_SHARE[0, 1] // 2, SCALAR_SHARE[0, 1])
+        quantize_w1(0, 1)
+        left(0, 0)
+        round_w1_shared(1, 1)
+        quantize_w1(1, 1)
+        for t in range(1, PACK):
+            left(0, t)
+
+        w3_codes = tile([P, PASSES, PACK * N], U8, "w3_codes", "w1_bf10")
+        nc.sync.dma_start(w3_codes.bitcast(I32), w3_words.rearrange("b p c i -> p b (c i)").bitcast(I32))
+        w3_planes = tile([P, PASSES, N], U8, "w3_planes", "picked00")
+        nc.gpsimd.memset(w3_planes.rearrange("p b c -> p (b c)").bitcast(I32), 0)
+        for quad in range(QUADRANTS):
             nc.sync.dma_start(
-                w3_planes[32 * q : 32 * q + 4, :, :].bitcast(I32),
-                w3_scales[:, 4 * q : 4 * q + 4, :].rearrange("a r c -> r a c").bitcast(I32),
+                w3_planes[32 * quad : 32 * quad + 4, :, :].bitcast(I32),
+                w3_scales[:, 4 * quad : 4 * quad + 4, :].rearrange("b r c -> r b c").bitcast(I32),
             )
-        bias_cols = tile([P, N // P], F32, "bias_cols", "w1_bf10")
+        bias_cols = tile([P, N // P], F32, "bias_cols", "w1_bf01")
         with nc.allow_non_contiguous_dma("one bias value for each partition"):
             nc.sync.dma_start(bias_cols, bias.rearrange("(n p) -> p n", p=P))
 
         left(1, 0)
-        right(1, 3)
         left(1, 1)
-        round_z(0, 0, 256, nc.scalar.copy)
-        quantize_z(0, 0, 256)
+        round_z(0, 0, MERGED // 2, nc.scalar.copy)
+        quantize_z(0, 0, MERGED // 2)
         left(1, 2)
-        round_z(0, 256, 512, nc.scalar.copy)
-        quantize_z(0, 256, 512)
-        left(1, 3, parts=((0, 256), (256, 384), (384, 512)))
-        round_z(1, 0, 256, nc.scalar.copy)
-        round_z(1, 256, 384, nc.vector.tensor_copy)
-        round_z(1, 384, 512, nc.vector.tensor_copy)
-        for m0, m1 in ((256, 384), (384, 512), (0, 256)):
-            quantize_z(1, m0, m1)
+        round_z(0, MERGED // 2, MERGED, nc.scalar.copy)
+        quantize_z(0, MERGED // 2, MERGED)
+        left(1, 3, (FIRST_PART,) + LATE_PARTS)
+        round_z(1, *FIRST_PART, nc.scalar.copy)
+        for part in LATE_PARTS:
+            round_z(1, *part, nc.vector.tensor_copy)
+        for part in LATE_PARTS + (FIRST_PART,):
+            quantize_z(1, *part)
 
         y = [tile([P, MERGED], F32, f"y{n}") for n in range(N // P)]
-        parts = list(z_mx)
+        ranges = list(z_mx)
         for n in range(N // P):
-            acc = psum.tile([P, BANK], F32, name="late", bufs=2)
-            for b, m0, m1 in parts:
-                codes, plane = z_mx[b, m0, m1]
+            acc = psum.tile([P, BANK], F32, name="y_acc", bufs=STAGE2_BANKS)
+            for b, c0, c1 in ranges:
+                codes, plane = z_mx[b, c0, c1]
                 nc.tensor.matmul_mx(
-                    out=acc[:, m0:m1],
-                    lhsT=w3_codes[:, b, 4 * P * n : 4 * P * (n + 1)].bitcast(E4M3),
+                    out=acc[:, c0:c1],
+                    lhsT=w3_codes[:, b, PACK * P * n : PACK * P * (n + 1)].bitcast(E4M3),
                     lhsT_scale=w3_planes[:, b, P * n : P * (n + 1)],
                     rhs=codes.bitcast(E4M3), rhs_scale=plane,
-                    start=((b, m0, m1) == parts[0]), stop=((b, m0, m1) == parts[-1]),
+                    start=((b, c0, c1) == ranges[0]), stop=((b, c0, c1) == ranges[-1]),
                 )
             nc.scalar.activation(y[n], acc[:], IDENTITY, bias=bias_cols[:, n : n + 1])
 
@@ -271,7 +285,7 @@ def tile_list_curriculum_merger_kernel(
         second = tile([P, N // P, TERMS], F32, "second")
         term = tile([P, N // P, TERMS], F32, "term")
         out_rows = out.rearrange("(n p) t -> p n t", p=P)
-        for n0, n1 in ((0, 2), (2, 3), (3, 4)):
+        for n0, n1 in STORES:
             for n in range(n0, n1):
                 nc.vector.tensor_copy(first[:, n, :], y[n].indirect(p3[:]))
                 nc.vector.tensor_copy(second[:, n, :], y[n].indirect(p4[:]))

@@ -14,6 +14,7 @@ U8 = mybir.dt.uint8
 E4M3 = mybir.dt.float8_e4m3fn_x4
 E2M1 = mybir.dt.float4_e2m1fn_x4
 MULT = mybir.AluOpType.mult
+ADD = mybir.AluOpType.add
 MAX = mybir.AluOpType.max
 COPY = mybir.ActivationFunctionType.Copy
 IDENTITY = mybir.ActivationFunctionType.Identity
@@ -24,14 +25,14 @@ PASS = P * PACK
 PASSES = 2
 BANK = 512
 QUADRANTS = 4
+HALF = MERGED // 2
 PER_COLUMN = 16
 LINE = 16
 
-STAGE1_BANKS = 4
-STAGE2_BANKS = 2
-WINDOWS = 8
+STAGE1_BANKS = 8
+WINDOWS = 16
 
-SCALAR_SHARE = {(0, 0): 96, (1, 0): 0, (0, 1): P, (1, 1): 64}
+SCALAR_SHARE = {(0, 0): 0, (1, 0): 0, (0, 1): 0, (1, 1): 64}
 FIRST_PART = (0, 256)
 LATE_PARTS = ((256, 384), (384, 512))
 STORES = ((0, 2), (2, 3), (3, 4))
@@ -46,77 +47,85 @@ def tile_list_curriculum_merger_kernel(
         lists = ctx.enter_context(tc.tile_pool(name="lists", bufs=1))
         keep = ctx.enter_context(tc.tile_pool(name="keep", bufs=1))
         rows = ctx.enter_context(tc.tile_pool(name="rows", bufs=WINDOWS))
+        laid = ctx.enter_context(tc.tile_pool(name="laid", bufs=1))
         psum = ctx.enter_context(tc.psum_pool(name="psum", bufs=1))
 
         def tile(shape, dtype, name, slot=None):
             return keep.tile(shape, dtype, name=name, tag=slot or name, align_bytes=64)[:]
+
+        def tile_at(shape, dtype, name, offset):
+            return laid.tile(shape, dtype, name=name, align_bytes=64, offset=offset)[:]
 
         def load_list(src, name):
             offsets = lists.tile(list(src.shape), U16, name=name)
             nc.sync.dma_start(offsets[:], src)
             return offsets
 
-        w2_rows = tile([P, H], U8, "w2_rows", "slot_w1")
-        tab_rows = tile([P, T], U8, "tab_rows", "slot_w2")
-        for dense in (w2_rows, tab_rows):
+        w2_rows = tile([P, H], U8, "w2_rows")
+        tab_rows = tile([P, T], U8, "tab_rows")
+        for dense in (tab_rows, w2_rows):
             nc.vector.memset(dense[32:64, :].bitcast(I32), 0)
             nc.vector.memset(dense[64:128, :].bitcast(I32), 0)
-        w2_planes = tile([P, PASSES, H], U8, "w2_planes")
-        v_planes = tile([P, PASSES, S], U8, "v_planes")
-        for planes in (w2_planes, v_planes):
-            nc.gpsimd.memset(planes.rearrange("p a c -> p (a c)").bitcast(I32), 0)
+        planes = tile([P, PASSES, S + H], U8, "planes")
+        nc.gpsimd.memset(planes.rearrange("p a c -> p (a c)").bitcast(I32), 0)
+        v_planes = planes[:, :, 0:S]
+        w2_planes = planes[:, :, S : S + H]
 
-        idx = load_list(offs, "idx")
-        nc.sync.dma_start(w2_rows[0:32, :].bitcast(I32), w2_scales.rearrange("a q c -> q a c").bitcast(I32))
-        nc.sync.dma_start(tab_rows[0:32, :].bitcast(I32), tab_scales.rearrange("a q t -> q a t").bitcast(I32))
-        p1 = load_list(pos1, "p1")
-        p2 = load_list(pos2, "p2")
-        p3 = load_list(pos3, "p3")
-        p4 = load_list(pos4, "p4")
-
-        tab, w2_raw, w1_raw = {}, {}, {}
+        tab, w1_raw = {}, {}
 
         def load_tab(a):
             tab[a] = tile([P, T], I32, f"tab{a}", f"slot_tab{a}")
             nc.sync.dma_start(tab[a], tab_words[a].rearrange("p t i -> p (t i)").bitcast(I32))
 
-        def load_w2(b, slot=None):
-            w2_raw[b] = tile([P, PASSES, 2 * PASS], U8, f"w2_raw{b}", slot)
+        idx = load_list(offs, "idx")
+        nc.sync.dma_start(tab_rows[0:32, :].bitcast(I32), tab_scales.rearrange("a q t -> q a t").bitcast(I32))
+        nc.sync.dma_start(w2_rows[0:32, :].bitcast(I32), w2_scales.rearrange("a q c -> q a c").bitcast(I32))
+        w2_raw = [tile([P, PASSES, 2 * PASS], U8, "w2_raw0"), None]
+
+        def load_w2(b):
             nc.sync.dma_start(
                 w2_raw[b].bitcast(I32),
                 w2_words[:, :, 2 * PASS * b : 2 * PASS * (b + 1)].rearrange("a p c -> p a c").bitcast(I32),
             )
 
+        load_w2(0)
+        load_tab(0)
+        p1 = load_list(pos1, "p1")
+        p2 = load_list(pos2, "p2")
+        p3 = load_list(pos3, "p3")
+        p4 = load_list(pos4, "p4")
+        load_tab(1)
+
         def load_w1(a, b, slot):
-            w1_raw[a, b] = tile([P, PACK, PASS], F32, f"w1_raw{a}{b}", slot)
+            if slot is None:
+                w1_raw[a, b] = tile_at([P, PACK, PASS], F32, f"w1_raw{a}{b}", 2048)
+            else:
+                w1_raw[a, b] = tile([P, PACK, PASS], F32, f"w1_raw{a}{b}", slot)
             nc.sync.dma_start(
                 w1_raw[a, b],
                 w1[PASS * a : PASS * (a + 1), PASS * b : PASS * (b + 1)].rearrange("(p j) c -> p j c", j=PACK),
             )
 
-        def spread_rows(planes, dense):
-            for quad in range(QUADRANTS):
-                nc.sync.dma_start(
-                    planes[32 * quad : 32 * quad + 4, :, :].bitcast(I32),
-                    dense[8 * quad : 8 * quad + 8, :].bitcast(I32),
-                )
-
-        load_tab(0)
-        load_w2(0)
-        load_tab(1)
-
-        w2_sorted = tile([P, H], U8, "w2_sorted")
+        v_rows = tile_at([P, S], U8, "v_rows", 1536)
+        nc.vector.tensor_copy(v_rows, tab_rows.indirect(idx[:]))
+        both = tile([P, S + H], U8, "both", "slot_b")
         nc.vector.tensor_copy(
-            w2_sorted.rearrange("p (b t g i) -> p b g t i", b=PASSES, t=PACK, i=LINE),
+            both[:, S : S + H].rearrange("p (b t g i) -> p b g t i", b=PASSES, t=PACK, i=LINE),
             w2_rows.rearrange("p (b g i t) -> p b g t i", b=PASSES, t=PACK, i=LINE),
         )
-        spread_rows(w2_planes, w2_sorted)
-        load_w1(0, 0, "slot_w1")
+        nc.vector.tensor_copy(both[0:32, 0:S].bitcast(I32), v_rows[0:32, :].bitcast(I32))
 
-        v_rows = tile([P, S], U8, "v_rows")
-        nc.vector.tensor_copy(v_rows, tab_rows.indirect(idx[:]))
-        spread_rows(v_planes, v_rows)
-        load_w2(1, "slot_w2")
+        def spread(c0, c1):
+            for quad in range(QUADRANTS):
+                nc.sync.dma_start(
+                    planes[32 * quad : 32 * quad + 4, :, c0:c1].bitcast(I32),
+                    both[8 * quad : 8 * quad + 8, c0:c1].bitcast(I32),
+                )
+
+        spread(0, S + H)
+        w2_raw[1] = tile_at([P, PASSES, 2 * PASS], U8, "w2_raw1", 0)
+        load_w2(1)
+        load_w1(0, 0, None)
 
         v_words, w2_codes, w1_bf, w1_codes, w1_planes, picked, z_bf, z_mx = {}, {}, {}, {}, {}, {}, {}, {}
 
@@ -136,150 +145,204 @@ def tile_list_curriculum_merger_kernel(
             nc.scalar.activation(dst, src, COPY)
 
         def round_w1(a, b, copy, m0, m1):
-            if (a, b) not in w1_bf:
-                w1_bf[a, b] = tile([P, PACK, P, PACK], BF16, f"w1_bf{a}{b}")
+            if b not in w1_bf:
+                w1_bf[b] = tile([P, PASSES, PACK, P, PACK], BF16, f"w1_bf{b}")
             copy(
-                w1_bf[a, b][:, :, m0:m1, :].rearrange("p t m j -> p m j t"),
+                w1_bf[b][:, a, :, m0:m1, :].rearrange("p t m j -> p m j t"),
                 w1_raw[a, b].rearrange("p j (m t) -> p m j t", t=PACK)[:, m0:m1, :, :],
+            )
+
+        def round_w1_gpsimd(a, b, m0, m1):
+            if b not in w1_bf:
+                w1_bf[b] = tile([P, PASSES, PACK, P, PACK], BF16, f"w1_bf{b}")
+            nc.gpsimd.tensor_scalar(
+                w1_bf[b][:, a, :, m0:m1, :].rearrange("p t m j -> p m t j"),
+                w1_raw[a, b].rearrange("p j (m t) -> p m t j", t=PACK)[:, m0:m1, :, :],
+                1.0, 0.0, MULT, ADD,
             )
 
         def round_w1_shared(a, b):
             share = SCALAR_SHARE[a, b]
-            if share > 0:
-                round_w1(a, b, scalar_round, 0, share)
-            round_w1(a, b, nc.vector.tensor_copy, share, P)
+            for m0 in range(0, share, 32):
+                round_w1(a, b, scalar_round, m0, m0 + 32)
+            for m0 in range(share, P, 32):
+                round_w1_gpsimd(a, b, m0, m0 + 32)
 
-        def quantize_w1(a, b):
-            w1_codes[a, b] = tile([P, PASS], U32, f"w1_codes{a}{b}")
-            w1_planes[a, b] = tile([P, PASS], U8, f"w1_planes{a}{b}")
+        def quantize_w1(b):
+            w1_codes[b] = tile([P, PASSES, PASS], U32, f"w1_codes{b}")
+            w1_planes[b] = tile([P, PASSES, PASS], U8, f"w1_planes{b}")
             nc.vector.quantize_mx(
-                out=w1_codes[a, b].bitcast(E4M3),
-                scales=w1_planes[a, b],
-                in_=w1_bf[a, b].rearrange("p t m j -> p (t m j)"),
+                out=w1_codes[b].rearrange("p a c -> p (a c)").bitcast(E4M3),
+                scales=w1_planes[b].rearrange("p a c -> p (a c)"),
+                in_=w1_bf[b].rearrange("p a t m j -> p (a t m j)"),
             )
 
         banks_taken = []
 
-        def first_stage(codes, planes, window):
-            for h in range(S // BANK):
-                acc = psum.tile([P, BANK], F32, name="acc", tag=f"bank{len(banks_taken) % STAGE1_BANKS}")
-                banks_taken.append(acc)
-                for a in range(PASSES):
-                    nc.tensor.matmul_mx(
-                        out=acc[:], lhsT=codes(a), lhsT_scale=planes(a),
-                        rhs=v_words[a, h].bitcast(E4M3), rhs_scale=v_planes[:, a, BANK * h : BANK * (h + 1)],
-                        start=(a == 0), stop=(a == PASSES - 1),
-                    )
-                nc.scalar.copy(window[:, BANK * h : BANK * (h + 1)], acc[:])
+        def bank_number(n):
+            return (n + 4) % STAGE1_BANKS
 
-        def right(b, t, window=None):
-            if window is None:
+        def bank():
+            acc = psum.tile([P, BANK], F32, name="acc", tag=f"bank{bank_number(len(banks_taken))}")
+            banks_taken.append(acc)
+            return acc
+
+        def one_pass(acc, codes, plane, a, h):
+            nc.tensor.matmul_mx(
+                out=acc[:], lhsT=codes, lhsT_scale=plane,
+                rhs=v_words[a, h].bitcast(E4M3), rhs_scale=v_planes[:, a, BANK * h : BANK * (h + 1)],
+                start=(a == 0), stop=(a == PASSES - 1),
+            )
+
+        def first_stage(codes, planes_of, opened=None, slot=None):
+            if slot is None:
                 window = rows.tile([P, S], F32, name="window")[:]
-            first_stage(
+            else:
+                window = tile([P, S], F32, "window_" + slot, slot)
+            for h in range(S // BANK):
+                if opened is None:
+                    acc = bank()
+                    one_pass(acc, codes(0), planes_of(0), 0, h)
+                else:
+                    acc = opened[h]
+                one_pass(acc, codes(1), planes_of(1), 1, h)
+                nc.scalar.copy(window[:, BANK * h : BANK * (h + 1)], acc[:])
+            return window
+
+        def w2_tile(b, t):
+            return (
                 lambda a: w2_codes[b][:, a, 2 * P * t : 2 * P * (t + 1)].bitcast(E2M1),
                 lambda a: w2_planes[:, a, PASS * b + P * t : PASS * b + P * (t + 1)],
-                window,
             )
-            picked[b, t] = tile([P, MERGED], F32, f"picked{b}{t}")
-            nc.vector.tensor_copy(picked[b, t], window.indirect(p2[:]))
 
-        z = [tile([P, PACK, MERGED], F32, f"z{b}") for b in range(PASSES)]
+        def open_right(t):
+            codes, planes_of = w2_tile(0, t)
+            opened = [bank() for h in range(S // BANK)]
+            for h in range(S // BANK):
+                one_pass(opened[h], codes(0), planes_of(0), 0, h)
+            return opened
 
-        def left(b, t, parts=((0, MERGED),)):
-            window = rows.tile([P, S], F32, name="window")[:]
-            first_stage(
-                lambda a: w1_codes[a, b][:, P * t : P * (t + 1)].bitcast(E4M3),
-                lambda a: w1_planes[a, b][:, P * t : P * (t + 1)],
-                window,
+        def right(b, t, opened=None, slot=None):
+            window = first_stage(*w2_tile(b, t), opened, slot)
+            if False:
+                for h in range(2):
+                    picked[b, t, HALF * h] = tile([P, HALF], F32, f"picked{b}{t}_{h}")
+                    cols = slice(HALF // PER_COLUMN * h, HALF // PER_COLUMN * (h + 1))
+                    nc.vector.tensor_copy(picked[b, t, HALF * h], window.indirect(p2[:, cols]))
+            else:
+                picked[b, t] = tile([P, MERGED], F32, f"picked{b}{t}")
+                nc.vector.tensor_copy(picked[b, t], window.indirect(p2[:]))
+
+        z, left_rows = {}, {}
+
+        def left(b, t, slot=None):
+            window = first_stage(
+                lambda a: w1_codes[b][:, a, P * t : P * (t + 1)].bitcast(E4M3),
+                lambda a: w1_planes[b][:, a, P * t : P * (t + 1)],
+                slot=slot,
             )
-            for c0, c1 in parts:
-                offsets = p1[:, c0 // PER_COLUMN : c1 // PER_COLUMN]
-                nc.vector.tensor_tensor(z[b][:, t, c0:c1], window.indirect(offsets), picked[b, t][:, c0:c1], MULT)
+            left_rows[b, t] = window
 
-        def round_z(b, c0, c1, copy):
-            z_bf[b, c0] = tile([P, c1 - c0, PACK], BF16, f"z_bf{b}_{c0}")
+        def merge(b, t, half, c0, c1):
+            offsets = p1[:, c0 // PER_COLUMN : c1 // PER_COLUMN]
+            other = picked[b, t][:, c0:c1]
+            nc.vector.tensor_tensor(half[:, t, :], left_rows[b, t].indirect(offsets), other, MULT)
+
+        def round_z(dst, src, copy):
             copy(
-                z_bf[b, c0].rearrange("p (g i) t -> p g t i", i=LINE // 4),
-                z[b][:, :, c0:c1].rearrange("p t (g i) -> p g t i", i=LINE // 4),
+                dst.rearrange("p (g i) t -> p g t i", i=LINE // 4),
+                src.rearrange("p t (g i) -> p g t i", i=LINE // 4),
             )
 
-        def quantize_z(b, c0, c1):
-            codes = tile([P, c1 - c0], U32, f"z_codes{b}_{c0}")
-            plane = tile([P, c1 - c0], U8, f"z_plane{b}_{c0}")
-            nc.vector.quantize_mx(out=codes.bitcast(E4M3), scales=plane, in_=z_bf[b, c0].rearrange("p c t -> p (c t)"))
-            z_mx[b, c0, c1] = (codes, plane)
+        def quantize_z(b, h):
+            codes = tile([P, HALF], U32, f"z_codes{b}{h}")
+            plane = tile([P, HALF], U8, f"z_plane{b}{h}")
+            nc.vector.quantize_mx(out=codes.bitcast(E4M3), scales=plane, in_=z_bf[b, h].rearrange("p c t -> p (c t)"))
+            z_mx[b, h] = (codes, plane)
 
         gather_words(0, 0)
+        order_w2(0)
         gather_words(0, 1)
         load_w1(1, 0, "slot_tab0")
-        order_w2(0)
         gather_words(1, 0)
         gather_words(1, 1)
         load_w1(0, 1, "slot_tab1")
+        load_w1(1, 1, "slot_b")
         order_w2(1)
-        load_w1(1, 1, "slot_w2")
 
-        round_w1_shared(0, 0)
-        quantize_w1(0, 0)
+        round_w1_gpsimd(0, 0, 64, 96)
+        round_w1_gpsimd(0, 0, 96, 128)
+        round_w1(0, 0, nc.vector.tensor_copy, 0, 64)
+        opened = [None, None, None, None]
+        for t in range(PACK):
+            right(0, t, opened[t])
         round_w1_shared(1, 0)
-        first_rows = tile([P, 2, S], F32, "first_rows", "slot_w1")
-        right(0, 0, first_rows[:, 0, :])
-        quantize_w1(1, 0)
-        right(0, 1, first_rows[:, 1, :])
-        for b, t in ((0, 2), (0, 3), (1, 0), (1, 1), (1, 2)):
-            right(b, t)
-
-        round_w1(0, 1, scalar_round, 0, SCALAR_SHARE[0, 1] // 2)
-        right(1, 3)
-        round_w1(0, 1, scalar_round, SCALAR_SHARE[0, 1] // 2, SCALAR_SHARE[0, 1])
-        quantize_w1(0, 1)
-        left(0, 0)
+        quantize_w1(0)
+        round_w1_shared(0, 1)
         round_w1_shared(1, 1)
-        quantize_w1(1, 1)
-        for t in range(1, PACK):
-            left(0, t)
+        for t in range(PACK):
+            right(1, t, slot=None)
+        quantize_w1(1)
+        z0 = tile([P, PACK, MERGED], F32, "z0", "slot_b")
+        for t in range(PACK):
+            left(0, t, slot=None)
+            merge(0, t, z0, 0, MERGED)
 
-        w3_codes = tile([P, PASSES, PACK * N], U8, "w3_codes", "w1_bf10")
+        w3_codes = tile([P, PASSES, PACK * N], U8, "w3_codes", "w2_codes0")
         nc.sync.dma_start(w3_codes.bitcast(I32), w3_words.rearrange("b p c i -> p b (c i)").bitcast(I32))
-        w3_planes = tile([P, PASSES, N], U8, "w3_planes", "picked00")
+        w3_planes = tile_at([P, PASSES, N], U8, "w3_planes", 2048)
         nc.gpsimd.memset(w3_planes.rearrange("p b c -> p (b c)").bitcast(I32), 0)
         for quad in range(QUADRANTS):
             nc.sync.dma_start(
                 w3_planes[32 * quad : 32 * quad + 4, :, :].bitcast(I32),
                 w3_scales[:, 4 * quad : 4 * quad + 4, :].rearrange("b r c -> r b c").bitcast(I32),
             )
-        bias_cols = tile([P, N // P], F32, "bias_cols", "w1_bf01")
+        bias_cols = tile([P, N // P], F32, "bias_cols", "slot_tab1")
         with nc.allow_non_contiguous_dma("one bias value for each partition"):
             nc.sync.dma_start(bias_cols, bias.rearrange("(n p) -> p n", p=P))
 
-        left(1, 0)
-        left(1, 1)
-        round_z(0, 0, MERGED // 2, nc.scalar.copy)
-        quantize_z(0, 0, MERGED // 2)
-        left(1, 2)
-        round_z(0, MERGED // 2, MERGED, nc.scalar.copy)
-        quantize_z(0, MERGED // 2, MERGED)
-        left(1, 3, (FIRST_PART,) + LATE_PARTS)
-        round_z(1, *FIRST_PART, nc.scalar.copy)
-        for part in LATE_PARTS:
-            round_z(1, *part, nc.vector.tensor_copy)
-        for part in LATE_PARTS + (FIRST_PART,):
-            quantize_z(1, *part)
-
         y = [tile([P, MERGED], F32, f"y{n}") for n in range(N // P)]
-        ranges = list(z_mx)
-        for n in range(N // P):
-            acc = psum.tile([P, BANK], F32, name="y_acc", bufs=STAGE2_BANKS)
-            for b, c0, c1 in ranges:
-                codes, plane = z_mx[b, c0, c1]
+        y_acc = {}
+
+        def second_stage(b, h):
+            codes, plane = z_mx[b, h]
+            for n in range(N // P):
+                if b == 0:
+                    y_acc[n, h] = psum.tile([P, BANK], F32, name="acc", tag=f"bank{4 * h + n}")
                 nc.tensor.matmul_mx(
-                    out=acc[:, c0:c1],
+                    out=y_acc[n, h][:, 0:HALF],
                     lhsT=w3_codes[:, b, PACK * P * n : PACK * P * (n + 1)].bitcast(E4M3),
                     lhsT_scale=w3_planes[:, b, P * n : P * (n + 1)],
                     rhs=codes.bitcast(E4M3), rhs_scale=plane,
-                    start=((b, c0, c1) == ranges[0]), stop=((b, c0, c1) == ranges[-1]),
+                    start=(b == 0), stop=(b == PASSES - 1),
                 )
-            nc.scalar.activation(y[n], acc[:], IDENTITY, bias=bias_cols[:, n : n + 1])
+                if b == PASSES - 1:
+                    nc.scalar.activation(
+                        y[n][:, HALF * h : HALF * (h + 1)], y_acc[n, h][:, 0:HALF], IDENTITY, bias=bias_cols[:, n : n + 1]
+                    )
+
+        z_early = tile([P, PACK, HALF], F32, "z_early")
+        for t in range(PACK):
+            left(1, t)
+            merge(1, t, z_early, 0, HALF)
+        z_bf[0, 0] = tile([P, HALF, PACK], BF16, "z_bf00", "w1_codes1")
+        z_bf[0, 1] = tile([P, HALF, PACK], BF16, "z_bf01", "w1_planes1")
+        z_bf[1, 0] = tile([P, HALF, PACK], BF16, "z_bf10")
+        for h in range(2):
+            round_z(z_bf[0, h], z0[:, :, HALF * h : HALF * (h + 1)], nc.scalar.copy)
+            quantize_z(0, h)
+        second_stage(0, 0)
+        second_stage(0, 1)
+        round_z(z_bf[1, 0], z_early, nc.scalar.copy)
+        z_late = tile([P, PACK, HALF], F32, "z_late", "w1_codes1")
+        quantize_z(1, 0)
+        second_stage(1, 0)
+        for t in range(PACK):
+            merge(1, t, z_late, HALF, MERGED)
+        z_bf[1, 1] = tile([P, HALF, PACK], BF16, "z_bf11", "z_bf10")
+        round_z(z_bf[1, 1], z_late, nc.vector.tensor_copy)
+        quantize_z(1, 1)
+        second_stage(1, 1)
 
         first = tile([P, N // P, TERMS], F32, "first")
         second = tile([P, N // P, TERMS], F32, "second")

@@ -88,28 +88,30 @@ def tile_list_curriculum_merger_kernel(
                 w2_words[:, :, 2 * PASS * b : 2 * PASS * (b + 1)].rearrange("a p c -> p a c").bitcast(I32),
             )
 
-        load_w2(0)
         load_tab(0)
+        load_w2(0)
         p1 = load_list(pos1, "p1")
         p2 = load_list(pos2, "p2")
         p3 = load_list(pos3, "p3")
         p4 = load_list(pos4, "p4")
         load_tab(1)
 
-        def load_w1(a, b, slot):
-            if slot is None:
-                w1_raw[a, b] = tile_at([P, PACK, PASS], F32, f"w1_raw{a}{b}", 2048)
-            else:
-                w1_raw[a, b] = tile([P, PACK, PASS], F32, f"w1_raw{a}{b}", slot)
-            nc.sync.dma_start(
-                w1_raw[a, b],
-                w1[PASS * a : PASS * (a + 1), PASS * b : PASS * (b + 1)].rearrange("(p j) c -> p j c", j=PACK),
-            )
+        def load_w1(a, b, place, m0=0, m1=P):
+            shape, name = [P, PACK, PACK * (m1 - m0)], f"w1_raw{a}{b}_{m0}"
+            raw = tile_at(shape, F32, name, place) if isinstance(place, int) else tile(shape, F32, name, place)
+            cols = slice(PASS * b + PACK * m0, PASS * b + PACK * m1)
+            nc.sync.dma_start(raw, w1[PASS * a : PASS * (a + 1), cols].rearrange("(p j) c -> p j c", j=PACK))
+            for m in range(m0, m1):
+                w1_raw[a, b, m] = (raw, m0)
 
-        v_rows = tile_at([P, S], U8, "v_rows", 1536)
+        def raw_view(a, b, m0, m1, order):
+            raw, first = w1_raw[a, b, m0]
+            return raw.rearrange("p j (m t) -> " + order, t=PACK)[:, m0 - first : m1 - first, :, :]
+
+        v_rows = tile_at([P, 7 * S], U8, "v_rows", 1536)[:, 0:S]
         nc.vector.tensor_copy(v_rows, tab_rows.indirect(idx[:]))
         both = tile([P, S + H], U8, "both", "slot_b")
-        nc.vector.tensor_copy(
+        nc.gpsimd.tensor_copy(
             both[:, S : S + H].rearrange("p (b t g i) -> p b g t i", b=PASSES, t=PACK, i=LINE),
             w2_rows.rearrange("p (b g i t) -> p b g t i", b=PASSES, t=PACK, i=LINE),
         )
@@ -125,7 +127,8 @@ def tile_list_curriculum_merger_kernel(
         spread(0, S + H)
         w2_raw[1] = tile_at([P, PASSES, 2 * PASS], U8, "w2_raw1", 0)
         load_w2(1)
-        load_w1(0, 0, None)
+        load_w1(0, 0, 4096, 0, 64)
+        load_w1(0, 0, 8192, 64, P)
 
         v_words, w2_codes, w1_bf, w1_codes, w1_planes, picked, z_bf, z_mx = {}, {}, {}, {}, {}, {}, {}, {}
 
@@ -141,6 +144,14 @@ def tile_list_curriculum_merger_kernel(
                 w2_raw[b].bitcast(U16).rearrange("p a (g i t) -> p a g t i", t=PACK, i=LINE // 2),
             )
 
+        def order_w2_gpsimd(b):
+            w2_codes[b] = tile_at([P, PASSES, 2 * PASS], U8, f"w2_codes{b}", 2048)
+            for a in range(PASSES):
+                nc.gpsimd.tensor_copy(
+                    w2_codes[b][:, a, :].rearrange("p (t g i e) -> p g t i e", t=PACK, i=LINE // 2, e=2),
+                    w2_raw[b][:, a, :].rearrange("p (g i t e) -> p g t i e", t=PACK, i=LINE // 2, e=2),
+                )
+
         def scalar_round(dst, src):
             nc.scalar.activation(dst, src, COPY)
 
@@ -149,7 +160,7 @@ def tile_list_curriculum_merger_kernel(
                 w1_bf[b] = tile([P, PASSES, PACK, P, PACK], BF16, f"w1_bf{b}")
             copy(
                 w1_bf[b][:, a, :, m0:m1, :].rearrange("p t m j -> p m j t"),
-                w1_raw[a, b].rearrange("p j (m t) -> p m j t", t=PACK)[:, m0:m1, :, :],
+                raw_view(a, b, m0, m1, "p m j t"),
             )
 
         def round_w1_gpsimd(a, b, m0, m1):
@@ -157,7 +168,7 @@ def tile_list_curriculum_merger_kernel(
                 w1_bf[b] = tile([P, PASSES, PACK, P, PACK], BF16, f"w1_bf{b}")
             nc.gpsimd.tensor_scalar(
                 w1_bf[b][:, a, :, m0:m1, :].rearrange("p t m j -> p m t j"),
-                w1_raw[a, b].rearrange("p j (m t) -> p m t j", t=PACK)[:, m0:m1, :, :],
+                raw_view(a, b, m0, m1, "p m t j"),
                 1.0, 0.0, MULT, ADD,
             )
 
@@ -261,13 +272,13 @@ def tile_list_curriculum_merger_kernel(
             z_mx[b, h] = (codes, plane)
 
         gather_words(0, 0)
-        order_w2(0)
+        order_w2_gpsimd(0)
         gather_words(0, 1)
         load_w1(1, 0, "slot_tab0")
         gather_words(1, 0)
         gather_words(1, 1)
-        load_w1(0, 1, "slot_tab1")
-        load_w1(1, 1, "slot_b")
+        load_w1(0, 1, "slot_b")
+        load_w1(1, 1, "slot_tab1")
         order_w2(1)
 
         round_w1_gpsimd(0, 0, 64, 96)
@@ -283,21 +294,21 @@ def tile_list_curriculum_merger_kernel(
         for t in range(PACK):
             right(1, t, slot=None)
         quantize_w1(1)
-        z0 = tile([P, PACK, MERGED], F32, "z0", "slot_b")
+        z0 = tile([P, PACK, MERGED], F32, "z0", "slot_tab1")
         for t in range(PACK):
             left(0, t, slot=None)
             merge(0, t, z0, 0, MERGED)
 
-        w3_codes = tile([P, PASSES, PACK * N], U8, "w3_codes", "w2_codes0")
+        w3_codes = tile([P, PASSES, PACK * N], U8, "w3_codes", "picked00")
         nc.sync.dma_start(w3_codes.bitcast(I32), w3_words.rearrange("b p c i -> p b (c i)").bitcast(I32))
-        w3_planes = tile_at([P, PASSES, N], U8, "w3_planes", 2048)
+        w3_planes = tile_at([P, PASSES, N], U8, "w3_planes", 8192)
         nc.gpsimd.memset(w3_planes.rearrange("p b c -> p (b c)").bitcast(I32), 0)
         for quad in range(QUADRANTS):
             nc.sync.dma_start(
                 w3_planes[32 * quad : 32 * quad + 4, :, :].bitcast(I32),
                 w3_scales[:, 4 * quad : 4 * quad + 4, :].rearrange("b r c -> r b c").bitcast(I32),
             )
-        bias_cols = tile([P, N // P], F32, "bias_cols", "slot_tab1")
+        bias_cols = tile([P, N // P], F32, "bias_cols", "slot_b")
         with nc.allow_non_contiguous_dma("one bias value for each partition"):
             nc.sync.dma_start(bias_cols, bias.rearrange("(n p) -> p n", p=P))
 

@@ -26,6 +26,7 @@ PASSES = 2
 BANK = 512
 QUADRANTS = 4
 HALF = MERGED // 2
+WARM_UPS = 5
 PER_COLUMN = 16
 LINE = 16
 
@@ -115,7 +116,7 @@ def tile_list_curriculum_merger_kernel(
             both[:, S : S + H].rearrange("p (b t g i) -> p b g t i", b=PASSES, t=PACK, i=LINE),
             w2_rows.rearrange("p (b g i t) -> p b g t i", b=PASSES, t=PACK, i=LINE),
         )
-        nc.vector.tensor_copy(both[0:32, 0:S].bitcast(I32), v_rows[0:32, :].bitcast(I32))
+        nc.vector.tensor_copy(both[:, 0:S].bitcast(I32), v_rows.bitcast(I32))
 
         def spread(c0, c1):
             for quad in range(QUADRANTS):
@@ -272,6 +273,12 @@ def tile_list_curriculum_merger_kernel(
             z_mx[b, h] = (codes, plane)
 
         gather_words(0, 0)
+        warm = psum.tile([P, BANK], F32, name="acc", tag="bank3")
+        for n in range(WARM_UPS):
+            nc.tensor.matmul_mx(
+                out=warm[:], lhsT=w2_raw[0][:, 0, 0 : 2 * P].bitcast(E2M1), lhsT_scale=both[:, S : S + P],
+                rhs=v_words[0, 0].bitcast(E4M3), rhs_scale=both[:, 0:BANK], start=True, stop=True,
+            )
         order_w2_gpsimd(0)
         gather_words(0, 1)
         load_w1(1, 0, "slot_tab0")

@@ -26,14 +26,16 @@ PASSES = 2
 BANK = 512
 QUADRANTS = 4
 HALF = MERGED // 2
-WARM_UPS = 5
+WARM_UPS = 4
 PER_COLUMN = 16
 LINE = 16
 
 STAGE1_BANKS = 8
 WINDOWS = 16
 
-SCALAR_SHARE = {(0, 0): 0, (1, 0): 0, (0, 1): 0, (1, 1): 64}
+SCALAR_SHARE = {(1, 0): 0, (0, 1): 0, (1, 1): 96}
+VECTOR_SHARE = {(1, 0): 0, (0, 1): 0, (1, 1): 0}
+GPSIMD_PIECE = 64
 FIRST_PART = (0, 256)
 LATE_PARTS = ((256, 384), (384, 512))
 STORES = ((0, 2), (2, 3), (3, 4))
@@ -64,11 +66,11 @@ def tile_list_curriculum_merger_kernel(
 
         w2_rows = tile([P, H], U8, "w2_rows")
         tab_rows = tile([P, T], U8, "tab_rows")
-        for dense in (tab_rows, w2_rows):
-            nc.vector.memset(dense[32:64, :].bitcast(I32), 0)
-            nc.vector.memset(dense[64:128, :].bitcast(I32), 0)
         planes = tile([P, PASSES, S + H], U8, "planes")
         nc.gpsimd.memset(planes.rearrange("p a c -> p (a c)").bitcast(I32), 0)
+        for engine, dense in ((nc.vector, tab_rows), (nc.gpsimd, w2_rows)):
+            engine.memset(dense[32:64, :].bitcast(I32), 0)
+            engine.memset(dense[64:128, :].bitcast(I32), 0)
         v_planes = planes[:, :, 0:S]
         w2_planes = planes[:, :, S : S + H]
 
@@ -97,19 +99,21 @@ def tile_list_curriculum_merger_kernel(
         p4 = load_list(pos4, "p4")
         load_tab(1)
 
-        def load_w1(a, b, place, m0=0, m1=P):
-            shape, name = [P, PACK, PACK * (m1 - m0)], f"w1_raw{a}{b}_{m0}"
+        def load_w1(a, b, place, parts):
+            width = PASS // parts
+            shape, name = [P, parts, PACK, width], f"w1_raw{a}{b}"
             raw = tile_at(shape, F32, name, place) if isinstance(place, int) else tile(shape, F32, name, place)
-            cols = slice(PASS * b + PACK * m0, PASS * b + PACK * m1)
-            nc.sync.dma_start(raw, w1[PASS * a : PASS * (a + 1), cols].rearrange("(p j) c -> p j c", j=PACK))
-            for m in range(m0, m1):
-                w1_raw[a, b, m] = (raw, m0)
+            for h in range(parts):
+                cols = slice(PASS * b + width * h, PASS * b + width * (h + 1))
+                nc.sync.dma_start(raw[:, h, :, :], w1[PASS * a : PASS * (a + 1), cols].rearrange("(p j) c -> p j c", j=PACK))
+                for m in range(P // parts * h, P // parts * (h + 1)):
+                    w1_raw[a, b, m] = (raw[:, h, :, :], P // parts * h)
 
         def raw_view(a, b, m0, m1, order):
             raw, first = w1_raw[a, b, m0]
             return raw.rearrange("p j (m t) -> " + order, t=PACK)[:, m0 - first : m1 - first, :, :]
 
-        v_rows = tile_at([P, 7 * S], U8, "v_rows", 1536)[:, 0:S]
+        v_rows = tile_at([P, 3 * S], U8, "v_rows", 1536)[:, 0:S]
         nc.vector.tensor_copy(v_rows, tab_rows.indirect(idx[:]))
         both = tile([P, S + H], U8, "both", "slot_b")
         nc.gpsimd.tensor_copy(
@@ -128,8 +132,7 @@ def tile_list_curriculum_merger_kernel(
         spread(0, S + H)
         w2_raw[1] = tile_at([P, PASSES, 2 * PASS], U8, "w2_raw1", 0)
         load_w2(1)
-        load_w1(0, 0, 4096, 0, 64)
-        load_w1(0, 0, 8192, 64, P)
+        load_w1(0, 0, 4096, 2)
 
         v_words, w2_codes, w1_bf, w1_codes, w1_planes, picked, z_bf, z_mx = {}, {}, {}, {}, {}, {}, {}, {}
 
@@ -158,7 +161,7 @@ def tile_list_curriculum_merger_kernel(
 
         def round_w1(a, b, copy, m0, m1):
             if b not in w1_bf:
-                w1_bf[b] = tile([P, PASSES, PACK, P, PACK], BF16, f"w1_bf{b}")
+                w1_bf[b] = tile([P, PASSES, PACK, P, PACK], BF16, f"w1_bf{b}", "w1_bf")
             copy(
                 w1_bf[b][:, a, :, m0:m1, :].rearrange("p t m j -> p m j t"),
                 raw_view(a, b, m0, m1, "p m j t"),
@@ -166,7 +169,7 @@ def tile_list_curriculum_merger_kernel(
 
         def round_w1_gpsimd(a, b, m0, m1):
             if b not in w1_bf:
-                w1_bf[b] = tile([P, PASSES, PACK, P, PACK], BF16, f"w1_bf{b}")
+                w1_bf[b] = tile([P, PASSES, PACK, P, PACK], BF16, f"w1_bf{b}", "w1_bf")
             nc.gpsimd.tensor_scalar(
                 w1_bf[b][:, a, :, m0:m1, :].rearrange("p t m j -> p m t j"),
                 raw_view(a, b, m0, m1, "p m t j"),
@@ -175,13 +178,14 @@ def tile_list_curriculum_merger_kernel(
 
         def round_w1_shared(a, b):
             share = SCALAR_SHARE[a, b]
-            for m0 in range(0, share, 32):
-                round_w1(a, b, scalar_round, m0, m0 + 32)
-            for m0 in range(share, P, 32):
-                round_w1_gpsimd(a, b, m0, m0 + 32)
+            rest = share + VECTOR_SHARE[a, b]
+            if rest > share:
+                round_w1(a, b, nc.vector.tensor_copy, share, rest)
+            for m0 in range(rest, P, GPSIMD_PIECE):
+                round_w1_gpsimd(a, b, m0, min(P, m0 + GPSIMD_PIECE))
 
         def quantize_w1(b):
-            w1_codes[b] = tile([P, PASSES, PASS], U32, f"w1_codes{b}")
+            w1_codes[b] = tile([P, PASSES, PASS], U32, f"w1_codes{b}", f"slot_q{b}")
             w1_planes[b] = tile([P, PASSES, PASS], U8, f"w1_planes{b}")
             nc.vector.quantize_mx(
                 out=w1_codes[b].rearrange("p a c -> p (a c)").bitcast(E4M3),
@@ -234,7 +238,7 @@ def tile_list_curriculum_merger_kernel(
                 one_pass(opened[h], codes(0), planes_of(0), 0, h)
             return opened
 
-        def right(b, t, opened=None, slot=None):
+        def right(b, t, opened=None, slot=None, into=None):
             window = first_stage(*w2_tile(b, t), opened, slot)
             if False:
                 for h in range(2):
@@ -242,7 +246,7 @@ def tile_list_curriculum_merger_kernel(
                     cols = slice(HALF // PER_COLUMN * h, HALF // PER_COLUMN * (h + 1))
                     nc.vector.tensor_copy(picked[b, t, HALF * h], window.indirect(p2[:, cols]))
             else:
-                picked[b, t] = tile([P, MERGED], F32, f"picked{b}{t}")
+                picked[b, t] = tile([P, MERGED], F32, f"picked{b}{t}", into)
                 nc.vector.tensor_copy(picked[b, t], window.indirect(p2[:]))
 
         z, left_rows = {}, {}
@@ -281,25 +285,25 @@ def tile_list_curriculum_merger_kernel(
             )
         order_w2_gpsimd(0)
         gather_words(0, 1)
-        load_w1(1, 0, "slot_tab0")
+        load_w1(1, 0, "slot_tab0", 2)
         gather_words(1, 0)
         gather_words(1, 1)
-        load_w1(0, 1, "slot_b")
-        load_w1(1, 1, "slot_tab1")
+        load_w1(0, 1, "slot_b", 1)
+        load_w1(1, 1, "slot_tab1", 1)
         order_w2(1)
 
-        round_w1_gpsimd(0, 0, 64, 96)
-        round_w1_gpsimd(0, 0, 96, 128)
+        round_w1_gpsimd(0, 0, 64, P)
         round_w1(0, 0, nc.vector.tensor_copy, 0, 64)
         opened = [None, None, None, None]
         for t in range(PACK):
-            right(0, t, opened[t])
+            right(0, t, opened[t], "slot_q0" if t == 3 else None)
         round_w1_shared(1, 0)
         quantize_w1(0)
         round_w1_shared(0, 1)
         round_w1_shared(1, 1)
         for t in range(PACK):
-            right(1, t, slot=None)
+            right(1, t, slot="slot_q1" if t == 3 else None, into="slot_tab0" if t == 0 else None)
+        round_w1(1, 1, scalar_round, 0, SCALAR_SHARE[1, 1])
         quantize_w1(1)
         z0 = tile([P, PACK, MERGED], F32, "z0", "slot_tab1")
         for t in range(PACK):
@@ -308,7 +312,7 @@ def tile_list_curriculum_merger_kernel(
 
         w3_codes = tile([P, PASSES, PACK * N], U8, "w3_codes", "picked00")
         nc.sync.dma_start(w3_codes.bitcast(I32), w3_words.rearrange("b p c i -> p b (c i)").bitcast(I32))
-        w3_planes = tile_at([P, PASSES, N], U8, "w3_planes", 8192)
+        w3_planes = tile([P, PASSES, N], U8, "w3_planes", "w2_raw0")
         nc.gpsimd.memset(w3_planes.rearrange("p b c -> p (b c)").bitcast(I32), 0)
         for quad in range(QUADRANTS):
             nc.sync.dma_start(
@@ -343,7 +347,7 @@ def tile_list_curriculum_merger_kernel(
         for t in range(PACK):
             left(1, t)
             merge(1, t, z_early, 0, HALF)
-        z_bf[0, 0] = tile([P, HALF, PACK], BF16, "z_bf00", "w1_codes1")
+        z_bf[0, 0] = tile([P, HALF, PACK], BF16, "z_bf00", "slot_q1")
         z_bf[0, 1] = tile([P, HALF, PACK], BF16, "z_bf01", "w1_planes1")
         z_bf[1, 0] = tile([P, HALF, PACK], BF16, "z_bf10")
         for h in range(2):
@@ -352,7 +356,7 @@ def tile_list_curriculum_merger_kernel(
         second_stage(0, 0)
         second_stage(0, 1)
         round_z(z_bf[1, 0], z_early, nc.scalar.copy)
-        z_late = tile([P, PACK, HALF], F32, "z_late", "w1_codes1")
+        z_late = tile([P, PACK, HALF], F32, "z_late", "slot_q1")
         quantize_z(1, 0)
         second_stage(1, 0)
         for t in range(PACK):

@@ -13,8 +13,8 @@ U16 = mybir.dt.uint16
 U8 = mybir.dt.uint8
 E4M3 = mybir.dt.float8_e4m3fn_x4
 E2M1 = mybir.dt.float4_e2m1fn_x4
-MULT = mybir.AluOpType.mult
 ADD = mybir.AluOpType.add
+MULT = mybir.AluOpType.mult
 MAX = mybir.AluOpType.max
 COPY = mybir.ActivationFunctionType.Copy
 IDENTITY = mybir.ActivationFunctionType.Identity
@@ -24,21 +24,20 @@ PACK = 4
 PASS = P * PACK
 PASSES = 2
 BANK = 512
+BANKS = 8
 QUADRANTS = 4
-HALF = MERGED // 2
-WARM_UPS = 4
+DENSE = 32
 PER_COLUMN = 16
 LINE = 16
+HALF = MERGED // 2
+WINDOWS = 14
+WARM_UPS = 4
 
-STAGE1_BANKS = 8
-WINDOWS = 16
-
-SCALAR_SHARE = {(1, 0): 0, (0, 1): 0, (1, 1): 96}
-VECTOR_SHARE = {(1, 0): 0, (0, 1): 0, (1, 1): 0}
-GPSIMD_PIECE = 64
-FIRST_PART = (0, 256)
-LATE_PARTS = ((256, 384), (384, 512))
-STORES = ((0, 2), (2, 3), (3, 4))
+PART = P // 2
+SCALAR_SHARE = 96
+STORES = ((0, 2, 0, TERMS), (2, 3, 0, TERMS), (3, 4, 0, TERMS // 2), (3, 4, TERMS // 2, TERMS))
+W2_SECOND_AT, GATHERED_AT, W2_CODES_AT, W1_FIRST_AT = 0, 1536, 2048, 4096
+GATHERED_SLOT = 3072
 
 
 def tile_list_curriculum_merger_kernel(
@@ -74,241 +73,182 @@ def tile_list_curriculum_merger_kernel(
         v_planes = planes[:, :, 0:S]
         w2_planes = planes[:, :, S : S + H]
 
-        tab, w1_raw = {}, {}
+        tab, w2_raw, w1_raw = {}, {}, {}
 
         def load_tab(a):
-            tab[a] = tile([P, T], I32, f"tab{a}", f"slot_tab{a}")
+            tab[a] = tile([P, T], I32, f"tab{a}")
             nc.sync.dma_start(tab[a], tab_words[a].rearrange("p t i -> p (t i)").bitcast(I32))
 
-        idx = load_list(offs, "idx")
-        nc.sync.dma_start(tab_rows[0:32, :].bitcast(I32), tab_scales.rearrange("a q t -> q a t").bitcast(I32))
-        nc.sync.dma_start(w2_rows[0:32, :].bitcast(I32), w2_scales.rearrange("a q c -> q a c").bitcast(I32))
-        w2_raw = [tile([P, PASSES, 2 * PASS], U8, "w2_raw0"), None]
-
-        def load_w2(b):
+        def load_w2(b, raw):
+            w2_raw[b] = raw
             nc.sync.dma_start(
-                w2_raw[b].bitcast(I32),
+                raw.bitcast(I32),
                 w2_words[:, :, 2 * PASS * b : 2 * PASS * (b + 1)].rearrange("a p c -> p a c").bitcast(I32),
             )
 
+        def load_w1(a, b, slot=None):
+            shape, name = [P, 2, PACK, PASS // 2], f"w1_raw{a}{b}"
+            raw = tile(shape, F32, name, slot) if slot else tile_at(shape, F32, name, W1_FIRST_AT)
+            w1_raw[a, b] = raw
+            for h in range(2):
+                cols = slice(PASS * b + PASS // 2 * h, PASS * b + PASS // 2 * (h + 1))
+                nc.sync.dma_start(
+                    raw[:, h, :, :], w1[PASS * a : PASS * (a + 1), cols].rearrange("(p j) c -> p j c", j=PACK)
+                )
+
+        idx = load_list(offs, "idx")
+        nc.sync.dma_start(tab_rows[0:DENSE, :].bitcast(I32), tab_scales.rearrange("a q t -> q a t").bitcast(I32))
+        nc.sync.dma_start(w2_rows[0:DENSE, :].bitcast(I32), w2_scales.rearrange("a q c -> q a c").bitcast(I32))
         load_tab(0)
-        load_w2(0)
+        load_w2(0, tile([P, PASSES, 2 * PASS], U8, "w2_raw0"))
         p1 = load_list(pos1, "p1")
         p2 = load_list(pos2, "p2")
         p3 = load_list(pos3, "p3")
         p4 = load_list(pos4, "p4")
         load_tab(1)
 
-        def load_w1(a, b, place, parts):
-            width = PASS // parts
-            shape, name = [P, parts, PACK, width], f"w1_raw{a}{b}"
-            raw = tile_at(shape, F32, name, place) if isinstance(place, int) else tile(shape, F32, name, place)
-            for h in range(parts):
-                cols = slice(PASS * b + width * h, PASS * b + width * (h + 1))
-                nc.sync.dma_start(raw[:, h, :, :], w1[PASS * a : PASS * (a + 1), cols].rearrange("(p j) c -> p j c", j=PACK))
-                for m in range(P // parts * h, P // parts * (h + 1)):
-                    w1_raw[a, b, m] = (raw[:, h, :, :], P // parts * h)
-
-        def raw_view(a, b, m0, m1, order):
-            raw, first = w1_raw[a, b, m0]
-            return raw.rearrange("p j (m t) -> " + order, t=PACK)[:, m0 - first : m1 - first, :, :]
-
-        v_rows = tile_at([P, 3 * S], U8, "v_rows", 1536)[:, 0:S]
+        v_rows = tile_at([P, GATHERED_SLOT], U8, "v_rows", GATHERED_AT)[:, 0:S]
         nc.vector.tensor_copy(v_rows, tab_rows.indirect(idx[:]))
-        both = tile([P, S + H], U8, "both", "slot_b")
+        both_rows = tile([P, S + H], U8, "both_rows")
         nc.gpsimd.tensor_copy(
-            both[:, S : S + H].rearrange("p (b t g i) -> p b g t i", b=PASSES, t=PACK, i=LINE),
+            both_rows[:, S : S + H].rearrange("p (b t g i) -> p b g t i", b=PASSES, t=PACK, i=LINE),
             w2_rows.rearrange("p (b g i t) -> p b g t i", b=PASSES, t=PACK, i=LINE),
         )
-        nc.vector.tensor_copy(both[:, 0:S].bitcast(I32), v_rows.bitcast(I32))
+        nc.vector.tensor_copy(both_rows[:, 0:S].bitcast(I32), v_rows.bitcast(I32))
+        for quad in range(QUADRANTS):
+            nc.sync.dma_start(
+                planes[32 * quad : 32 * quad + 4, :, :].bitcast(I32),
+                both_rows[8 * quad : 8 * quad + 8, :].bitcast(I32),
+            )
+        load_w2(1, tile_at([P, PASSES, 2 * PASS], U8, "w2_raw1", W2_SECOND_AT))
+        load_w1(0, 0)
 
-        def spread(c0, c1):
-            for quad in range(QUADRANTS):
-                nc.sync.dma_start(
-                    planes[32 * quad : 32 * quad + 4, :, c0:c1].bitcast(I32),
-                    both[8 * quad : 8 * quad + 8, c0:c1].bitcast(I32),
-                )
-
-        spread(0, S + H)
-        w2_raw[1] = tile_at([P, PASSES, 2 * PASS], U8, "w2_raw1", 0)
-        load_w2(1)
-        load_w1(0, 0, 4096, 2)
-
-        v_words, w2_codes, w1_bf, w1_codes, w1_planes, picked, z_bf, z_mx = {}, {}, {}, {}, {}, {}, {}, {}
+        v_words, w2_codes, w1_codes, w1_planes, picked, left_rows, z_mx, y_acc = {}, {}, {}, {}, {}, {}, {}, {}
 
         def gather_words(a, h):
             v_words[a, h] = tile([P, BANK], U32, f"v_words{a}{h}")
             cols = slice(BANK // PER_COLUMN * h, BANK // PER_COLUMN * (h + 1))
             nc.vector.tensor_copy(v_words[a, h], tab[a].bitcast(U32).indirect(idx[:, cols]))
 
-        def order_w2(b):
-            w2_codes[b] = tile([P, PASSES, 2 * PASS], U8, f"w2_codes{b}")
-            nc.vector.tensor_copy(
-                w2_codes[b].bitcast(U16).rearrange("p a (t g i) -> p a g t i", t=PACK, i=LINE // 2),
-                w2_raw[b].bitcast(U16).rearrange("p a (g i t) -> p a g t i", t=PACK, i=LINE // 2),
-            )
+        def w1_views(dst, a, b, m0, m1, walk):
+            h = m0 // PART
+            src = w1_raw[a, b][:, h, :, :].rearrange("p j (m t) -> " + walk, t=PACK)
+            return dst[:, :, m0:m1, :].rearrange("p t m j -> " + walk), src[:, m0 - PART * h : m1 - PART * h, :, :]
 
-        def order_w2_gpsimd(b):
-            w2_codes[b] = tile_at([P, PASSES, 2 * PASS], U8, f"w2_codes{b}", 2048)
-            for a in range(PASSES):
-                nc.gpsimd.tensor_copy(
-                    w2_codes[b][:, a, :].rearrange("p (t g i e) -> p g t i e", t=PACK, i=LINE // 2, e=2),
-                    w2_raw[b][:, a, :].rearrange("p (g i t e) -> p g t i e", t=PACK, i=LINE // 2, e=2),
-                )
+        def round_on_gpsimd(dst, a, b, m0, m1):
+            nc.gpsimd.tensor_scalar(*w1_views(dst, a, b, m0, m1, "p m t j"), 1.0, 0.0, MULT, ADD)
 
-        def scalar_round(dst, src):
-            nc.scalar.activation(dst, src, COPY)
+        def w1_operand(b):
+            w1_codes[b] = tile([P, PASSES * PASS], U32, f"w1_codes{b}", f"last_window{b}")
+            w1_planes[b] = tile([P, PASSES * PASS], U8, f"w1_planes{b}")
 
-        def round_w1(a, b, copy, m0, m1):
-            if b not in w1_bf:
-                w1_bf[b] = tile([P, PASSES, PACK, P, PACK], BF16, f"w1_bf{b}", "w1_bf")
-            copy(
-                w1_bf[b][:, a, :, m0:m1, :].rearrange("p t m j -> p m j t"),
-                raw_view(a, b, m0, m1, "p m j t"),
-            )
-
-        def round_w1_gpsimd(a, b, m0, m1):
-            if b not in w1_bf:
-                w1_bf[b] = tile([P, PASSES, PACK, P, PACK], BF16, f"w1_bf{b}", "w1_bf")
-            nc.gpsimd.tensor_scalar(
-                w1_bf[b][:, a, :, m0:m1, :].rearrange("p t m j -> p m t j"),
-                raw_view(a, b, m0, m1, "p m t j"),
-                1.0, 0.0, MULT, ADD,
-            )
-
-        def round_w1_shared(a, b):
-            share = SCALAR_SHARE[a, b]
-            rest = share + VECTOR_SHARE[a, b]
-            if rest > share:
-                round_w1(a, b, nc.vector.tensor_copy, share, rest)
-            for m0 in range(rest, P, GPSIMD_PIECE):
-                round_w1_gpsimd(a, b, m0, min(P, m0 + GPSIMD_PIECE))
-
-        def quantize_w1(b):
-            w1_codes[b] = tile([P, PASSES, PASS], U32, f"w1_codes{b}", f"slot_q{b}")
-            w1_planes[b] = tile([P, PASSES, PASS], U8, f"w1_planes{b}")
-            nc.vector.quantize_mx(
-                out=w1_codes[b].rearrange("p a c -> p (a c)").bitcast(E4M3),
-                scales=w1_planes[b].rearrange("p a c -> p (a c)"),
-                in_=w1_bf[b].rearrange("p a t m j -> p (a t m j)"),
-            )
+        def quantize_w1(b, cols, rounded):
+            nc.vector.quantize_mx(out=w1_codes[b][:, cols].bitcast(E4M3), scales=w1_planes[b][:, cols], in_=rounded)
 
         banks_taken = []
 
-        def bank_number(n):
-            return (n + 4) % STAGE1_BANKS
-
-        def bank():
-            acc = psum.tile([P, BANK], F32, name="acc", tag=f"bank{bank_number(len(banks_taken))}")
-            banks_taken.append(acc)
-            return acc
-
-        def one_pass(acc, codes, plane, a, h):
-            nc.tensor.matmul_mx(
-                out=acc[:], lhsT=codes, lhsT_scale=plane,
-                rhs=v_words[a, h].bitcast(E4M3), rhs_scale=v_planes[:, a, BANK * h : BANK * (h + 1)],
-                start=(a == 0), stop=(a == PASSES - 1),
-            )
-
-        def first_stage(codes, planes_of, opened=None, slot=None):
-            if slot is None:
-                window = rows.tile([P, S], F32, name="window")[:]
-            else:
-                window = tile([P, S], F32, "window_" + slot, slot)
+        def first_stage(codes, plane, window):
             for h in range(S // BANK):
-                if opened is None:
-                    acc = bank()
-                    one_pass(acc, codes(0), planes_of(0), 0, h)
-                else:
-                    acc = opened[h]
-                one_pass(acc, codes(1), planes_of(1), 1, h)
+                acc = psum.tile([P, BANK], F32, name="acc", tag=f"bank{(len(banks_taken) + BANKS // 2) % BANKS}")
+                banks_taken.append(acc)
+                for a in range(PASSES):
+                    nc.tensor.matmul_mx(
+                        out=acc[:], lhsT=codes(a), lhsT_scale=plane(a),
+                        rhs=v_words[a, h].bitcast(E4M3), rhs_scale=v_planes[:, a, BANK * h : BANK * (h + 1)],
+                        start=(a == 0), stop=(a == PASSES - 1),
+                    )
                 nc.scalar.copy(window[:, BANK * h : BANK * (h + 1)], acc[:])
-            return window
 
-        def w2_tile(b, t):
-            return (
+        def right(b, t, picked_slot=None):
+            if t == PACK - 1:
+                window = tile([P, S], F32, f"last_window{b}")
+            else:
+                window = rows.tile([P, S], F32, name="window")[:]
+            first_stage(
                 lambda a: w2_codes[b][:, a, 2 * P * t : 2 * P * (t + 1)].bitcast(E2M1),
                 lambda a: w2_planes[:, a, PASS * b + P * t : PASS * b + P * (t + 1)],
+                window,
+            )
+            picked[b, t] = tile([P, MERGED], F32, f"picked{b}{t}", picked_slot)
+            nc.vector.tensor_copy(picked[b, t], window.indirect(p2[:]))
+
+        def left(b, t):
+            left_rows[b, t] = rows.tile([P, S], F32, name="window")[:]
+            first_stage(
+                lambda a: w1_codes[b][:, PASS * a + P * t : PASS * a + P * (t + 1)].bitcast(E4M3),
+                lambda a: w1_planes[b][:, PASS * a + P * t : PASS * a + P * (t + 1)],
+                left_rows[b, t],
             )
 
-        def open_right(t):
-            codes, planes_of = w2_tile(0, t)
-            opened = [bank() for h in range(S // BANK)]
-            for h in range(S // BANK):
-                one_pass(opened[h], codes(0), planes_of(0), 0, h)
-            return opened
-
-        def right(b, t, opened=None, slot=None, into=None):
-            window = first_stage(*w2_tile(b, t), opened, slot)
-            if False:
-                for h in range(2):
-                    picked[b, t, HALF * h] = tile([P, HALF], F32, f"picked{b}{t}_{h}")
-                    cols = slice(HALF // PER_COLUMN * h, HALF // PER_COLUMN * (h + 1))
-                    nc.vector.tensor_copy(picked[b, t, HALF * h], window.indirect(p2[:, cols]))
-            else:
-                picked[b, t] = tile([P, MERGED], F32, f"picked{b}{t}", into)
-                nc.vector.tensor_copy(picked[b, t], window.indirect(p2[:]))
-
-        z, left_rows = {}, {}
-
-        def left(b, t, slot=None):
-            window = first_stage(
-                lambda a: w1_codes[b][:, a, P * t : P * (t + 1)].bitcast(E4M3),
-                lambda a: w1_planes[b][:, a, P * t : P * (t + 1)],
-                slot=slot,
-            )
-            left_rows[b, t] = window
-
-        def merge(b, t, half, c0, c1):
+        def merge(dst, b, t, c0, c1):
             offsets = p1[:, c0 // PER_COLUMN : c1 // PER_COLUMN]
-            other = picked[b, t][:, c0:c1]
-            nc.vector.tensor_tensor(half[:, t, :], left_rows[b, t].indirect(offsets), other, MULT)
+            nc.vector.tensor_tensor(dst[:, t, :], left_rows[b, t].indirect(offsets), picked[b, t][:, c0:c1], MULT)
 
-        def round_z(dst, src, copy):
+        def round_z(copy, src, name, slot=None):
+            rounded = tile([P, HALF, PACK], BF16, name, slot)
             copy(
-                dst.rearrange("p (g i) t -> p g t i", i=LINE // 4),
+                rounded.rearrange("p (g i) t -> p g t i", i=LINE // 4),
                 src.rearrange("p t (g i) -> p g t i", i=LINE // 4),
             )
+            return rounded
 
-        def quantize_z(b, h):
+        def quantize_z(b, h, rounded):
             codes = tile([P, HALF], U32, f"z_codes{b}{h}")
             plane = tile([P, HALF], U8, f"z_plane{b}{h}")
-            nc.vector.quantize_mx(out=codes.bitcast(E4M3), scales=plane, in_=z_bf[b, h].rearrange("p c t -> p (c t)"))
+            nc.vector.quantize_mx(out=codes.bitcast(E4M3), scales=plane, in_=rounded.rearrange("p c t -> p (c t)"))
             z_mx[b, h] = (codes, plane)
 
         gather_words(0, 0)
         warm = psum.tile([P, BANK], F32, name="acc", tag="bank3")
-        for n in range(WARM_UPS):
+        for warm_up in range(WARM_UPS):
             nc.tensor.matmul_mx(
-                out=warm[:], lhsT=w2_raw[0][:, 0, 0 : 2 * P].bitcast(E2M1), lhsT_scale=both[:, S : S + P],
-                rhs=v_words[0, 0].bitcast(E4M3), rhs_scale=both[:, 0:BANK], start=True, stop=True,
+                out=warm[:], lhsT=w2_raw[0][:, 0, 0 : 2 * P].bitcast(E2M1), lhsT_scale=both_rows[:, S : S + P],
+                rhs=v_words[0, 0].bitcast(E4M3), rhs_scale=both_rows[:, 0:BANK], start=True, stop=True,
             )
-        order_w2_gpsimd(0)
+        w2_codes[0] = tile_at([P, PASSES, 2 * PASS], U8, "w2_codes0", W2_CODES_AT)
+        for a in range(PASSES):
+            nc.gpsimd.tensor_copy(
+                w2_codes[0][:, a, :].rearrange("p (t g i e) -> p g t i e", t=PACK, i=LINE // 2, e=2),
+                w2_raw[0][:, a, :].rearrange("p (g i t e) -> p g t i e", t=PACK, i=LINE // 2, e=2),
+            )
         gather_words(0, 1)
-        load_w1(1, 0, "slot_tab0", 2)
+        load_w1(1, 0, "tab0")
         gather_words(1, 0)
         gather_words(1, 1)
-        load_w1(0, 1, "slot_b", 1)
-        load_w1(1, 1, "slot_tab1", 1)
-        order_w2(1)
+        load_w1(1, 1, "both_rows")
+        load_w1(0, 1, "tab1")
+        w2_codes[1] = tile([P, PASSES, 2 * PASS], U8, "w2_codes1")
+        nc.vector.tensor_copy(
+            w2_codes[1].bitcast(U16).rearrange("p a (t g i) -> p a g t i", t=PACK, i=LINE // 2),
+            w2_raw[1].bitcast(U16).rearrange("p a (g i t) -> p a g t i", t=PACK, i=LINE // 2),
+        )
 
-        round_w1_gpsimd(0, 0, 64, P)
-        round_w1(0, 0, nc.vector.tensor_copy, 0, 64)
-        opened = [None, None, None, None]
+        w1_bf0 = tile([P, PASSES, PACK, P, PACK], BF16, "w1_bf0")
+        nc.vector.tensor_copy(*w1_views(w1_bf0[:, 0], 0, 0, 0, PART, "p m j t"))
+        round_on_gpsimd(w1_bf0[:, 0], 0, 0, PART, P)
         for t in range(PACK):
-            right(0, t, opened[t], "slot_q0" if t == 3 else None)
-        round_w1_shared(1, 0)
-        quantize_w1(0)
-        round_w1_shared(0, 1)
-        round_w1_shared(1, 1)
+            right(0, t)
+        for m0 in range(0, P, PART):
+            round_on_gpsimd(w1_bf0[:, 1], 1, 0, m0, m0 + PART)
+        w1_operand(0)
+        quantize_w1(0, slice(0, PASSES * PASS), w1_bf0.rearrange("p a t m j -> p (a t m j)"))
+        w1_bf11 = tile([P, PACK, P, PACK], BF16, "w1_bf11", "w1_bf0")
+        for m0 in range(0, P, PART):
+            round_on_gpsimd(w1_bf11, 1, 1, m0, m0 + PART)
+        right(1, 0, "tab0")
+        for t in range(1, PACK):
+            right(1, t)
+        w1_bf01 = tile([P, PACK, P, PACK], BF16, "w1_bf01", "w2_codes1")
+        for m0, m1 in ((0, PART), (PART, SCALAR_SHARE)):
+            nc.scalar.activation(*w1_views(w1_bf01, 0, 1, m0, m1, "p m j t"), COPY)
+        round_on_gpsimd(w1_bf01, 0, 1, SCALAR_SHARE, P)
+        w1_operand(1)
+        quantize_w1(1, slice(PASS, 2 * PASS), w1_bf11.rearrange("p t m j -> p (t m j)"))
+        quantize_w1(1, slice(0, PASS), w1_bf01.rearrange("p t m j -> p (t m j)"))
+        z_first = tile([P, PACK, MERGED], F32, "z_first", "tab1")
         for t in range(PACK):
-            right(1, t, slot="slot_q1" if t == 3 else None, into="slot_tab0" if t == 0 else None)
-        round_w1(1, 1, scalar_round, 0, SCALAR_SHARE[1, 1])
-        quantize_w1(1)
-        z0 = tile([P, PACK, MERGED], F32, "z0", "slot_tab1")
-        for t in range(PACK):
-            left(0, t, slot=None)
-            merge(0, t, z0, 0, MERGED)
+            left(0, t)
+            merge(z_first, 0, t, 0, MERGED)
 
         w3_codes = tile([P, PASSES, PACK * N], U8, "w3_codes", "picked00")
         nc.sync.dma_start(w3_codes.bitcast(I32), w3_words.rearrange("b p c i -> p b (c i)").bitcast(I32))
@@ -319,60 +259,52 @@ def tile_list_curriculum_merger_kernel(
                 w3_planes[32 * quad : 32 * quad + 4, :, :].bitcast(I32),
                 w3_scales[:, 4 * quad : 4 * quad + 4, :].rearrange("b r c -> r b c").bitcast(I32),
             )
-        bias_cols = tile([P, N // P], F32, "bias_cols", "slot_b")
+        bias_cols = tile([P, N // P], F32, "bias_cols", "both_rows")
         with nc.allow_non_contiguous_dma("one bias value for each partition"):
             nc.sync.dma_start(bias_cols, bias.rearrange("(n p) -> p n", p=P))
 
         y = [tile([P, MERGED], F32, f"y{n}") for n in range(N // P)]
-        y_acc = {}
 
         def second_stage(b, h):
             codes, plane = z_mx[b, h]
             for n in range(N // P):
                 if b == 0:
-                    y_acc[n, h] = psum.tile([P, BANK], F32, name="acc", tag=f"bank{4 * h + n}")
+                    y_acc[n, h] = psum.tile([P, BANK], F32, name="acc", tag=f"bank{N // P * h + n}")[:, 0:HALF]
                 nc.tensor.matmul_mx(
-                    out=y_acc[n, h][:, 0:HALF],
+                    out=y_acc[n, h],
                     lhsT=w3_codes[:, b, PACK * P * n : PACK * P * (n + 1)].bitcast(E4M3),
                     lhsT_scale=w3_planes[:, b, P * n : P * (n + 1)],
                     rhs=codes.bitcast(E4M3), rhs_scale=plane,
                     start=(b == 0), stop=(b == PASSES - 1),
                 )
                 if b == PASSES - 1:
-                    nc.scalar.activation(
-                        y[n][:, HALF * h : HALF * (h + 1)], y_acc[n, h][:, 0:HALF], IDENTITY, bias=bias_cols[:, n : n + 1]
-                    )
+                    cols = slice(HALF * h, HALF * (h + 1))
+                    nc.scalar.activation(y[n][:, cols], y_acc[n, h], IDENTITY, bias=bias_cols[:, n : n + 1])
 
         z_early = tile([P, PACK, HALF], F32, "z_early")
         for t in range(PACK):
             left(1, t)
-            merge(1, t, z_early, 0, HALF)
-        z_bf[0, 0] = tile([P, HALF, PACK], BF16, "z_bf00", "slot_q1")
-        z_bf[0, 1] = tile([P, HALF, PACK], BF16, "z_bf01", "w1_planes1")
-        z_bf[1, 0] = tile([P, HALF, PACK], BF16, "z_bf10")
-        for h in range(2):
-            round_z(z_bf[0, h], z0[:, :, HALF * h : HALF * (h + 1)], nc.scalar.copy)
-            quantize_z(0, h)
+            merge(z_early, 1, t, 0, HALF)
+        for h, slot in enumerate(("last_window1", "w1_planes1")):
+            quantize_z(0, h, round_z(nc.scalar.copy, z_first[:, :, HALF * h : HALF * (h + 1)], f"z_bf0{h}", slot))
         second_stage(0, 0)
         second_stage(0, 1)
-        round_z(z_bf[1, 0], z_early, nc.scalar.copy)
-        z_late = tile([P, PACK, HALF], F32, "z_late", "slot_q1")
-        quantize_z(1, 0)
+        quantize_z(1, 0, round_z(nc.scalar.copy, z_early, "z_bf10"))
         second_stage(1, 0)
+        z_late = tile([P, PACK, HALF], F32, "z_late", "last_window1")
         for t in range(PACK):
-            merge(1, t, z_late, HALF, MERGED)
-        z_bf[1, 1] = tile([P, HALF, PACK], BF16, "z_bf11", "z_bf10")
-        round_z(z_bf[1, 1], z_late, nc.vector.tensor_copy)
-        quantize_z(1, 1)
+            merge(z_late, 1, t, HALF, MERGED)
+        quantize_z(1, 1, round_z(nc.vector.tensor_copy, z_late, "z_bf11", "z_bf10"))
         second_stage(1, 1)
 
         first = tile([P, N // P, TERMS], F32, "first")
         second = tile([P, N // P, TERMS], F32, "second")
         term = tile([P, N // P, TERMS], F32, "term")
         out_rows = out.rearrange("(n p) t -> p n t", p=P)
-        for n0, n1 in STORES:
+        for n0, n1, c0, c1 in STORES:
             for n in range(n0, n1):
-                nc.vector.tensor_copy(first[:, n, :], y[n].indirect(p3[:]))
-                nc.vector.tensor_copy(second[:, n, :], y[n].indirect(p4[:]))
-            nc.vector.tensor_tensor(term[:, n0:n1, :], first[:, n0:n1, :], second[:, n0:n1, :], MAX)
-            nc.sync.dma_start(out_rows[:, n0:n1, :], term[:, n0:n1, :])
+                if c0 == 0:
+                    nc.vector.tensor_copy(first[:, n, :], y[n].indirect(p3[:]))
+                nc.vector.tensor_copy(second[:, n, c0:c1], y[n].indirect(p4[:, c0 // PER_COLUMN : c1 // PER_COLUMN]))
+            nc.vector.tensor_tensor(term[:, n0:n1, c0:c1], first[:, n0:n1, c0:c1], second[:, n0:n1, c0:c1], MAX)
+            nc.sync.dma_start(out_rows[:, n0:n1, c0:c1], term[:, n0:n1, c0:c1])

@@ -24,7 +24,7 @@ PACK = 4
 PASS = P * PACK
 PASSES = 2
 BANK = 512
-BANKS = 8
+STAGE1_BANKS = 5
 QUADRANTS = 4
 DENSE = 32
 PER_COLUMN = 16
@@ -149,7 +149,7 @@ def tile_list_curriculum_merger_kernel(
 
         def first_stage(codes, plane, window):
             for h in range(S // BANK):
-                acc = psum.tile([P, BANK], F32, name="acc", tag=f"bank{(len(banks_taken) + BANKS // 2) % BANKS}")
+                acc = psum.tile([P, BANK], F32, name="acc", tag=f"bank{len(banks_taken) % STAGE1_BANKS}")
                 banks_taken.append(acc)
                 for a in range(PASSES):
                     nc.tensor.matmul_mx(
@@ -199,7 +199,7 @@ def tile_list_curriculum_merger_kernel(
             z_mx[b, h] = (codes, plane)
 
         gather_words(0, 0)
-        warm = psum.tile([P, BANK], F32, name="acc", tag="bank3")
+        warm = psum.tile([P, BANK], F32, name="acc", tag=f"bank{STAGE1_BANKS}")
         for warm_up in range(WARM_UPS):
             nc.tensor.matmul_mx(
                 out=warm[:], lhsT=w2_raw[0][:, 0, 0 : 2 * P].bitcast(E2M1), lhsT_scale=both_rows[:, S : S + P],

@@ -16,6 +16,8 @@ E2M1 = mybir.dt.float4_e2m1fn_x4
 ADD = mybir.AluOpType.add
 MULT = mybir.AluOpType.mult
 MAX = mybir.AluOpType.max
+SUBTRACT = mybir.AluOpType.subtract
+RELU = mybir.ActivationFunctionType.Relu
 COPY = mybir.ActivationFunctionType.Copy
 IDENTITY = mybir.ActivationFunctionType.Identity
 
@@ -35,7 +37,7 @@ WARM_UPS = 4
 
 PART = P // 2
 SCALAR_SHARE = 96
-STORES = ((0, 2, 0, TERMS), (2, 3, 0, TERMS), (3, 4, 0, TERMS // 2), (3, 4, TERMS // 2, TERMS))
+STORES = ((2, 3, 0, TERMS), (3, 4, 0, TERMS // 2), (3, 4, TERMS // 2, TERMS))
 W2_SECOND_AT, GATHERED_AT, W2_CODES_AT, W1_FIRST_AT = 0, 1536, 2048, 4096
 GATHERED_SLOT = 3072
 
@@ -127,8 +129,11 @@ def tile_list_curriculum_merger_kernel(
 
         def gather_words(a, h):
             v_words[a, h] = tile([P, BANK], U32, f"v_words{a}{h}")
-            cols = slice(BANK // PER_COLUMN * h, BANK // PER_COLUMN * (h + 1))
-            nc.vector.tensor_copy(v_words[a, h], tab[a].bitcast(U32).indirect(idx[:, cols]))
+            pieces = 2 if (a, h) == (1, 1) else 1
+            width = BANK // pieces
+            for e0 in range(0, BANK, width):
+                cols = slice((BANK * h + e0) // PER_COLUMN, (BANK * h + e0 + width) // PER_COLUMN)
+                nc.vector.tensor_copy(v_words[a, h][:, e0 : e0 + width], tab[a].bitcast(U32).indirect(idx[:, cols]))
 
         def w1_views(dst, a, b, m0, m1, walk):
             h = m0 // PART
@@ -147,8 +152,24 @@ def tile_list_curriculum_merger_kernel(
 
         banks_taken = []
 
-        def first_stage(codes, plane, window):
+        def first_columns(codes, plane, window, e0, bank):
+            acc = psum.tile([P, BANK], F32, name="acc", tag=f"bank{bank}")
+            steps = [(a, c) for a in range(PASSES) for c in range(e0, e0 + HALF, P)]
+            for a, c in steps:
+                nc.tensor.matmul_mx(
+                    out=acc[:, c - e0 : c - e0 + P], lhsT=codes(a), lhsT_scale=plane(a),
+                    rhs=v_words[a, c // BANK][:, c % BANK : c % BANK + P].bitcast(E4M3),
+                    rhs_scale=v_planes[:, a, c : c + P],
+                    start=((a, c) == steps[0]), stop=((a, c) == steps[-1]),
+                )
+            nc.scalar.copy(window[:, e0 : e0 + HALF], acc[:, 0:HALF])
+
+        def first_stage(codes, plane, window, very_first=False):
             for h in range(S // BANK):
+                if very_first and h == 1:
+                    for quarter in range(2):
+                        first_columns(codes, plane, window, BANK + HALF * quarter, STAGE1_BANKS + 1 + quarter)
+                    continue
                 acc = psum.tile([P, BANK], F32, name="acc", tag=f"bank{len(banks_taken) % STAGE1_BANKS}")
                 banks_taken.append(acc)
                 for a in range(PASSES):
@@ -167,7 +188,7 @@ def tile_list_curriculum_merger_kernel(
             first_stage(
                 lambda a: w2_codes[b][:, a, 2 * P * t : 2 * P * (t + 1)].bitcast(E2M1),
                 lambda a: w2_planes[:, a, PASS * b + P * t : PASS * b + P * (t + 1)],
-                window,
+                window, (b, t) == (0, 0),
             )
             picked[b, t] = tile([P, MERGED], F32, f"picked{b}{t}", picked_slot)
             nc.vector.tensor_copy(picked[b, t], window.indirect(p2[:]))
@@ -301,6 +322,14 @@ def tile_list_curriculum_merger_kernel(
         second = tile([P, N // P, TERMS], F32, "second")
         term = tile([P, N // P, TERMS], F32, "term")
         out_rows = out.rearrange("(n p) t -> p n t", p=P)
+        for n in range(2):
+            nc.vector.tensor_copy(second[:, n, :], y[n].indirect(p4[:]))
+        above = tile([P, 2, TERMS], F32, "above")
+        for n in range(2):
+            nc.vector.tensor_tensor(first[:, n, :], y[n].indirect(p3[:]), second[:, n, :], SUBTRACT)
+            nc.scalar.activation(above[:, n, :], first[:, n, :], RELU)
+            nc.gpsimd.tensor_tensor(term[:, n, :], above[:, n, :], second[:, n, :], ADD)
+            nc.scalar.dma_start(out_rows[:, n, :], term[:, n, :])
         for n0, n1, c0, c1 in STORES:
             for n in range(n0, n1):
                 if c0 == 0:

@@ -32,11 +32,12 @@ DENSE = 32
 PER_COLUMN = 16
 LINE = 16
 HALF = MERGED // 2
-WINDOWS = 14
+WINDOWS = 16
 WARM_UPS = 4
 
 PART = P // 2
 SCALAR_SHARE = 96
+SCALAR_LAST = 80
 STORES = ((2, 3, 0, TERMS), (3, 4, 0, TERMS // 2), (3, 4, TERMS // 2, TERMS))
 W2_SECOND_AT, GATHERED_AT, W2_CODES_AT, W1_FIRST_AT = 0, 1536, 2048, 4096
 GATHERED_SLOT = 3072
@@ -181,10 +182,7 @@ def tile_list_curriculum_merger_kernel(
                 nc.scalar.copy(window[:, BANK * h : BANK * (h + 1)], acc[:])
 
         def right(b, t, picked_slot=None):
-            if t == PACK - 1:
-                window = tile([P, S], F32, f"last_window{b}")
-            else:
-                window = rows.tile([P, S], F32, name="window")[:]
+            window = rows.tile([P, S], F32, name="window")[:]
             first_stage(
                 lambda a: w2_codes[b][:, a, 2 * P * t : 2 * P * (t + 1)].bitcast(E2M1),
                 lambda a: w2_planes[:, a, PASS * b + P * t : PASS * b + P * (t + 1)],
@@ -214,10 +212,13 @@ def tile_list_curriculum_merger_kernel(
             return rounded
 
         def quantize_z(b, h, rounded):
-            codes = tile([P, HALF], U32, f"z_codes{b}{h}")
-            plane = tile([P, HALF], U8, f"z_plane{b}{h}")
-            nc.vector.quantize_mx(out=codes.bitcast(E4M3), scales=plane, in_=rounded.rearrange("p c t -> p (c t)"))
-            z_mx[b, h] = (codes, plane)
+            if h == 0:
+                z_mx[b] = (tile([P, MERGED], U32, f"z_codes{b}"), tile([P, MERGED], U8, f"z_plane{b}"))
+            codes, plane = z_mx[b]
+            cols = slice(HALF * h, HALF * (h + 1))
+            nc.vector.quantize_mx(
+                out=codes[:, cols].bitcast(E4M3), scales=plane[:, cols], in_=rounded.rearrange("p c t -> p (c t)")
+            )
 
         gather_words(0, 0)
         warm = psum.tile([P, BANK], F32, name="acc", tag=f"bank{STAGE1_BANKS}")
@@ -229,8 +230,8 @@ def tile_list_curriculum_merger_kernel(
         w2_codes[0] = tile_at([P, PASSES, 2 * PASS], U8, "w2_codes0", W2_CODES_AT)
         for a in range(PASSES):
             nc.gpsimd.tensor_copy(
-                w2_codes[0][:, a, :].rearrange("p (t g i e) -> p g t i e", t=PACK, i=LINE // 2, e=2),
-                w2_raw[0][:, a, :].rearrange("p (g i t e) -> p g t i e", t=PACK, i=LINE // 2, e=2),
+                w2_codes[0][:, a, :].bitcast(U16).rearrange("p (t g i) -> p g t i", t=PACK, i=LINE // 2),
+                w2_raw[0][:, a, :].bitcast(U16).rearrange("p (g i t) -> p g t i", t=PACK, i=LINE // 2),
             )
         gather_words(0, 1)
         load_w1(1, 0, "tab0")
@@ -273,7 +274,7 @@ def tile_list_curriculum_merger_kernel(
 
         w3_codes = tile([P, PASSES, PACK * N], U8, "w3_codes", "picked00")
         nc.sync.dma_start(w3_codes.bitcast(I32), w3_words.rearrange("b p c i -> p b (c i)").bitcast(I32))
-        w3_planes = tile([P, PASSES, N], U8, "w3_planes", "w2_raw0")
+        w3_planes = tile([P, PASSES, N], U8, "w3_planes", "w2_codes1")
         nc.gpsimd.memset(w3_planes.rearrange("p b c -> p (b c)").bitcast(I32), 0)
         for quad in range(QUADRANTS):
             nc.sync.dma_start(
@@ -287,20 +288,26 @@ def tile_list_curriculum_merger_kernel(
         y = [tile([P, MERGED], F32, f"y{n}") for n in range(N // P)]
 
         def second_stage(b, h):
-            codes, plane = z_mx[b, h]
+            codes, plane = z_mx[b]
             for n in range(N // P):
-                if b == 0:
-                    y_acc[n, h] = psum.tile([P, BANK], F32, name="acc", tag=f"bank{N // P * h + n}")[:, 0:HALF]
+                split = n < 2
+                cols = slice(HALF * h, HALF * (h + 1))
+                if b == PASSES - 1 and not split:
+                    if h == 0:
+                        continue
+                    cols = slice(0, MERGED)
+                if b == 0 and (split or h == 0):
+                    y_acc[n, h] = psum.tile([P, BANK], F32, name="acc", tag=f"bank{N // P * (1 - h) + n}")[:]
+                acc = y_acc[n, h if split else 0]
                 nc.tensor.matmul_mx(
-                    out=y_acc[n, h],
+                    out=acc[:, cols],
                     lhsT=w3_codes[:, b, PACK * P * n : PACK * P * (n + 1)].bitcast(E4M3),
                     lhsT_scale=w3_planes[:, b, P * n : P * (n + 1)],
-                    rhs=codes.bitcast(E4M3), rhs_scale=plane,
-                    start=(b == 0), stop=(b == PASSES - 1),
+                    rhs=codes[:, cols].bitcast(E4M3), rhs_scale=plane[:, cols],
+                    start=(b == 0 and (split or h == 0)), stop=(b == PASSES - 1 and (split or h == 1)),
                 )
-                if b == PASSES - 1:
-                    cols = slice(HALF * h, HALF * (h + 1))
-                    nc.scalar.activation(y[n][:, cols], y_acc[n, h], IDENTITY, bias=bias_cols[:, n : n + 1])
+                if b == PASSES - 1 and (split or h == 1):
+                    nc.scalar.activation(y[n][:, cols], acc[:, cols], IDENTITY, bias=bias_cols[:, n : n + 1])
 
         z_early = tile([P, PACK, HALF], F32, "z_early")
         for t in range(PACK):
@@ -312,10 +319,16 @@ def tile_list_curriculum_merger_kernel(
         second_stage(0, 1)
         quantize_z(1, 0, round_z(nc.scalar.copy, z_early, "z_bf10"))
         second_stage(1, 0)
-        z_late = tile([P, PACK, HALF], F32, "z_late", "last_window1")
+        z_late = z_first[:, :, 0:HALF]
         for t in range(PACK):
             merge(z_late, 1, t, HALF, MERGED)
-        quantize_z(1, 1, round_z(nc.vector.tensor_copy, z_late, "z_bf11", "z_bf10"))
+        z_bf11 = tile([P, HALF, PACK], BF16, "z_bf11", "z_early")
+        for copy, c0, c1 in ((nc.scalar.copy, 0, SCALAR_LAST), (nc.vector.tensor_copy, SCALAR_LAST, HALF)):
+            copy(
+                z_bf11[:, c0:c1, :].rearrange("p (g i) t -> p g t i", i=LINE // 4),
+                z_late[:, :, c0:c1].rearrange("p t (g i) -> p g t i", i=LINE // 4),
+            )
+        quantize_z(1, 1, z_bf11)
         second_stage(1, 1)
 
         first = tile([P, N // P, TERMS], F32, "first")

@@ -69,10 +69,10 @@ def tile_list_curriculum_merger_kernel(
         w2_rows = tile([P, H], U8, "w2_rows")
         tab_rows = tile([P, T], U8, "tab_rows")
         planes = tile([P, PASSES, S + H], U8, "planes")
-        nc.gpsimd.memset(planes.rearrange("p a c -> p (a c)").bitcast(I32), 0)
-        for engine, dense in ((nc.vector, tab_rows), (nc.gpsimd, w2_rows)):
-            engine.memset(dense[32:64, :].bitcast(I32), 0)
-            engine.memset(dense[64:128, :].bitcast(I32), 0)
+        for dense in (tab_rows, w2_rows):
+            nc.gpsimd.memset(dense[32:64, :].bitcast(I32), 0)
+            nc.gpsimd.memset(dense[64:128, :].bitcast(I32), 0)
+        nc.vector.memset(planes.rearrange("p a c -> p (a c)").bitcast(I32), 0)
         v_planes = planes[:, :, 0:S]
         w2_planes = planes[:, :, S : S + H]
 
@@ -145,7 +145,7 @@ def tile_list_curriculum_merger_kernel(
             nc.gpsimd.tensor_scalar(*w1_views(dst, a, b, m0, m1, "p m t j"), 1.0, 0.0, MULT, ADD)
 
         def w1_operand(b):
-            w1_codes[b] = tile([P, PASSES * PASS], U32, f"w1_codes{b}", f"last_window{b}")
+            w1_codes[b] = tile([P, PASSES * PASS], U32, f"w1_codes{b}", ("w2_fifth", "tab1")[b])
             w1_planes[b] = tile([P, PASSES * PASS], U8, f"w1_planes{b}")
 
         def quantize_w1(b, cols, rounded):
@@ -184,7 +184,7 @@ def tile_list_curriculum_merger_kernel(
         def right(b, t, picked_slot=None):
             window = rows.tile([P, S], F32, name="window")[:]
             first_stage(
-                lambda a: w2_codes[b][:, a, 2 * P * t : 2 * P * (t + 1)].bitcast(E2M1),
+                lambda a: w2_tile[b, t][:, a, :].bitcast(E2M1),
                 lambda a: w2_planes[:, a, PASS * b + P * t : PASS * b + P * (t + 1)],
                 window, (b, t) == (0, 0),
             )
@@ -233,17 +233,22 @@ def tile_list_curriculum_merger_kernel(
                 w2_codes[0][:, a, :].bitcast(U16).rearrange("p (t g i) -> p g t i", t=PACK, i=LINE // 2),
                 w2_raw[0][:, a, :].bitcast(U16).rearrange("p (g i t) -> p g t i", t=PACK, i=LINE // 2),
             )
+        w2_tile = {(0, t): w2_codes[0][:, :, 2 * P * t : 2 * P * (t + 1)] for t in range(PACK)}
         gather_words(0, 1)
         load_w1(1, 0, "tab0")
         gather_words(1, 0)
         gather_words(1, 1)
         load_w1(1, 1, "both_rows")
         load_w1(0, 1, "tab1")
-        w2_codes[1] = tile([P, PASSES, 2 * PASS], U8, "w2_codes1")
-        nc.vector.tensor_copy(
-            w2_codes[1].bitcast(U16).rearrange("p a (t g i) -> p a g t i", t=PACK, i=LINE // 2),
-            w2_raw[1].bitcast(U16).rearrange("p a (g i t) -> p a g t i", t=PACK, i=LINE // 2),
-        )
+        w2_fifth = tile([P, PASSES, 2 * P], U8, "w2_fifth")
+        w2_rest = tile([P, PASSES, 2 * P * (PACK - 1)], U8, "w2_codes1")
+        for codes, t0, t1 in ((w2_fifth, 0, 1), (w2_rest, 1, PACK)):
+            nc.vector.tensor_copy(
+                codes.bitcast(U16).rearrange("p a (t g i) -> p a g t i", t=t1 - t0, i=LINE // 2),
+                w2_raw[1].bitcast(U16).rearrange("p a (g i t) -> p a g t i", t=PACK, i=LINE // 2)[:, :, :, t0:t1, :],
+            )
+            for t in range(t0, t1):
+                w2_tile[1, t] = codes[:, :, 2 * P * (t - t0) : 2 * P * (t - t0 + 1)]
 
         w1_bf0 = tile([P, PASSES, PACK, P, PACK], BF16, "w1_bf0")
         nc.vector.tensor_copy(*w1_views(w1_bf0[:, 0], 0, 0, 0, PART, "p m j t"))
@@ -267,7 +272,9 @@ def tile_list_curriculum_merger_kernel(
         w1_operand(1)
         quantize_w1(1, slice(PASS, 2 * PASS), w1_bf11.rearrange("p t m j -> p (t m j)"))
         quantize_w1(1, slice(0, PASS), w1_bf01.rearrange("p t m j -> p (t m j)"))
-        z_first = tile([P, PACK, MERGED], F32, "z_first", "tab1")
+        z_rows = tile([P, HALF + PACK * MERGED], F32, "z_rows", "both_rows")
+        z_first = z_rows[:, HALF:].rearrange("p (t c) -> p t c", t=PACK)
+        z_late = z_rows[:, 0 : PACK * HALF].rearrange("p (t c) -> p t c", t=PACK)
         for t in range(PACK):
             left(0, t)
             merge(z_first, 0, t, 0, MERGED)
@@ -281,7 +288,7 @@ def tile_list_curriculum_merger_kernel(
                 w3_planes[32 * quad : 32 * quad + 4, :, :].bitcast(I32),
                 w3_scales[:, 4 * quad : 4 * quad + 4, :].rearrange("b r c -> r b c").bitcast(I32),
             )
-        bias_cols = tile([P, N // P], F32, "bias_cols", "both_rows")
+        bias_cols = tile([P, N // P], F32, "bias_cols", "picked01")
         with nc.allow_non_contiguous_dma("one bias value for each partition"):
             nc.sync.dma_start(bias_cols, bias.rearrange("(n p) -> p n", p=P))
 
@@ -313,14 +320,14 @@ def tile_list_curriculum_merger_kernel(
         for t in range(PACK):
             left(1, t)
             merge(z_early, 1, t, 0, HALF)
-        for h, slot in enumerate(("last_window1", "w1_planes1")):
+        merge(z_late, 1, 0, HALF, MERGED)
+        for h, slot in enumerate(("tab1", "w1_planes1")):
             quantize_z(0, h, round_z(nc.scalar.copy, z_first[:, :, HALF * h : HALF * (h + 1)], f"z_bf0{h}", slot))
         second_stage(0, 0)
         second_stage(0, 1)
         quantize_z(1, 0, round_z(nc.scalar.copy, z_early, "z_bf10"))
         second_stage(1, 0)
-        z_late = z_first[:, :, 0:HALF]
-        for t in range(PACK):
+        for t in range(1, PACK):
             merge(z_late, 1, t, HALF, MERGED)
         z_bf11 = tile([P, HALF, PACK], BF16, "z_bf11", "z_early")
         for copy, c0, c1 in ((nc.scalar.copy, 0, SCALAR_LAST), (nc.vector.tensor_copy, SCALAR_LAST, HALF)):

@@ -99,16 +99,18 @@ def tile_list_curriculum_merger_kernel(
                     raw[:, h, :, :], w1[PASS * a : PASS * (a + 1), cols].rearrange("(p j) c -> p j c", j=PACK)
                 )
 
-        idx = load_list(offs, "idx")
         nc.sync.dma_start(tab_rows[0:DENSE, :].bitcast(I32), tab_scales.rearrange("a q t -> q a t").bitcast(I32))
+        idx = load_list(offs, "idx")
         nc.sync.dma_start(w2_rows[0:DENSE, :].bitcast(I32), w2_scales.rearrange("a q c -> q a c").bitcast(I32))
         load_tab(0)
-        load_w2(0, tile([P, PASSES, 2 * PASS], U8, "w2_raw0"))
+        w2_raw[0] = tile([P, PASSES, 2 * PASS], U8, "w2_raw0")
+        nc.sync.dma_start(w2_raw[0][:, 0, :].bitcast(I32), w2_words[0, :, 0 : 2 * PASS].bitcast(I32))
         p1 = load_list(pos1, "p1")
         p2 = load_list(pos2, "p2")
         p3 = load_list(pos3, "p3")
         p4 = load_list(pos4, "p4")
         load_tab(1)
+        nc.sync.dma_start(w2_raw[0][:, 1, :].bitcast(I32), w2_words[1, :, 0 : 2 * PASS].bitcast(I32))
 
         v_rows = tile_at([P, GATHERED_SLOT], U8, "v_rows", GATHERED_AT)[:, 0:S]
         nc.vector.tensor_copy(v_rows, tab_rows.indirect(idx[:]))
@@ -153,50 +155,68 @@ def tile_list_curriculum_merger_kernel(
 
         banks_taken = []
 
-        def first_columns(codes, plane, window, e0, bank):
-            acc = psum.tile([P, BANK], F32, name="acc", tag=f"bank{bank}")
-            steps = [(a, c) for a in range(PASSES) for c in range(e0, e0 + HALF, P)]
-            for a, c in steps:
-                nc.tensor.matmul_mx(
-                    out=acc[:, c - e0 : c - e0 + P], lhsT=codes(a), lhsT_scale=plane(a),
-                    rhs=v_words[a, c // BANK][:, c % BANK : c % BANK + P].bitcast(E4M3),
-                    rhs_scale=v_planes[:, a, c : c + P],
-                    start=((a, c) == steps[0]), stop=((a, c) == steps[-1]),
-                )
-            nc.scalar.copy(window[:, e0 : e0 + HALF], acc[:, 0:HALF])
+        def next_bank():
+            acc = psum.tile([P, BANK], F32, name="acc", tag=f"bank{len(banks_taken) % STAGE1_BANKS}")
+            banks_taken.append(acc)
+            return acc
 
-        def first_stage(codes, plane, window, very_first=False):
-            for h in range(S // BANK):
-                if very_first and h == 1:
-                    for quarter in range(2):
-                        first_columns(codes, plane, window, BANK + HALF * quarter, STAGE1_BANKS + 1 + quarter)
-                    continue
-                acc = psum.tile([P, BANK], F32, name="acc", tag=f"bank{len(banks_taken) % STAGE1_BANKS}")
-                banks_taken.append(acc)
+        def multiply(acc, codes, plane, a, e0, e1, width):
+            for e in range(e0, e1, width):
+                nc.tensor.matmul_mx(
+                    out=acc[:, e - e0 : e - e0 + width], lhsT=codes(a), lhsT_scale=plane(a),
+                    rhs=v_words[a, e // BANK][:, e % BANK : e % BANK + width].bitcast(E4M3),
+                    rhs_scale=v_planes[:, a, e : e + width],
+                    start=(a == 0 and e == e0), stop=(a == PASSES - 1 and e + width == e1),
+                )
+
+        def first_stage(codes, plane, window, halves):
+            for h in halves:
+                acc = next_bank()
                 for a in range(PASSES):
-                    nc.tensor.matmul_mx(
-                        out=acc[:], lhsT=codes(a), lhsT_scale=plane(a),
-                        rhs=v_words[a, h].bitcast(E4M3), rhs_scale=v_planes[:, a, BANK * h : BANK * (h + 1)],
-                        start=(a == 0), stop=(a == PASSES - 1),
-                    )
+                    multiply(acc, codes, plane, a, BANK * h, BANK * (h + 1), BANK)
                 nc.scalar.copy(window[:, BANK * h : BANK * (h + 1)], acc[:])
 
-        def right(b, t, picked_slot=None):
-            window = rows.tile([P, S], F32, name="window")[:]
-            first_stage(
+        def w2_operand(b, t):
+            return (
                 lambda a: w2_tile[b, t][:, a, :].bitcast(E2M1),
                 lambda a: w2_planes[:, a, PASS * b + P * t : PASS * b + P * (t + 1)],
-                window, (b, t) == (0, 0),
             )
-            picked[b, t] = tile([P, MERGED], F32, f"picked{b}{t}", picked_slot)
+
+        def pick(b, t, window, slot=None):
+            picked[b, t] = tile([P, MERGED], F32, f"picked{b}{t}", slot)
             nc.vector.tensor_copy(picked[b, t], window.indirect(p2[:]))
+
+        def right(b, t, slot=None):
+            window = rows.tile([P, S], F32, name="window")[:]
+            first_stage(*w2_operand(b, t), window, range(S // BANK))
+            pick(b, t, window, slot)
+
+        def first_two_of_right():
+            first_window = rows.tile([P, S], F32, name="window")[:]
+            first_stage(*w2_operand(0, 0), first_window, [0])
+            pieces = []
+            for piece in range(2):
+                acc = psum.tile([P, BANK], F32, name="acc", tag=f"bank{STAGE1_BANKS + 1 + piece}")
+                pieces.append((acc, BANK + HALF * piece, BANK + HALF * (piece + 1)))
+                multiply(acc, *w2_operand(0, 0), 0, pieces[piece][1], pieces[piece][2], P)
+            opened = next_bank()
+            multiply(opened, *w2_operand(0, 1), 0, 0, BANK, BANK)
+            for acc, e0, e1 in pieces:
+                multiply(acc, *w2_operand(0, 0), 1, e0, e1, P)
+                nc.scalar.copy(first_window[:, e0:e1], acc[:, 0:HALF])
+            pick(0, 0, first_window)
+            second_window = rows.tile([P, S], F32, name="window")[:]
+            multiply(opened, *w2_operand(0, 1), 1, 0, BANK, BANK)
+            nc.scalar.copy(second_window[:, 0:BANK], opened[:])
+            first_stage(*w2_operand(0, 1), second_window, [1])
+            pick(0, 1, second_window)
 
         def left(b, t):
             left_rows[b, t] = rows.tile([P, S], F32, name="window")[:]
             first_stage(
                 lambda a: w1_codes[b][:, PASS * a + P * t : PASS * a + P * (t + 1)].bitcast(E4M3),
                 lambda a: w1_planes[b][:, PASS * a + P * t : PASS * a + P * (t + 1)],
-                left_rows[b, t],
+                left_rows[b, t], range(S // BANK),
             )
 
         def merge(dst, b, t, c0, c1):
@@ -253,7 +273,8 @@ def tile_list_curriculum_merger_kernel(
         w1_bf0 = tile([P, PASSES, PACK, P, PACK], BF16, "w1_bf0")
         nc.vector.tensor_copy(*w1_views(w1_bf0[:, 0], 0, 0, 0, PART, "p m j t"))
         round_on_gpsimd(w1_bf0[:, 0], 0, 0, PART, P)
-        for t in range(PACK):
+        first_two_of_right()
+        for t in range(2, PACK):
             right(0, t)
         for m0 in range(0, P, PART):
             round_on_gpsimd(w1_bf0[:, 1], 1, 0, m0, m0 + PART)

@@ -36,10 +36,12 @@ WINDOWS = 16
 WARM_UPS = 4
 
 PART = P // 2
-SCALAR_SHARE = 96
+SCALAR_SHARE = 80
 SCALAR_LAST = 80
 STORES = ((2, 3, 0, TERMS), (3, 4, 0, TERMS // 2), (3, 4, TERMS // 2, TERMS))
 W2_SECOND_AT, GATHERED_AT, W2_CODES_AT, W1_FIRST_AT = 0, 1536, 2048, 4096
+TAB_FIRST_AT, TAB_SECOND_AT = 12288, 20480
+RAW = 8192
 GATHERED_SLOT = 3072
 
 
@@ -79,7 +81,7 @@ def tile_list_curriculum_merger_kernel(
         tab, w2_raw, w1_raw = {}, {}, {}
 
         def load_tab(a):
-            tab[a] = tile([P, T], I32, f"tab{a}")
+            tab[a] = tile_at([P, (a + 1) * T], I32, f"tab{a}", (TAB_FIRST_AT, TAB_SECOND_AT)[a])[:, 0:T]
             nc.sync.dma_start(tab[a], tab_words[a].rearrange("p t i -> p (t i)").bitcast(I32))
 
         def load_w2(b, raw):
@@ -89,9 +91,9 @@ def tile_list_curriculum_merger_kernel(
                 w2_words[:, :, 2 * PASS * b : 2 * PASS * (b + 1)].rearrange("a p c -> p a c").bitcast(I32),
             )
 
-        def load_w1(a, b, slot=None):
+        def load_w1(a, b, slot):
             shape, name = [P, 2, PACK, PASS // 2], f"w1_raw{a}{b}"
-            raw = tile(shape, F32, name, slot) if slot else tile_at(shape, F32, name, W1_FIRST_AT)
+            raw = tile_at(shape, F32, name, slot)
             w1_raw[a, b] = raw
             for h in range(2):
                 cols = slice(PASS * b + PASS // 2 * h, PASS * b + PASS // 2 * (h + 1))
@@ -126,7 +128,7 @@ def tile_list_curriculum_merger_kernel(
                 both_rows[8 * quad : 8 * quad + 8, :].bitcast(I32),
             )
         load_w2(1, tile_at([P, PASSES, 2 * PASS], U8, "w2_raw1", W2_SECOND_AT))
-        load_w1(0, 0)
+        load_w1(0, 0, W1_FIRST_AT)
 
         v_words, w2_codes, w1_codes, w1_planes, picked, left_rows, z_mx, y_acc = {}, {}, {}, {}, {}, {}, {}, {}
 
@@ -138,16 +140,20 @@ def tile_list_curriculum_merger_kernel(
                 cols = slice((BANK * h + e0) // PER_COLUMN, (BANK * h + e0 + width) // PER_COLUMN)
                 nc.vector.tensor_copy(v_words[a, h][:, e0 : e0 + width], tab[a].bitcast(U32).indirect(idx[:, cols]))
 
-        def w1_views(dst, a, b, m0, m1, walk):
+        def w1_views(dst, a, b, m0, m1, walk, t0=0, t1=PACK):
             h = m0 // PART
-            src = w1_raw[a, b][:, h, :, :].rearrange("p j (m t) -> " + walk, t=PACK)
-            return dst[:, :, m0:m1, :].rearrange("p t m j -> " + walk), src[:, m0 - PART * h : m1 - PART * h, :, :]
+            src = w1_raw[a, b][:, h, :, :].rearrange("p j (m t) -> p t m j", t=PACK)
+            src = src[:, t0:t1, m0 - PART * h : m1 - PART * h, :]
+            return dst[:, :, m0:m1, :].rearrange("p t m j -> " + walk), src.rearrange("p t m j -> " + walk)
 
-        def round_on_gpsimd(dst, a, b, m0, m1):
-            nc.gpsimd.tensor_scalar(*w1_views(dst, a, b, m0, m1, "p m t j"), 1.0, 0.0, MULT, ADD)
+        def round_on_gpsimd(dst, a, b, m0, m1, t1=PACK):
+            nc.gpsimd.tensor_scalar(*w1_views(dst, a, b, m0, m1, "p m t j", 0, t1), 1.0, 0.0, MULT, ADD)
 
         def w1_operand(b):
-            w1_codes[b] = tile([P, PASSES * PASS], U32, f"w1_codes{b}", ("w2_fifth", "tab1")[b])
+            if b == 0:
+                w1_codes[b] = tile_at([P, PASSES * PASS], U32, "w1_codes0", TAB_FIRST_AT)
+            else:
+                w1_codes[b] = tile_at([P, PASSES * PASS], U32, "w1_codes1", TAB_SECOND_AT)
             w1_planes[b] = tile([P, PASSES * PASS], U8, f"w1_planes{b}")
 
         def quantize_w1(b, cols, rounded):
@@ -178,18 +184,21 @@ def tile_list_curriculum_merger_kernel(
 
         def w2_operand(b, t):
             return (
-                lambda a: w2_tile[b, t][:, a, :].bitcast(E2M1),
+                lambda a: w2_codes[b][:, a, 2 * P * t : 2 * P * (t + 1)].bitcast(E2M1),
                 lambda a: w2_planes[:, a, PASS * b + P * t : PASS * b + P * (t + 1)],
             )
 
-        def pick(b, t, window, slot=None):
-            picked[b, t] = tile([P, MERGED], F32, f"picked{b}{t}", slot)
+        def pick(b, t, window):
+            if (b, t) == (1, 0):
+                picked[b, t] = tile_at([P, MERGED], F32, "picked10", TAB_FIRST_AT + 4 * PASSES * PASS)
+            else:
+                picked[b, t] = tile([P, MERGED], F32, f"picked{b}{t}")
             nc.vector.tensor_copy(picked[b, t], window.indirect(p2[:]))
 
-        def right(b, t, slot=None):
+        def right(b, t):
             window = rows.tile([P, S], F32, name="window")[:]
             first_stage(*w2_operand(b, t), window, range(S // BANK))
-            pick(b, t, window, slot)
+            pick(b, t, window)
 
         def first_two_of_right():
             first_window = rows.tile([P, S], F32, name="window")[:]
@@ -253,38 +262,36 @@ def tile_list_curriculum_merger_kernel(
                 w2_codes[0][:, a, :].bitcast(U16).rearrange("p (t g i) -> p g t i", t=PACK, i=LINE // 2),
                 w2_raw[0][:, a, :].bitcast(U16).rearrange("p (g i t) -> p g t i", t=PACK, i=LINE // 2),
             )
-        w2_tile = {(0, t): w2_codes[0][:, :, 2 * P * t : 2 * P * (t + 1)] for t in range(PACK)}
         gather_words(0, 1)
-        load_w1(1, 0, "tab0")
+        load_w1(1, 0, TAB_FIRST_AT)
         gather_words(1, 0)
         gather_words(1, 1)
-        load_w1(1, 1, "both_rows")
-        load_w1(0, 1, "tab1")
-        w2_fifth = tile([P, PASSES, 2 * P], U8, "w2_fifth")
-        w2_rest = tile([P, PASSES, 2 * P * (PACK - 1)], U8, "w2_codes1")
-        for codes, t0, t1 in ((w2_fifth, 0, 1), (w2_rest, 1, PACK)):
-            nc.vector.tensor_copy(
-                codes.bitcast(U16).rearrange("p a (t g i) -> p a g t i", t=t1 - t0, i=LINE // 2),
-                w2_raw[1].bitcast(U16).rearrange("p a (g i t) -> p a g t i", t=PACK, i=LINE // 2)[:, :, :, t0:t1, :],
-            )
-            for t in range(t0, t1):
-                w2_tile[1, t] = codes[:, :, 2 * P * (t - t0) : 2 * P * (t - t0 + 1)]
+        load_w1(1, 1, TAB_SECOND_AT + RAW)
+        load_w1(0, 1, TAB_SECOND_AT)
+        w2_codes[1] = tile([P, PASSES, 2 * PASS], U8, "w2_codes1")
+        nc.vector.tensor_copy(
+            w2_codes[1].bitcast(U16).rearrange("p a (t g i) -> p a g t i", t=PACK, i=LINE // 2),
+            w2_raw[1].bitcast(U16).rearrange("p a (g i t) -> p a g t i", t=PACK, i=LINE // 2),
+        )
 
-        w1_bf0 = tile([P, PASSES, PACK, P, PACK], BF16, "w1_bf0")
-        nc.vector.tensor_copy(*w1_views(w1_bf0[:, 0], 0, 0, 0, PART, "p m j t"))
-        round_on_gpsimd(w1_bf0[:, 0], 0, 0, PART, P)
+        w1_bf0 = tile([P, PASSES * PACK - 1, P, PACK], BF16, "w1_bf0")
+        nc.vector.tensor_copy(*w1_views(w1_bf0[:, 0:PACK], 0, 0, 0, PART, "p m j t"))
+        round_on_gpsimd(w1_bf0[:, 0:PACK], 0, 0, PART, P)
         first_two_of_right()
         for t in range(2, PACK):
             right(0, t)
+        w1_last = tile_at([P, 1, P, PACK], BF16, "w1_last", W2_CODES_AT)
         for m0 in range(0, P, PART):
-            round_on_gpsimd(w1_bf0[:, 1], 1, 0, m0, m0 + PART)
+            round_on_gpsimd(w1_bf0[:, PACK:], 1, 0, m0, m0 + PART, PACK - 1)
+            nc.scalar.activation(*w1_views(w1_last, 1, 0, m0, m0 + PART, "p t m j", PACK - 1, PACK), COPY)
         w1_operand(0)
-        quantize_w1(0, slice(0, PASSES * PASS), w1_bf0.rearrange("p a t m j -> p (a t m j)"))
+        for t0, t1 in ((0, 4), (4, 6), (6, 7)):
+            quantize_w1(0, slice(P * t0, P * t1), w1_bf0[:, t0:t1].rearrange("p t m j -> p (t m j)"))
+        quantize_w1(0, slice(P * 7, P * 8), w1_last.rearrange("p t m j -> p (t m j)"))
         w1_bf11 = tile([P, PACK, P, PACK], BF16, "w1_bf11", "w1_bf0")
         for m0 in range(0, P, PART):
             round_on_gpsimd(w1_bf11, 1, 1, m0, m0 + PART)
-        right(1, 0, "tab0")
-        for t in range(1, PACK):
+        for t in range(PACK):
             right(1, t)
         w1_bf01 = tile([P, PACK, P, PACK], BF16, "w1_bf01", "w2_codes1")
         for m0, m1 in ((0, PART), (PART, SCALAR_SHARE)):
@@ -293,7 +300,7 @@ def tile_list_curriculum_merger_kernel(
         w1_operand(1)
         quantize_w1(1, slice(PASS, 2 * PASS), w1_bf11.rearrange("p t m j -> p (t m j)"))
         quantize_w1(1, slice(0, PASS), w1_bf01.rearrange("p t m j -> p (t m j)"))
-        z_rows = tile([P, HALF + PACK * MERGED], F32, "z_rows", "both_rows")
+        z_rows = tile_at([P, HALF + PACK * MERGED], F32, "z_rows", TAB_SECOND_AT + RAW)
         z_first = z_rows[:, HALF:].rearrange("p (t c) -> p t c", t=PACK)
         z_late = z_rows[:, 0 : PACK * HALF].rearrange("p (t c) -> p t c", t=PACK)
         for t in range(PACK):
@@ -342,8 +349,13 @@ def tile_list_curriculum_merger_kernel(
             left(1, t)
             merge(z_early, 1, t, 0, HALF)
         merge(z_late, 1, 0, HALF, MERGED)
-        for h, slot in enumerate(("tab1", "w1_planes1")):
-            quantize_z(0, h, round_z(nc.scalar.copy, z_first[:, :, HALF * h : HALF * (h + 1)], f"z_bf0{h}", slot))
+        z_bf0 = tile([P, 2, HALF, PACK], BF16, "z_bf0", "w1_planes1")
+        for h in range(2):
+            nc.scalar.copy(
+                z_bf0[:, h].rearrange("p (g i) t -> p g t i", i=LINE // 4),
+                z_first[:, :, HALF * h : HALF * (h + 1)].rearrange("p t (g i) -> p g t i", i=LINE // 4),
+            )
+            quantize_z(0, h, z_bf0[:, h])
         second_stage(0, 0)
         second_stage(0, 1)
         quantize_z(1, 0, round_z(nc.scalar.copy, z_early, "z_bf10"))

@@ -31,18 +31,21 @@ QUADRANTS = 4
 DENSE = 32
 PER_COLUMN = 16
 LINE = 16
-HALF = MERGED // 2
-WINDOWS = 16
+SIDE = MERGED // 2
+WORDS_PIECE = BANK // 2
+WINDOWS = 2 * PASSES * PACK
 WARM_UPS = 4
 
 PART = P // 2
-SCALAR_SHARE = 80
+FIRST_RUNS = ((0, 4), (4, 6), (6, 7))
 SCALAR_LAST = 80
-STORES = ((2, 3, 0, TERMS), (3, 4, 0, TERMS // 2), (3, 4, TERMS // 2, TERMS))
+EARLY_ROWS = 2
+STORES = ((2, 0, TERMS), (3, 0, TERMS // 2), (3, TERMS // 2, TERMS))
+QUARTER = 4 * PACK * PASS
 W2_SECOND_AT, GATHERED_AT, W2_CODES_AT, W1_FIRST_AT = 0, 1536, 2048, 4096
-TAB_FIRST_AT, TAB_SECOND_AT = 12288, 20480
-RAW = 8192
 GATHERED_SLOT = 3072
+TAB_AT = (W1_FIRST_AT + QUARTER, W1_FIRST_AT + 2 * QUARTER)
+W1_AT = {(0, 0): W1_FIRST_AT, (1, 0): TAB_AT[0], (0, 1): TAB_AT[1], (1, 1): TAB_AT[1] + QUARTER}
 
 
 def tile_list_curriculum_merger_kernel(
@@ -81,24 +84,16 @@ def tile_list_curriculum_merger_kernel(
         tab, w2_raw, w1_raw = {}, {}, {}
 
         def load_tab(a):
-            tab[a] = tile_at([P, (a + 1) * T], I32, f"tab{a}", (TAB_FIRST_AT, TAB_SECOND_AT)[a])[:, 0:T]
+            tab[a] = tile_at([P, (a + 1) * T], I32, f"tab{a}", TAB_AT[a])[:, 0:T]
             nc.sync.dma_start(tab[a], tab_words[a].rearrange("p t i -> p (t i)").bitcast(I32))
 
-        def load_w2(b, raw):
-            w2_raw[b] = raw
-            nc.sync.dma_start(
-                raw.bitcast(I32),
-                w2_words[:, :, 2 * PASS * b : 2 * PASS * (b + 1)].rearrange("a p c -> p a c").bitcast(I32),
-            )
-
-        def load_w1(a, b, slot):
-            shape, name = [P, 2, PACK, PASS // 2], f"w1_raw{a}{b}"
-            raw = tile_at(shape, F32, name, slot)
+        def load_w1(a, b):
+            raw = tile_at([P, 2, PACK, PASS // 2], F32, f"w1_raw{a}{b}", W1_AT[a, b])
             w1_raw[a, b] = raw
-            for h in range(2):
-                cols = slice(PASS * b + PASS // 2 * h, PASS * b + PASS // 2 * (h + 1))
+            for part in range(2):
+                cols = slice(PASS * b + PASS // 2 * part, PASS * b + PASS // 2 * (part + 1))
                 nc.sync.dma_start(
-                    raw[:, h, :, :], w1[PASS * a : PASS * (a + 1), cols].rearrange("(p j) c -> p j c", j=PACK)
+                    raw[:, part, :, :], w1[PASS * a : PASS * (a + 1), cols].rearrange("(p j) c -> p j c", j=PACK)
                 )
 
         nc.sync.dma_start(tab_rows[0:DENSE, :].bitcast(I32), tab_scales.rearrange("a q t -> q a t").bitcast(I32))
@@ -127,33 +122,31 @@ def tile_list_curriculum_merger_kernel(
                 planes[32 * quad : 32 * quad + 4, :, :].bitcast(I32),
                 both_rows[8 * quad : 8 * quad + 8, :].bitcast(I32),
             )
-        load_w2(1, tile_at([P, PASSES, 2 * PASS], U8, "w2_raw1", W2_SECOND_AT))
-        load_w1(0, 0, W1_FIRST_AT)
+        w2_raw[1] = tile_at([P, PASSES, 2 * PASS], U8, "w2_raw1", W2_SECOND_AT)
+        nc.sync.dma_start(
+            w2_raw[1].bitcast(I32), w2_words[:, :, 2 * PASS : 4 * PASS].rearrange("a p c -> p a c").bitcast(I32)
+        )
+        load_w1(0, 0)
 
         v_words, w2_codes, w1_codes, w1_planes, picked, left_rows, z_mx, y_acc = {}, {}, {}, {}, {}, {}, {}, {}
 
-        def gather_words(a, h):
+        def gather_words(a, h, width=BANK):
             v_words[a, h] = tile([P, BANK], U32, f"v_words{a}{h}")
-            pieces = 2 if (a, h) == (1, 1) else 1
-            width = BANK // pieces
             for e0 in range(0, BANK, width):
                 cols = slice((BANK * h + e0) // PER_COLUMN, (BANK * h + e0 + width) // PER_COLUMN)
                 nc.vector.tensor_copy(v_words[a, h][:, e0 : e0 + width], tab[a].bitcast(U32).indirect(idx[:, cols]))
 
         def w1_views(dst, a, b, m0, m1, walk, t0=0, t1=PACK):
-            h = m0 // PART
-            src = w1_raw[a, b][:, h, :, :].rearrange("p j (m t) -> p t m j", t=PACK)
-            src = src[:, t0:t1, m0 - PART * h : m1 - PART * h, :]
+            part = m0 // PART
+            src = w1_raw[a, b][:, part, :, :].rearrange("p j (m t) -> p t m j", t=PACK)
+            src = src[:, t0:t1, m0 - PART * part : m1 - PART * part, :]
             return dst[:, :, m0:m1, :].rearrange("p t m j -> " + walk), src.rearrange("p t m j -> " + walk)
 
         def round_on_gpsimd(dst, a, b, m0, m1, t1=PACK):
             nc.gpsimd.tensor_scalar(*w1_views(dst, a, b, m0, m1, "p m t j", 0, t1), 1.0, 0.0, MULT, ADD)
 
-        def w1_operand(b):
-            if b == 0:
-                w1_codes[b] = tile_at([P, PASSES * PASS], U32, "w1_codes0", TAB_FIRST_AT)
-            else:
-                w1_codes[b] = tile_at([P, PASSES * PASS], U32, "w1_codes1", TAB_SECOND_AT)
+        def w1_operand(b, slot_of):
+            w1_codes[b] = tile_at([P, PASSES * PASS], U32, f"w1_codes{b}", W1_AT[slot_of])
             w1_planes[b] = tile([P, PASSES * PASS], U8, f"w1_planes{b}")
 
         def quantize_w1(b, cols, rounded):
@@ -190,7 +183,7 @@ def tile_list_curriculum_merger_kernel(
 
         def pick(b, t, window):
             if (b, t) == (1, 0):
-                picked[b, t] = tile_at([P, MERGED], F32, "picked10", TAB_FIRST_AT + 4 * PASSES * PASS)
+                picked[b, t] = tile_at([P, MERGED], F32, "picked10", W1_AT[1, 0] + QUARTER // 2)
             else:
                 picked[b, t] = tile([P, MERGED], F32, f"picked{b}{t}")
             nc.vector.tensor_copy(picked[b, t], window.indirect(p2[:]))
@@ -204,15 +197,15 @@ def tile_list_curriculum_merger_kernel(
             first_window = rows.tile([P, S], F32, name="window")[:]
             first_stage(*w2_operand(0, 0), first_window, [0])
             pieces = []
-            for piece in range(2):
-                acc = psum.tile([P, BANK], F32, name="acc", tag=f"bank{STAGE1_BANKS + 1 + piece}")
-                pieces.append((acc, BANK + HALF * piece, BANK + HALF * (piece + 1)))
-                multiply(acc, *w2_operand(0, 0), 0, pieces[piece][1], pieces[piece][2], P)
+            for e0 in range(BANK, S, WORDS_PIECE):
+                acc = psum.tile([P, BANK], F32, name="acc", tag=f"bank{STAGE1_BANKS + 1 + len(pieces)}")
+                pieces.append((acc, e0, e0 + WORDS_PIECE))
+                multiply(acc, *w2_operand(0, 0), 0, e0, e0 + WORDS_PIECE, P)
             opened = next_bank()
             multiply(opened, *w2_operand(0, 1), 0, 0, BANK, BANK)
             for acc, e0, e1 in pieces:
                 multiply(acc, *w2_operand(0, 0), 1, e0, e1, P)
-                nc.scalar.copy(first_window[:, e0:e1], acc[:, 0:HALF])
+                nc.scalar.copy(first_window[:, e0:e1], acc[:, 0:WORDS_PIECE])
             pick(0, 0, first_window)
             second_window = rows.tile([P, S], F32, name="window")[:]
             multiply(opened, *w2_operand(0, 1), 1, 0, BANK, BANK)
@@ -232,19 +225,17 @@ def tile_list_curriculum_merger_kernel(
             offsets = p1[:, c0 // PER_COLUMN : c1 // PER_COLUMN]
             nc.vector.tensor_tensor(dst[:, t, :], left_rows[b, t].indirect(offsets), picked[b, t][:, c0:c1], MULT)
 
-        def round_z(copy, src, name, slot=None):
-            rounded = tile([P, HALF, PACK], BF16, name, slot)
+        def round_z(copy, rounded, src):
             copy(
                 rounded.rearrange("p (g i) t -> p g t i", i=LINE // 4),
                 src.rearrange("p t (g i) -> p g t i", i=LINE // 4),
             )
-            return rounded
 
-        def quantize_z(b, h, rounded):
-            if h == 0:
+        def quantize_z(b, side, rounded):
+            if side == 0:
                 z_mx[b] = (tile([P, MERGED], U32, f"z_codes{b}"), tile([P, MERGED], U8, f"z_plane{b}"))
             codes, plane = z_mx[b]
-            cols = slice(HALF * h, HALF * (h + 1))
+            cols = slice(SIDE * side, SIDE * (side + 1))
             nc.vector.quantize_mx(
                 out=codes[:, cols].bitcast(E4M3), scales=plane[:, cols], in_=rounded.rearrange("p c t -> p (c t)")
             )
@@ -263,11 +254,11 @@ def tile_list_curriculum_merger_kernel(
                 w2_raw[0][:, a, :].bitcast(U16).rearrange("p (g i t) -> p g t i", t=PACK, i=LINE // 2),
             )
         gather_words(0, 1)
-        load_w1(1, 0, TAB_FIRST_AT)
+        load_w1(1, 0)
         gather_words(1, 0)
-        gather_words(1, 1)
-        load_w1(1, 1, TAB_SECOND_AT + RAW)
-        load_w1(0, 1, TAB_SECOND_AT)
+        gather_words(1, 1, WORDS_PIECE)
+        load_w1(1, 1)
+        load_w1(0, 1)
         w2_codes[1] = tile([P, PASSES, 2 * PASS], U8, "w2_codes1")
         nc.vector.tensor_copy(
             w2_codes[1].bitcast(U16).rearrange("p a (t g i) -> p a g t i", t=PACK, i=LINE // 2),
@@ -284,25 +275,24 @@ def tile_list_curriculum_merger_kernel(
         for m0 in range(0, P, PART):
             round_on_gpsimd(w1_bf0[:, PACK:], 1, 0, m0, m0 + PART, PACK - 1)
             nc.scalar.activation(*w1_views(w1_last, 1, 0, m0, m0 + PART, "p t m j", PACK - 1, PACK), COPY)
-        w1_operand(0)
-        for t0, t1 in ((0, 4), (4, 6), (6, 7)):
+        w1_operand(0, (1, 0))
+        for t0, t1 in FIRST_RUNS:
             quantize_w1(0, slice(P * t0, P * t1), w1_bf0[:, t0:t1].rearrange("p t m j -> p (t m j)"))
-        quantize_w1(0, slice(P * 7, P * 8), w1_last.rearrange("p t m j -> p (t m j)"))
+        quantize_w1(0, slice(PASSES * PASS - P, PASSES * PASS), w1_last.rearrange("p t m j -> p (t m j)"))
         w1_bf11 = tile([P, PACK, P, PACK], BF16, "w1_bf11", "w1_bf0")
         for m0 in range(0, P, PART):
             round_on_gpsimd(w1_bf11, 1, 1, m0, m0 + PART)
         for t in range(PACK):
             right(1, t)
         w1_bf01 = tile([P, PACK, P, PACK], BF16, "w1_bf01", "w2_codes1")
-        for m0, m1 in ((0, PART), (PART, SCALAR_SHARE)):
-            nc.scalar.activation(*w1_views(w1_bf01, 0, 1, m0, m1, "p m j t"), COPY)
-        round_on_gpsimd(w1_bf01, 0, 1, SCALAR_SHARE, P)
-        w1_operand(1)
+        nc.scalar.activation(*w1_views(w1_bf01, 0, 1, 0, PART, "p m j t"), COPY)
+        round_on_gpsimd(w1_bf01, 0, 1, PART, P)
+        w1_operand(1, (0, 1))
         quantize_w1(1, slice(PASS, 2 * PASS), w1_bf11.rearrange("p t m j -> p (t m j)"))
         quantize_w1(1, slice(0, PASS), w1_bf01.rearrange("p t m j -> p (t m j)"))
-        z_rows = tile_at([P, HALF + PACK * MERGED], F32, "z_rows", TAB_SECOND_AT + RAW)
-        z_first = z_rows[:, HALF:].rearrange("p (t c) -> p t c", t=PACK)
-        z_late = z_rows[:, 0 : PACK * HALF].rearrange("p (t c) -> p t c", t=PACK)
+        z_rows = tile_at([P, SIDE + PACK * MERGED], F32, "z_rows", W1_AT[1, 1])
+        z_first = z_rows[:, SIDE:].rearrange("p (t c) -> p t c", t=PACK)
+        z_late = z_rows[:, 0 : PACK * SIDE].rearrange("p (t c) -> p t c", t=PACK)
         for t in range(PACK):
             left(0, t)
             merge(z_first, 0, t, 0, MERGED)
@@ -322,52 +312,48 @@ def tile_list_curriculum_merger_kernel(
 
         y = [tile([P, MERGED], F32, f"y{n}") for n in range(N // P)]
 
-        def second_stage(b, h):
+        def second_stage(b, side):
             codes, plane = z_mx[b]
             for n in range(N // P):
-                split = n < 2
-                cols = slice(HALF * h, HALF * (h + 1))
+                split = n < EARLY_ROWS
+                cols = slice(SIDE * side, SIDE * (side + 1))
                 if b == PASSES - 1 and not split:
-                    if h == 0:
+                    if side == 0:
                         continue
                     cols = slice(0, MERGED)
-                if b == 0 and (split or h == 0):
-                    y_acc[n, h] = psum.tile([P, BANK], F32, name="acc", tag=f"bank{N // P * (1 - h) + n}")[:]
-                acc = y_acc[n, h if split else 0]
+                if b == 0 and (split or side == 0):
+                    y_acc[n, side] = psum.tile([P, BANK], F32, name="acc", tag=f"bank{N // P * (1 - side) + n}")[:]
+                acc = y_acc[n, side if split else 0]
                 nc.tensor.matmul_mx(
                     out=acc[:, cols],
                     lhsT=w3_codes[:, b, PACK * P * n : PACK * P * (n + 1)].bitcast(E4M3),
                     lhsT_scale=w3_planes[:, b, P * n : P * (n + 1)],
                     rhs=codes[:, cols].bitcast(E4M3), rhs_scale=plane[:, cols],
-                    start=(b == 0 and (split or h == 0)), stop=(b == PASSES - 1 and (split or h == 1)),
+                    start=(b == 0 and (split or side == 0)), stop=(b == PASSES - 1 and (split or side == 1)),
                 )
-                if b == PASSES - 1 and (split or h == 1):
+                if b == PASSES - 1 and (split or side == 1):
                     nc.scalar.activation(y[n][:, cols], acc[:, cols], IDENTITY, bias=bias_cols[:, n : n + 1])
 
-        z_early = tile([P, PACK, HALF], F32, "z_early")
+        z_early = tile([P, PACK, SIDE], F32, "z_early")
         for t in range(PACK):
             left(1, t)
-            merge(z_early, 1, t, 0, HALF)
-        merge(z_late, 1, 0, HALF, MERGED)
-        z_bf0 = tile([P, 2, HALF, PACK], BF16, "z_bf0", "w1_planes1")
-        for h in range(2):
-            nc.scalar.copy(
-                z_bf0[:, h].rearrange("p (g i) t -> p g t i", i=LINE // 4),
-                z_first[:, :, HALF * h : HALF * (h + 1)].rearrange("p t (g i) -> p g t i", i=LINE // 4),
-            )
-            quantize_z(0, h, z_bf0[:, h])
+            merge(z_early, 1, t, 0, SIDE)
+        merge(z_late, 1, 0, SIDE, MERGED)
+        z_bf0 = tile([P, 2, SIDE, PACK], BF16, "z_bf0", "w1_planes1")
+        for side in range(2):
+            round_z(nc.scalar.copy, z_bf0[:, side], z_first[:, :, SIDE * side : SIDE * (side + 1)])
+            quantize_z(0, side, z_bf0[:, side])
         second_stage(0, 0)
         second_stage(0, 1)
-        quantize_z(1, 0, round_z(nc.scalar.copy, z_early, "z_bf10"))
+        z_bf10 = tile([P, SIDE, PACK], BF16, "z_bf10")
+        round_z(nc.scalar.copy, z_bf10, z_early)
+        quantize_z(1, 0, z_bf10)
         second_stage(1, 0)
         for t in range(1, PACK):
-            merge(z_late, 1, t, HALF, MERGED)
-        z_bf11 = tile([P, HALF, PACK], BF16, "z_bf11", "z_early")
-        for copy, c0, c1 in ((nc.scalar.copy, 0, SCALAR_LAST), (nc.vector.tensor_copy, SCALAR_LAST, HALF)):
-            copy(
-                z_bf11[:, c0:c1, :].rearrange("p (g i) t -> p g t i", i=LINE // 4),
-                z_late[:, :, c0:c1].rearrange("p t (g i) -> p g t i", i=LINE // 4),
-            )
+            merge(z_late, 1, t, SIDE, MERGED)
+        z_bf11 = tile([P, SIDE, PACK], BF16, "z_bf11", "z_early")
+        for copy, c0, c1 in ((nc.scalar.copy, 0, SCALAR_LAST), (nc.vector.tensor_copy, SCALAR_LAST, SIDE)):
+            round_z(copy, z_bf11[:, c0:c1, :], z_late[:, :, c0:c1])
         quantize_z(1, 1, z_bf11)
         second_stage(1, 1)
 
@@ -375,18 +361,17 @@ def tile_list_curriculum_merger_kernel(
         second = tile([P, N // P, TERMS], F32, "second")
         term = tile([P, N // P, TERMS], F32, "term")
         out_rows = out.rearrange("(n p) t -> p n t", p=P)
-        for n in range(2):
+        for n in range(EARLY_ROWS):
             nc.vector.tensor_copy(second[:, n, :], y[n].indirect(p4[:]))
-        above = tile([P, 2, TERMS], F32, "above")
-        for n in range(2):
+        above = tile([P, EARLY_ROWS, TERMS], F32, "above")
+        for n in range(EARLY_ROWS):
             nc.vector.tensor_tensor(first[:, n, :], y[n].indirect(p3[:]), second[:, n, :], SUBTRACT)
             nc.scalar.activation(above[:, n, :], first[:, n, :], RELU)
             nc.gpsimd.tensor_tensor(term[:, n, :], above[:, n, :], second[:, n, :], ADD)
             nc.scalar.dma_start(out_rows[:, n, :], term[:, n, :])
-        for n0, n1, c0, c1 in STORES:
-            for n in range(n0, n1):
-                if c0 == 0:
-                    nc.vector.tensor_copy(first[:, n, :], y[n].indirect(p3[:]))
-                nc.vector.tensor_copy(second[:, n, c0:c1], y[n].indirect(p4[:, c0 // PER_COLUMN : c1 // PER_COLUMN]))
-            nc.vector.tensor_tensor(term[:, n0:n1, c0:c1], first[:, n0:n1, c0:c1], second[:, n0:n1, c0:c1], MAX)
-            nc.sync.dma_start(out_rows[:, n0:n1, c0:c1], term[:, n0:n1, c0:c1])
+        for n, c0, c1 in STORES:
+            if c0 == 0:
+                nc.vector.tensor_copy(first[:, n, :], y[n].indirect(p3[:]))
+            nc.vector.tensor_copy(second[:, n, c0:c1], y[n].indirect(p4[:, c0 // PER_COLUMN : c1 // PER_COLUMN]))
+            nc.vector.tensor_tensor(term[:, n, c0:c1], first[:, n, c0:c1], second[:, n, c0:c1], MAX)
+            nc.sync.dma_start(out_rows[:, n, c0:c1], term[:, n, c0:c1])

@@ -73,13 +73,14 @@ def tile_list_curriculum_merger_kernel(
 
         w2_rows = tile([P, H], U8, "w2_rows")
         tab_rows = tile([P, T], U8, "tab_rows")
-        planes = tile([P, PASSES, S + H], U8, "planes")
+        planes = tile([P, PASSES, S + PASS], U8, "planes")
         for dense in (tab_rows, w2_rows):
             nc.gpsimd.memset(dense[32:64, :].bitcast(I32), 0)
             nc.gpsimd.memset(dense[64:128, :].bitcast(I32), 0)
         nc.vector.memset(planes.rearrange("p a c -> p (a c)").bitcast(I32), 0)
         v_planes = planes[:, :, 0:S]
-        w2_planes = planes[:, :, S : S + H]
+        w2_planes = {0: planes[:, :, S : S + PASS], 1: tile([P, PASSES, PASS], U8, "late_planes")}
+        nc.vector.memset(w2_planes[1].rearrange("p a c -> p (a c)").bitcast(I32), 0)
 
         tab, w2_raw, w1_raw = {}, {}, {}
 
@@ -111,17 +112,24 @@ def tile_list_curriculum_merger_kernel(
 
         v_rows = tile_at([P, GATHERED_SLOT], U8, "v_rows", GATHERED_AT)[:, 0:S]
         nc.vector.tensor_copy(v_rows, tab_rows.indirect(idx[:]))
-        both_rows = tile([P, S + H], U8, "both_rows")
-        nc.gpsimd.tensor_copy(
-            both_rows[:, S : S + H].rearrange("p (b t g i) -> p b g t i", b=PASSES, t=PACK, i=LINE),
-            w2_rows.rearrange("p (b g i t) -> p b g t i", b=PASSES, t=PACK, i=LINE),
-        )
-        nc.vector.tensor_copy(both_rows[:, 0:S].bitcast(I32), v_rows.bitcast(I32))
-        for quad in range(QUADRANTS):
-            nc.sync.dma_start(
-                planes[32 * quad : 32 * quad + 4, :, :].bitcast(I32),
-                both_rows[8 * quad : 8 * quad + 8, :].bitcast(I32),
+        both_rows = tile([P, S + PASS], U8, "both_rows")
+
+        def reorder_scales(b, dst):
+            nc.gpsimd.tensor_copy(
+                dst.rearrange("p (t g i) -> p g t i", t=PACK, i=LINE),
+                w2_rows[:, PASS * b : PASS * (b + 1)].rearrange("p (g i t) -> p g t i", t=PACK, i=LINE),
             )
+
+        reorder_scales(0, both_rows[:, S:])
+        nc.vector.tensor_copy(both_rows[:, 0:S].bitcast(I32), v_rows.bitcast(I32))
+
+        def spread(dst, dense):
+            for quad in (0, 2, 1, 3):
+                nc.sync.dma_start(
+                    dst[32 * quad : 32 * quad + 4, :, :].bitcast(I32), dense[8 * quad : 8 * quad + 8, :].bitcast(I32)
+                )
+
+        spread(planes, both_rows)
         w2_raw[1] = tile_at([P, PASSES, 2 * PASS], U8, "w2_raw1", W2_SECOND_AT)
         nc.sync.dma_start(
             w2_raw[1].bitcast(I32), w2_words[:, :, 2 * PASS : 4 * PASS].rearrange("a p c -> p a c").bitcast(I32)
@@ -178,7 +186,7 @@ def tile_list_curriculum_merger_kernel(
         def w2_operand(b, t):
             return (
                 lambda a: w2_codes[b][:, a, 2 * P * t : 2 * P * (t + 1)].bitcast(E2M1),
-                lambda a: w2_planes[:, a, PASS * b + P * t : PASS * b + P * (t + 1)],
+                lambda a: w2_planes[b][:, a, P * t : P * (t + 1)],
             )
 
         def pick(b, t, window):
@@ -253,10 +261,13 @@ def tile_list_curriculum_merger_kernel(
                 w2_codes[0][:, a, :].bitcast(U16).rearrange("p (t g i) -> p g t i", t=PACK, i=LINE // 2),
                 w2_raw[0][:, a, :].bitcast(U16).rearrange("p (g i t) -> p g t i", t=PACK, i=LINE // 2),
             )
+        late_rows = tile([P, PASS], U8, "late_rows", "w2_raw0")
+        reorder_scales(1, late_rows)
         gather_words(0, 1)
         load_w1(1, 0)
         gather_words(1, 0)
         gather_words(1, 1, WORDS_PIECE)
+        spread(w2_planes[1], late_rows)
         load_w1(1, 1)
         load_w1(0, 1)
         w2_codes[1] = tile([P, PASSES, 2 * PASS], U8, "w2_codes1")

@@ -114,13 +114,13 @@ def tile_list_curriculum_merger_kernel(
         nc.vector.tensor_copy(v_rows, tab_rows.indirect(idx[:]))
         both_rows = tile([P, S + PASS], U8, "both_rows")
 
-        def reorder_scales(b, dst):
-            nc.gpsimd.tensor_copy(
+        def reorder_scales(engine, b, dst):
+            engine.tensor_copy(
                 dst.rearrange("p (t g i) -> p g t i", t=PACK, i=LINE),
                 w2_rows[:, PASS * b : PASS * (b + 1)].rearrange("p (g i t) -> p g t i", t=PACK, i=LINE),
             )
 
-        reorder_scales(0, both_rows[:, S:])
+        reorder_scales(nc.gpsimd, 0, both_rows[:, S:])
         nc.vector.tensor_copy(both_rows[:, 0:S].bitcast(I32), v_rows.bitcast(I32))
 
         def spread(dst, dense):
@@ -256,17 +256,17 @@ def tile_list_curriculum_merger_kernel(
                 rhs=v_words[0, 0].bitcast(E4M3), rhs_scale=both_rows[:, 0:BANK], start=True, stop=True,
             )
         w2_codes[0] = tile_at([P, PASSES, 2 * PASS], U8, "w2_codes0", W2_CODES_AT)
-        for a in range(PASSES):
+        for a, t0, t1 in ((0, 0, PACK), (1, 0, 1), (1, 1, PACK)):
             nc.gpsimd.tensor_copy(
-                w2_codes[0][:, a, :].bitcast(U16).rearrange("p (t g i) -> p g t i", t=PACK, i=LINE // 2),
-                w2_raw[0][:, a, :].bitcast(U16).rearrange("p (g i t) -> p g t i", t=PACK, i=LINE // 2),
+                w2_codes[0][:, a, :].bitcast(U16).rearrange("p (t g i) -> p g t i", t=PACK, i=LINE // 2)[:, :, t0:t1],
+                w2_raw[0][:, a, :].bitcast(U16).rearrange("p (g i t) -> p g t i", t=PACK, i=LINE // 2)[:, :, t0:t1],
             )
-        late_rows = tile([P, PASS], U8, "late_rows", "w2_raw0")
-        reorder_scales(1, late_rows)
         gather_words(0, 1)
         load_w1(1, 0)
         gather_words(1, 0)
         gather_words(1, 1, WORDS_PIECE)
+        late_rows = tile([P, PASS], U8, "late_rows", "w2_raw0")
+        reorder_scales(nc.vector, 1, late_rows)
         spread(w2_planes[1], late_rows)
         load_w1(1, 1)
         load_w1(0, 1)

@@ -151,7 +151,7 @@ def tile_list_curriculum_merger_kernel(
             return dst[:, :, m0:m1, :].rearrange("p t m j -> " + walk), src.rearrange("p t m j -> " + walk)
 
         def round_on_gpsimd(dst, a, b, m0, m1, t1=PACK):
-            nc.gpsimd.tensor_scalar(*w1_views(dst, a, b, m0, m1, "p m t j", 0, t1), 1.0, 0.0, MULT, ADD)
+            nc.gpsimd.tensor_scalar(*w1_views(dst, a, b, m0, m1, "p m j t", 0, t1), 1.0, 0.0, MULT, ADD)
 
         def w1_operand(b, slot_of):
             w1_codes[b] = tile_at([P, PASSES * PASS], U32, f"w1_codes{b}", W1_AT[slot_of])

@@ -32,20 +32,28 @@ DENSE = 32
 PER_COLUMN = 16
 LINE = 16
 SIDE = MERGED // 2
+PIECE = SIDE // 2
+RANGES = ((0, SIDE), (SIDE, SIDE + PIECE), (SIDE + PIECE, MERGED))
 WORDS_PIECE = BANK // 2
-WINDOWS = 2 * PASSES * PACK
+WINDOWS = 3 * PACK
 WARM_UPS = 4
 
 PART = P // 2
-FIRST_RUNS = ((0, 4), (4, 6), (6, 7))
-SCALAR_LAST = 80
+SCALAR_FROM, SCALAR_TO, LAST_FROM = 96, 64, 80
 EARLY_ROWS = 2
 STORES = ((2, 0, TERMS), (3, 0, TERMS // 2), (3, TERMS // 2, TERMS))
 QUARTER = 4 * PACK * PASS
-W2_SECOND_AT, GATHERED_AT, W2_CODES_AT, W1_FIRST_AT = 0, 1536, 2048, 4096
-GATHERED_SLOT = 3072
-TAB_AT = (W1_FIRST_AT + QUARTER, W1_FIRST_AT + 2 * QUARTER)
-W1_AT = {(0, 0): W1_FIRST_AT, (1, 0): TAB_AT[0], (0, 1): TAB_AT[1], (1, 1): TAB_AT[1] + QUARTER}
+W2_SECOND_AT, GATHERED_AT, W2_CODES_AT, LATE_ROWS_AT, W1_FIRST_AT = 0, 1536, 2048, 4096, 4608
+GATHERED_SLOT = 3584
+COLUMN = QUARTER // P
+W1_SECOND_AT = W1_FIRST_AT + 2 * QUARTER
+SHARE_AT = W1_SECOND_AT + COLUMN * SCALAR_FROM
+W2_ROWS_AT = W1_SECOND_AT + COLUMN * PART - H // 2
+W2_ROWS_SLOT = SHARE_AT + H // 2 - W2_ROWS_AT
+LATE_WINDOWS_AT = SHARE_AT + COLUMN * (P - SCALAR_FROM) // 2
+LATE_PICKS_AT = LATE_WINDOWS_AT - 4 * PACK * MERGED
+TAB_AT = (W1_FIRST_AT + QUARTER, LATE_WINDOWS_AT + 4 * PACK * S)
+W1_AT = {(0, 0): W1_FIRST_AT, (1, 0): W1_SECOND_AT, (0, 1): TAB_AT[1], (1, 1): TAB_AT[1] + QUARTER}
 
 
 def tile_list_curriculum_merger_kernel(
@@ -71,7 +79,7 @@ def tile_list_curriculum_merger_kernel(
             nc.sync.dma_start(offsets[:], src)
             return offsets
 
-        w2_rows = tile([P, H], U8, "w2_rows")
+        w2_rows = tile_at([P, W2_ROWS_SLOT], U8, "w2_rows", W2_ROWS_AT)[:, 0:H]
         tab_rows = tile([P, T], U8, "tab_rows")
         planes = tile([P, PASSES, S + PASS], U8, "planes")
         for dense in (tab_rows, w2_rows):
@@ -88,13 +96,17 @@ def tile_list_curriculum_merger_kernel(
             tab[a] = tile_at([P, (a + 1) * T], I32, f"tab{a}", TAB_AT[a])[:, 0:T]
             nc.sync.dma_start(tab[a], tab_words[a].rearrange("p t i -> p (t i)").bitcast(I32))
 
-        def load_w1(a, b):
-            raw = tile_at([P, 2, PACK, PASS // 2], F32, f"w1_raw{a}{b}", W1_AT[a, b])
-            w1_raw[a, b] = raw
-            for part in range(2):
-                cols = slice(PASS * b + PASS // 2 * part, PASS * b + PASS // 2 * (part + 1))
+        def load_w1(a, b, cuts=(0, PART, P)):
+            start = cuts[0]
+            raw = tile_at(
+                [P, PACK * PACK * (cuts[-1] - start)], F32, f"w1_raw{a}{b}_{start}", W1_AT[a, b] + COLUMN * start
+            )
+            for m0, m1 in zip(cuts, cuts[1:]):
+                piece = raw[:, PACK * PACK * (m0 - start) : PACK * PACK * (m1 - start)]
+                w1_raw[a, b, m0] = piece.rearrange("p (j c) -> p j c", j=PACK)
+                cols = slice(PASS * b + PACK * m0, PASS * b + PACK * m1)
                 nc.sync.dma_start(
-                    raw[:, part, :, :], w1[PASS * a : PASS * (a + 1), cols].rearrange("(p j) c -> p j c", j=PACK)
+                    w1_raw[a, b, m0], w1[PASS * a : PASS * (a + 1), cols].rearrange("(p j) c -> p j c", j=PACK)
                 )
 
         nc.sync.dma_start(tab_rows[0:DENSE, :].bitcast(I32), tab_scales.rearrange("a q t -> q a t").bitcast(I32))
@@ -136,7 +148,7 @@ def tile_list_curriculum_merger_kernel(
         )
         load_w1(0, 0)
 
-        v_words, w2_codes, w1_codes, w1_planes, picked, left_rows, z_mx, y_acc = {}, {}, {}, {}, {}, {}, {}, {}
+        v_words, w2_codes, w1_codes, w1_planes, picked, left_rows = {}, {}, {}, {}, {}, {}
 
         def gather_words(a, h, width=BANK):
             v_words[a, h] = tile([P, BANK], U32, f"v_words{a}{h}")
@@ -144,17 +156,19 @@ def tile_list_curriculum_merger_kernel(
                 cols = slice((BANK * h + e0) // PER_COLUMN, (BANK * h + e0 + width) // PER_COLUMN)
                 nc.vector.tensor_copy(v_words[a, h][:, e0 : e0 + width], tab[a].bitcast(U32).indirect(idx[:, cols]))
 
-        def w1_views(dst, a, b, m0, m1, walk, t0=0, t1=PACK):
-            part = m0 // PART
-            src = w1_raw[a, b][:, part, :, :].rearrange("p j (m t) -> p t m j", t=PACK)
-            src = src[:, t0:t1, m0 - PART * part : m1 - PART * part, :]
-            return dst[:, :, m0:m1, :].rearrange("p t m j -> " + walk), src.rearrange("p t m j -> " + walk)
+        def w1_views(dst, a, b, m0, m1, walk="p m j t"):
+            first = max(m for a1, b1, m in w1_raw if (a1, b1) == (a, b) and m <= m0)
+            src = w1_raw[a, b, first].rearrange("p j (m t) -> " + walk, t=PACK)
+            return dst[:, :, m0:m1, :].rearrange("p t m j -> " + walk), src[:, m0 - first : m1 - first]
 
-        def round_on_gpsimd(dst, a, b, m0, m1, t1=PACK):
-            nc.gpsimd.tensor_scalar(*w1_views(dst, a, b, m0, m1, "p m j t", 0, t1), 1.0, 0.0, MULT, ADD)
+        def round_on_gpsimd(dst, a, b, m0, m1):
+            nc.gpsimd.tensor_scalar(*w1_views(dst, a, b, m0, m1), 1.0, 0.0, MULT, ADD)
 
         def w1_operand(b, slot_of):
-            w1_codes[b] = tile_at([P, PASSES * PASS], U32, f"w1_codes{b}", W1_AT[slot_of])
+            if slot_of is None:
+                w1_codes[b] = tile([P, PASSES * PASS], U32, f"w1_codes{b}")
+            else:
+                w1_codes[b] = tile_at([P, PASSES * PASS], U32, f"w1_codes{b}", W1_AT[slot_of])
             w1_planes[b] = tile([P, PASSES * PASS], U8, f"w1_planes{b}")
 
         def quantize_w1(b, cols, rounded):
@@ -190,9 +204,7 @@ def tile_list_curriculum_merger_kernel(
             )
 
         def pick(b, t, window):
-            if (b, t) == (1, 0):
-                picked[b, t] = tile_at([P, MERGED], F32, "picked10", W1_AT[1, 0] + QUARTER // 2)
-            else:
+            if (b, t) not in picked:
                 picked[b, t] = tile([P, MERGED], F32, f"picked{b}{t}")
             nc.vector.tensor_copy(picked[b, t], window.indirect(p2[:]))
 
@@ -239,15 +251,6 @@ def tile_list_curriculum_merger_kernel(
                 src.rearrange("p t (g i) -> p g t i", i=LINE // 4),
             )
 
-        def quantize_z(b, side, rounded):
-            if side == 0:
-                z_mx[b] = (tile([P, MERGED], U32, f"z_codes{b}"), tile([P, MERGED], U8, f"z_plane{b}"))
-            codes, plane = z_mx[b]
-            cols = slice(SIDE * side, SIDE * (side + 1))
-            nc.vector.quantize_mx(
-                out=codes[:, cols].bitcast(E4M3), scales=plane[:, cols], in_=rounded.rearrange("p c t -> p (c t)")
-            )
-
         gather_words(0, 0)
         warm = psum.tile([P, BANK], F32, name="acc", tag=f"bank{STAGE1_BANKS}")
         for warm_up in range(WARM_UPS):
@@ -256,54 +259,60 @@ def tile_list_curriculum_merger_kernel(
                 rhs=v_words[0, 0].bitcast(E4M3), rhs_scale=both_rows[:, 0:BANK], start=True, stop=True,
             )
         w2_codes[0] = tile_at([P, PASSES, 2 * PASS], U8, "w2_codes0", W2_CODES_AT)
-        for a, t0, t1 in ((0, 0, PACK), (1, 0, 1), (1, 1, PACK)):
-            nc.gpsimd.tensor_copy(
-                w2_codes[0][:, a, :].bitcast(U16).rearrange("p (t g i) -> p g t i", t=PACK, i=LINE // 2)[:, :, t0:t1],
-                w2_raw[0][:, a, :].bitcast(U16).rearrange("p (g i t) -> p g t i", t=PACK, i=LINE // 2)[:, :, t0:t1],
+        for a in range(PASSES):
+            nc.scalar.copy(
+                w2_codes[0][:, a, :].bitcast(U16).rearrange("p (t m) -> p m t", t=PACK),
+                w2_raw[0][:, a, :].bitcast(U16).rearrange("p (m t) -> p m t", t=PACK),
             )
+        late_rows = tile_at([P, PASS], U8, "late_rows", LATE_ROWS_AT)
+        reorder_scales(nc.gpsimd, 1, late_rows)
+        spread(w2_planes[1], late_rows)
+        load_w1(1, 0, (0, PART))
+        load_w1(1, 0, (SCALAR_FROM, P))
+        load_w1(1, 0, (PART, SCALAR_FROM))
         gather_words(0, 1)
-        load_w1(1, 0)
         gather_words(1, 0)
         gather_words(1, 1, WORDS_PIECE)
-        late_rows = tile([P, PASS], U8, "late_rows", "w2_raw0")
-        reorder_scales(nc.vector, 1, late_rows)
-        spread(w2_planes[1], late_rows)
-        load_w1(1, 1)
-        load_w1(0, 1)
+        load_w1(1, 1, (0, P))
+        load_w1(0, 1, (0, LAST_FROM, P))
         w2_codes[1] = tile([P, PASSES, 2 * PASS], U8, "w2_codes1")
         nc.vector.tensor_copy(
             w2_codes[1].bitcast(U16).rearrange("p a (t g i) -> p a g t i", t=PACK, i=LINE // 2),
             w2_raw[1].bitcast(U16).rearrange("p a (g i t) -> p a g t i", t=PACK, i=LINE // 2),
         )
 
-        w1_bf0 = tile([P, PASSES * PACK - 1, P, PACK], BF16, "w1_bf0")
-        nc.vector.tensor_copy(*w1_views(w1_bf0[:, 0:PACK], 0, 0, 0, PART, "p m j t"))
+        w1_bf0 = tile([P, PASSES * PACK, P, PACK], BF16, "w1_bf0")
+        nc.vector.tensor_copy(*w1_views(w1_bf0[:, 0:PACK], 0, 0, 0, PART))
         round_on_gpsimd(w1_bf0[:, 0:PACK], 0, 0, PART, P)
         first_two_of_right()
         for t in range(2, PACK):
             right(0, t)
-        w1_last = tile_at([P, 1, P, PACK], BF16, "w1_last", W2_CODES_AT)
-        for m0 in range(0, P, PART):
-            round_on_gpsimd(w1_bf0[:, PACK:], 1, 0, m0, m0 + PART, PACK - 1)
-            nc.scalar.activation(*w1_views(w1_last, 1, 0, m0, m0 + PART, "p t m j", PACK - 1, PACK), COPY)
-        w1_operand(0, (1, 0))
-        for t0, t1 in FIRST_RUNS:
-            quantize_w1(0, slice(P * t0, P * t1), w1_bf0[:, t0:t1].rearrange("p t m j -> p (t m j)"))
-        quantize_w1(0, slice(PASSES * PASS - P, PASSES * PASS), w1_last.rearrange("p t m j -> p (t m j)"))
+        round_on_gpsimd(w1_bf0[:, PACK:], 1, 0, 0, PART)
+        round_on_gpsimd(w1_bf0[:, PACK:], 1, 0, PART, SCALAR_FROM)
+        nc.scalar.activation(*w1_views(w1_bf0[:, PACK:], 1, 0, SCALAR_FROM, P), COPY)
+        w1_operand(0, None)
+        quantize_w1(0, slice(0, PASSES * PASS), w1_bf0.rearrange("p t m j -> p (t m j)"))
         w1_bf11 = tile([P, PACK, P, PACK], BF16, "w1_bf11", "w1_bf0")
-        for m0 in range(0, P, PART):
-            round_on_gpsimd(w1_bf11, 1, 1, m0, m0 + PART)
+        round_on_gpsimd(w1_bf11, 1, 1, 0, P)
+        late_picks = tile_at([P, PACK, MERGED], F32, "late_picks", LATE_PICKS_AT)
+        late_windows = tile_at([P, PACK * S], F32, "late_windows", LATE_WINDOWS_AT)
         for t in range(PACK):
-            right(1, t)
+            picked[1, t] = late_picks[:, t, :]
+            window = late_windows[:, S * t : S * (t + 1)]
+            first_stage(*w2_operand(1, t), window, range(S // BANK))
+            pick(1, t, window)
         w1_bf01 = tile([P, PACK, P, PACK], BF16, "w1_bf01", "w2_codes1")
-        nc.scalar.activation(*w1_views(w1_bf01, 0, 1, 0, PART, "p m j t"), COPY)
-        round_on_gpsimd(w1_bf01, 0, 1, PART, P)
+        nc.scalar.activation(*w1_views(w1_bf01, 0, 1, 0, SCALAR_TO), COPY)
+        round_on_gpsimd(w1_bf01, 0, 1, SCALAR_TO, LAST_FROM)
+        round_on_gpsimd(w1_bf01, 0, 1, LAST_FROM, P)
         w1_operand(1, (0, 1))
         quantize_w1(1, slice(PASS, 2 * PASS), w1_bf11.rearrange("p t m j -> p (t m j)"))
         quantize_w1(1, slice(0, PASS), w1_bf01.rearrange("p t m j -> p (t m j)"))
         z_rows = tile_at([P, SIDE + PACK * MERGED], F32, "z_rows", W1_AT[1, 1])
         z_first = z_rows[:, SIDE:].rearrange("p (t c) -> p t c", t=PACK)
-        z_late = z_rows[:, 0 : PACK * SIDE].rearrange("p (t c) -> p t c", t=PACK)
+        z_pieces = [
+            z_rows[:, PACK * PIECE * i : PACK * PIECE * (i + 1)].rearrange("p (t c) -> p t c", t=PACK) for i in range(2)
+        ]
         for t in range(PACK):
             left(0, t)
             merge(z_first, 0, t, 0, MERGED)
@@ -322,51 +331,66 @@ def tile_list_curriculum_merger_kernel(
             nc.sync.dma_start(bias_cols, bias.rearrange("(n p) -> p n", p=P))
 
         y = [tile([P, MERGED], F32, f"y{n}") for n in range(N // P)]
+        z_codes = [tile([P, MERGED], U32, f"z_codes{b}") for b in range(PASSES)]
+        z_planes = [tile([P, MERGED], U8, f"z_planes{b}") for b in range(PASSES)]
 
-        def second_stage(b, side):
-            codes, plane = z_mx[b]
-            for n in range(N // P):
-                split = n < EARLY_ROWS
-                cols = slice(SIDE * side, SIDE * (side + 1))
-                if b == PASSES - 1 and not split:
-                    if side == 0:
-                        continue
-                    cols = slice(0, MERGED)
-                if b == 0 and (split or side == 0):
-                    y_acc[n, side] = psum.tile([P, BANK], F32, name="acc", tag=f"bank{N // P * (1 - side) + n}")[:]
-                acc = y_acc[n, side if split else 0]
-                nc.tensor.matmul_mx(
-                    out=acc[:, cols],
-                    lhsT=w3_codes[:, b, PACK * P * n : PACK * P * (n + 1)].bitcast(E4M3),
-                    lhsT_scale=w3_planes[:, b, P * n : P * (n + 1)],
-                    rhs=codes[:, cols].bitcast(E4M3), rhs_scale=plane[:, cols],
-                    start=(b == 0 and (split or side == 0)), stop=(b == PASSES - 1 and (split or side == 1)),
-                )
-                if b == PASSES - 1 and (split or side == 1):
-                    nc.scalar.activation(y[n][:, cols], acc[:, cols], IDENTITY, bias=bias_cols[:, n : n + 1])
+        def quantize_z(b, c0, c1, rounded):
+            nc.vector.quantize_mx(
+                out=z_codes[b][:, c0:c1].bitcast(E4M3), scales=z_planes[b][:, c0:c1],
+                in_=rounded.rearrange("p c t -> p (c t)"),
+            )
+
+        def second_pass(acc, n, b, c0, c1, start, stop):
+            nc.tensor.matmul_mx(
+                out=acc[:, c0:c1], lhsT=w3_codes[:, b, PACK * P * n : PACK * P * (n + 1)].bitcast(E4M3),
+                lhsT_scale=w3_planes[:, b, P * n : P * (n + 1)],
+                rhs=z_codes[b][:, c0:c1].bitcast(E4M3), rhs_scale=z_planes[b][:, c0:c1], start=start, stop=stop,
+            )
+
+        def finish(acc, n, c0, c1):
+            second_pass(acc, n, 1, c0, c1, False, True)
+            nc.scalar.activation(y[n][:, c0:c1], acc[:, c0:c1], IDENTITY, bias=bias_cols[:, n : n + 1])
+
+        def bank(index):
+            return psum.tile([P, BANK], F32, name="acc", tag=f"bank{index}")[:]
 
         z_early = tile([P, PACK, SIDE], F32, "z_early")
         for t in range(PACK):
             left(1, t)
             merge(z_early, 1, t, 0, SIDE)
-        merge(z_late, 1, 0, SIDE, MERGED)
         z_bf0 = tile([P, 2, SIDE, PACK], BF16, "z_bf0", "w1_planes1")
+        y_first = [bank(N // P + i) for i in range(len(RANGES))]
+        y_second = [bank(1), bank(2 * N // P - 1)]
+        y_rest = {n: bank(n) for n in range(2, N // P)}
+        for t in range(2):
+            merge(z_pieces[0], 1, t, *RANGES[1])
         for side in range(2):
-            round_z(nc.scalar.copy, z_bf0[:, side], z_first[:, :, SIDE * side : SIDE * (side + 1)])
-            quantize_z(0, side, z_bf0[:, side])
-        second_stage(0, 0)
-        second_stage(0, 1)
+            c0, c1 = SIDE * side, SIDE * (side + 1)
+            round_z(nc.scalar.copy, z_bf0[:, side], z_first[:, :, c0:c1])
+            quantize_z(0, c0, c1, z_bf0[:, side])
+            for i in ((0,), (1, 2))[side]:
+                second_pass(y_first[i], 0, 0, *RANGES[i], True, False)
+            second_pass(y_second[side], 1, 0, c0, c1, True, False)
+            for n in y_rest:
+                second_pass(y_rest[n], n, 0, c0, c1, side == 0, False)
+            for t in ((2, 3), (0, 1, 2, 3))[side]:
+                merge(z_pieces[side], 1, t, *RANGES[1 + side])
         z_bf10 = tile([P, SIDE, PACK], BF16, "z_bf10")
         round_z(nc.scalar.copy, z_bf10, z_early)
-        quantize_z(1, 0, z_bf10)
-        second_stage(1, 0)
-        for t in range(1, PACK):
-            merge(z_late, 1, t, SIDE, MERGED)
-        z_bf11 = tile([P, SIDE, PACK], BF16, "z_bf11", "z_early")
-        for copy, c0, c1 in ((nc.scalar.copy, 0, SCALAR_LAST), (nc.vector.tensor_copy, SCALAR_LAST, SIDE)):
-            round_z(copy, z_bf11[:, c0:c1, :], z_late[:, :, c0:c1])
-        quantize_z(1, 1, z_bf11)
-        second_stage(1, 1)
+        quantize_z(1, *RANGES[0], z_bf10)
+        z_bf11 = tile([P, PIECE, PACK], BF16, "z_bf11")
+        round_z(nc.scalar.copy, z_bf11, z_pieces[0])
+        finish(y_first[0], 0, *RANGES[0])
+        finish(y_second[0], 1, *RANGES[0])
+        z_bf12 = tile([P, PIECE, PACK], BF16, "z_bf12", "z_early")
+        round_z(nc.vector.tensor_copy, z_bf12, z_pieces[1])
+        quantize_z(1, *RANGES[1], z_bf11)
+        finish(y_first[1], 0, *RANGES[1])
+        quantize_z(1, *RANGES[2], z_bf12)
+        finish(y_first[2], 0, *RANGES[2])
+        finish(y_second[1], 1, SIDE, MERGED)
+        for n in y_rest:
+            finish(y_rest[n], n, 0, MERGED)
 
         first = tile([P, N // P, TERMS], F32, "first")
         second = tile([P, N // P, TERMS], F32, "second")

from contextlib import ExitStack

import concourse.mybir as mybir

K, T, S, MERGED, TERMS, H, N = 1024, 2048, 1024, 512, 256, 1024, 512
FLOPS = 2 * (2 * K * H * S + H * N * MERGED)

F32 = mybir.dt.float32
BF16 = mybir.dt.bfloat16
I32 = mybir.dt.int32
U32 = mybir.dt.uint32
U16 = mybir.dt.uint16
U8 = mybir.dt.uint8
E4M3 = mybir.dt.float8_e4m3fn_x4
E2M1 = mybir.dt.float4_e2m1fn_x4
ADD = mybir.AluOpType.add
MULT = mybir.AluOpType.mult
MAX = mybir.AluOpType.max
SUBTRACT = mybir.AluOpType.subtract
RELU = mybir.ActivationFunctionType.Relu
COPY = mybir.ActivationFunctionType.Copy
IDENTITY = mybir.ActivationFunctionType.Identity

P = 128
PACK = 4
PASS = P * PACK
PASSES = 2
BANK = 512
STAGE1_BANKS = 5
QUADRANTS = 4
DENSE = 32
PER_COLUMN = 16
LINE = 16
SIDE = MERGED // 2
PIECE = SIDE // 2
RANGES = ((0, SIDE), (SIDE, SIDE + PIECE), (SIDE + PIECE, MERGED))
WORDS_PIECE = BANK // 2
WINDOWS = 3 * PACK
WARM_UPS = 4

PART = P // 2
SCALAR_FROM, SCALAR_TO, LAST_FROM = 96, 64, 80
EARLY_ROWS = 2
STORES = ((2, 0, TERMS), (3, 0, TERMS // 2), (3, TERMS // 2, TERMS))
QUARTER = 4 * PACK * PASS
W2_SECOND_AT, GATHERED_AT, W2_CODES_AT, LATE_ROWS_AT, W1_FIRST_AT = 0, 1536, 2048, 4096, 4608
GATHERED_SLOT = 3584
COLUMN = QUARTER // P
W1_SECOND_AT = W1_FIRST_AT + 2 * QUARTER
SHARE_AT = W1_SECOND_AT + COLUMN * SCALAR_FROM
W2_ROWS_AT = W1_SECOND_AT + COLUMN * PART - H // 2
W2_ROWS_SLOT = SHARE_AT + H // 2 - W2_ROWS_AT
LATE_WINDOWS_AT = SHARE_AT + COLUMN * (P - SCALAR_FROM) // 2
LATE_PICKS_AT = LATE_WINDOWS_AT - 4 * PACK * MERGED
TAB_AT = (W1_FIRST_AT + QUARTER, LATE_WINDOWS_AT + 4 * PACK * S)
W1_AT = {(0, 0): W1_FIRST_AT, (1, 0): W1_SECOND_AT, (0, 1): TAB_AT[1], (1, 1): TAB_AT[1] + QUARTER}


def tile_list_curriculum_merger_kernel(
    tc, tab_words, tab_scales, offs, pos1, pos2, pos3, pos4,
    w1, w2_words, w2_scales, w3_words, w3_scales, bias, out,
):
    nc = tc.nc
    with ExitStack() as ctx:
        lists = ctx.enter_context(tc.tile_pool(name="lists", bufs=1))
        keep = ctx.enter_context(tc.tile_pool(name="keep", bufs=1))
        rows = ctx.enter_context(tc.tile_pool(name="rows", bufs=WINDOWS))
        laid = ctx.enter_context(tc.tile_pool(name="laid", bufs=1))
        psum = ctx.enter_context(tc.psum_pool(name="psum", bufs=1))

        def tile(shape, dtype, name, slot=None):
            return keep.tile(shape, dtype, name=name, tag=slot or name, align_bytes=64)[:]

        def tile_at(shape, dtype, name, offset):
            return laid.tile(shape, dtype, name=name, align_bytes=64, offset=offset)[:]

        def load_list(src, name):
            offsets = lists.tile(list(src.shape), U16, name=name)
            nc.sync.dma_start(offsets[:], src)
            return offsets

        w2_rows = tile_at([P, W2_ROWS_SLOT], U8, "w2_rows", W2_ROWS_AT)[:, 0:H]
        tab_rows = tile([P, T], U8, "tab_rows")
        planes = tile([P, PASSES, S + PASS], U8, "planes")
        for dense in (tab_rows, w2_rows):
            nc.gpsimd.memset(dense[32:64, :].bitcast(I32), 0)
            nc.gpsimd.memset(dense[64:128, :].bitcast(I32), 0)
        nc.vector.memset(planes.rearrange("p a c -> p (a c)").bitcast(I32), 0)
        v_planes = planes[:, :, 0:S]
        w2_planes = {0: planes[:, :, S : S + PASS], 1: tile([P, PASSES, PASS], U8, "late_planes")}
        nc.vector.memset(w2_planes[1].rearrange("p a c -> p (a c)").bitcast(I32), 0)

        tab, w2_raw, w1_raw = {}, {}, {}

        def load_tab(a):
            tab[a] = tile_at([P, (a + 1) * T], I32, f"tab{a}", TAB_AT[a])[:, 0:T]
            nc.sync.dma_start(tab[a], tab_words[a].rearrange("p t i -> p (t i)").bitcast(I32))

        def load_w1(a, b, cuts=(0, PART, P)):
            start = cuts[0]
            raw = tile_at(
                [P, PACK * PACK * (cuts[-1] - start)], F32, f"w1_raw{a}{b}_{start}", W1_AT[a, b] + COLUMN * start
            )
            for m0, m1 in zip(cuts, cuts[1:]):
                piece = raw[:, PACK * PACK * (m0 - start) : PACK * PACK * (m1 - start)]
                w1_raw[a, b, m0] = piece.rearrange("p (j c) -> p j c", j=PACK)
                cols = slice(PASS * b + PACK * m0, PASS * b + PACK * m1)
                nc.sync.dma_start(
                    w1_raw[a, b, m0], w1[PASS * a : PASS * (a + 1), cols].rearrange("(p j) c -> p j c", j=PACK)
                )

        nc.sync.dma_start(tab_rows[0:DENSE, :].bitcast(I32), tab_scales.rearrange("a q t -> q a t").bitcast(I32))
        idx = load_list(offs, "idx")
        nc.sync.dma_start(w2_rows[0:DENSE, :].bitcast(I32), w2_scales.rearrange("a q c -> q a c").bitcast(I32))
        load_tab(0)
        w2_raw[0] = tile([P, PASSES, 2 * PASS], U8, "w2_raw0")
        nc.sync.dma_start(w2_raw[0][:, 0, :].bitcast(I32), w2_words[0, :, 0 : 2 * PASS].bitcast(I32))
        p1 = load_list(pos1, "p1")
        p2 = load_list(pos2, "p2")
        p3 = load_list(pos3, "p3")
        p4 = load_list(pos4, "p4")
        load_tab(1)
        nc.sync.dma_start(w2_raw[0][:, 1, :].bitcast(I32), w2_words[1, :, 0 : 2 * PASS].bitcast(I32))

        v_rows = tile_at([P, GATHERED_SLOT], U8, "v_rows", GATHERED_AT)[:, 0:S]
        nc.vector.tensor_copy(v_rows, tab_rows.indirect(idx[:]))
        both_rows = tile([P, S + PASS], U8, "both_rows")

        def reorder_scales(engine, b, dst):
            engine.tensor_copy(
                dst.rearrange("p (t g i) -> p g t i", t=PACK, i=LINE),
                w2_rows[:, PASS * b : PASS * (b + 1)].rearrange("p (g i t) -> p g t i", t=PACK, i=LINE),
            )

        reorder_scales(nc.gpsimd, 0, both_rows[:, S:])
        nc.vector.tensor_copy(both_rows[:, 0:S].bitcast(I32), v_rows.bitcast(I32))

        def spread(dst, dense):
            for quad in (0, 2, 1, 3):
                nc.sync.dma_start(
                    dst[32 * quad : 32 * quad + 4, :, :].bitcast(I32), dense[8 * quad : 8 * quad + 8, :].bitcast(I32)
                )

        spread(planes, both_rows)
        w2_raw[1] = tile_at([P, PASSES, 2 * PASS], U8, "w2_raw1", W2_SECOND_AT)
        nc.sync.dma_start(
            w2_raw[1].bitcast(I32), w2_words[:, :, 2 * PASS : 4 * PASS].rearrange("a p c -> p a c").bitcast(I32)
        )
        load_w1(0, 0)

        v_words, w2_codes, w1_codes, w1_planes, picked, left_rows = {}, {}, {}, {}, {}, {}

        def gather_words(a, h, width=BANK):
            v_words[a, h] = tile([P, BANK], U32, f"v_words{a}{h}")
            for e0 in range(0, BANK, width):
                cols = slice((BANK * h + e0) // PER_COLUMN, (BANK * h + e0 + width) // PER_COLUMN)
                nc.vector.tensor_copy(v_words[a, h][:, e0 : e0 + width], tab[a].bitcast(U32).indirect(idx[:, cols]))

        def w1_views(dst, a, b, m0, m1, walk="p m j t"):
            first = max(m for a1, b1, m in w1_raw if (a1, b1) == (a, b) and m <= m0)
            src = w1_raw[a, b, first].rearrange("p j (m t) -> " + walk, t=PACK)
            return dst[:, :, m0:m1, :].rearrange("p t m j -> " + walk), src[:, m0 - first : m1 - first]

        def round_on_gpsimd(dst, a, b, m0, m1):
            nc.gpsimd.tensor_scalar(*w1_views(dst, a, b, m0, m1), 1.0, 0.0, MULT, ADD)

        def w1_operand(b, slot_of):
            if slot_of is None:
                w1_codes[b] = tile([P, PASSES * PASS], U32, f"w1_codes{b}")
            else:
                w1_codes[b] = tile_at([P, PASSES * PASS], U32, f"w1_codes{b}", W1_AT[slot_of])
            w1_planes[b] = tile([P, PASSES * PASS], U8, f"w1_planes{b}")

        def quantize_w1(b, cols, rounded):
            nc.vector.quantize_mx(out=w1_codes[b][:, cols].bitcast(E4M3), scales=w1_planes[b][:, cols], in_=rounded)

        banks_taken = []

        def next_bank():
            acc = psum.tile([P, BANK], F32, name="acc", tag=f"bank{len(banks_taken) % STAGE1_BANKS}")
            banks_taken.append(acc)
            return acc

        def multiply(acc, codes, plane, a, e0, e1, width):
            for e in range(e0, e1, width):
                nc.tensor.matmul_mx(
                    out=acc[:, e - e0 : e - e0 + width], lhsT=codes(a), lhsT_scale=plane(a),
                    rhs=v_words[a, e // BANK][:, e % BANK : e % BANK + width].bitcast(E4M3),
                    rhs_scale=v_planes[:, a, e : e + width],
                    start=(a == 0 and e == e0), stop=(a == PASSES - 1 and e + width == e1),
                )

        def first_stage(codes, plane, window, halves):
            for h in halves:
                acc = next_bank()
                for a in range(PASSES):
                    multiply(acc, codes, plane, a, BANK * h, BANK * (h + 1), BANK)
                nc.scalar.copy(window[:, BANK * h : BANK * (h + 1)], acc[:])

        def w2_operand(b, t):
            return (
                lambda a: w2_codes[b][:, a, 2 * P * t : 2 * P * (t + 1)].bitcast(E2M1),
                lambda a: w2_planes[b][:, a, P * t : P * (t + 1)],
            )

        def pick(b, t, window):
            if (b, t) not in picked:
                picked[b, t] = tile([P, MERGED], F32, f"picked{b}{t}")
            nc.vector.tensor_copy(picked[b, t], window.indirect(p2[:]))

        def right(b, t):
            window = rows.tile([P, S], F32, name="window")[:]
            first_stage(*w2_operand(b, t), window, range(S // BANK))
            pick(b, t, window)

        def first_two_of_right():
            first_window = rows.tile([P, S], F32, name="window")[:]
            first_stage(*w2_operand(0, 0), first_window, [0])
            pieces = []
            for e0 in range(BANK, S, WORDS_PIECE):
                acc = psum.tile([P, BANK], F32, name="acc", tag=f"bank{STAGE1_BANKS + 1 + len(pieces)}")
                pieces.append((acc, e0, e0 + WORDS_PIECE))
                multiply(acc, *w2_operand(0, 0), 0, e0, e0 + WORDS_PIECE, P)
            opened = next_bank()
            multiply(opened, *w2_operand(0, 1), 0, 0, BANK, BANK)
            for acc, e0, e1 in pieces:
                multiply(acc, *w2_operand(0, 0), 1, e0, e1, P)
                nc.scalar.copy(first_window[:, e0:e1], acc[:, 0:WORDS_PIECE])
            pick(0, 0, first_window)
            second_window = rows.tile([P, S], F32, name="window")[:]
            multiply(opened, *w2_operand(0, 1), 1, 0, BANK, BANK)
            nc.scalar.copy(second_window[:, 0:BANK], opened[:])
            first_stage(*w2_operand(0, 1), second_window, [1])
            pick(0, 1, second_window)

        def left(b, t):
            left_rows[b, t] = rows.tile([P, S], F32, name="window")[:]
            first_stage(
                lambda a: w1_codes[b][:, PASS * a + P * t : PASS * a + P * (t + 1)].bitcast(E4M3),
                lambda a: w1_planes[b][:, PASS * a + P * t : PASS * a + P * (t + 1)],
                left_rows[b, t], range(S // BANK),
            )

        def merge(dst, b, t, c0, c1):
            offsets = p1[:, c0 // PER_COLUMN : c1 // PER_COLUMN]
            nc.vector.tensor_tensor(dst[:, t, :], left_rows[b, t].indirect(offsets), picked[b, t][:, c0:c1], MULT)

        def round_z(copy, rounded, src):
            copy(
                rounded.rearrange("p (g i) t -> p g t i", i=LINE // 4),
                src.rearrange("p t (g i) -> p g t i", i=LINE // 4),
            )

        gather_words(0, 0)
        warm = psum.tile([P, BANK], F32, name="acc", tag=f"bank{STAGE1_BANKS}")
        for warm_up in range(WARM_UPS):
            nc.tensor.matmul_mx(
                out=warm[:], lhsT=w2_raw[0][:, 0, 0 : 2 * P].bitcast(E2M1), lhsT_scale=both_rows[:, S : S + P],
                rhs=v_words[0, 0].bitcast(E4M3), rhs_scale=both_rows[:, 0:BANK], start=True, stop=True,
            )
        w2_codes[0] = tile_at([P, PASSES, 2 * PASS], U8, "w2_codes0", W2_CODES_AT)
        for a in range(PASSES):
            nc.scalar.copy(
                w2_codes[0][:, a, :].bitcast(U16).rearrange("p (t m) -> p m t", t=PACK),
                w2_raw[0][:, a, :].bitcast(U16).rearrange("p (m t) -> p m t", t=PACK),
            )
        late_rows = tile_at([P, PASS], U8, "late_rows", LATE_ROWS_AT)
        reorder_scales(nc.gpsimd, 1, late_rows)
        spread(w2_planes[1], late_rows)
        load_w1(1, 0, (0, PART))
        load_w1(1, 0, (SCALAR_FROM, P))
        load_w1(1, 0, (PART, SCALAR_FROM))
        gather_words(0, 1)
        gather_words(1, 0)
        gather_words(1, 1, WORDS_PIECE)
        load_w1(1, 1, (0, P))
        load_w1(0, 1, (0, LAST_FROM, P))
        w2_codes[1] = tile([P, PASSES, 2 * PASS], U8, "w2_codes1")
        nc.vector.tensor_copy(
            w2_codes[1].bitcast(U16).rearrange("p a (t g i) -> p a g t i", t=PACK, i=LINE // 2),
            w2_raw[1].bitcast(U16).rearrange("p a (g i t) -> p a g t i", t=PACK, i=LINE // 2),
        )

        w1_bf0 = tile([P, PASSES * PACK, P, PACK], BF16, "w1_bf0")
        nc.vector.tensor_copy(*w1_views(w1_bf0[:, 0:PACK], 0, 0, 0, PART))
        round_on_gpsimd(w1_bf0[:, 0:PACK], 0, 0, PART, P)
        first_two_of_right()
        for t in range(2, PACK):
            right(0, t)
        round_on_gpsimd(w1_bf0[:, PACK:], 1, 0, 0, PART)
        round_on_gpsimd(w1_bf0[:, PACK:], 1, 0, PART, SCALAR_FROM)
        nc.scalar.activation(*w1_views(w1_bf0[:, PACK:], 1, 0, SCALAR_FROM, P), COPY)
        w1_operand(0, None)
        quantize_w1(0, slice(0, PASSES * PASS), w1_bf0.rearrange("p t m j -> p (t m j)"))
        w1_bf11 = tile([P, PACK, P, PACK], BF16, "w1_bf11", "w1_bf0")
        round_on_gpsimd(w1_bf11, 1, 1, 0, P)
        late_picks = tile_at([P, PACK, MERGED], F32, "late_picks", LATE_PICKS_AT)
        late_windows = tile_at([P, PACK * S], F32, "late_windows", LATE_WINDOWS_AT)
        for t in range(PACK):
            picked[1, t] = late_picks[:, t, :]
            window = late_windows[:, S * t : S * (t + 1)]
            first_stage(*w2_operand(1, t), window, range(S // BANK))
            pick(1, t, window)
        w1_bf01 = tile([P, PACK, P, PACK], BF16, "w1_bf01", "w2_codes1")
        nc.scalar.activation(*w1_views(w1_bf01, 0, 1, 0, SCALAR_TO), COPY)
        round_on_gpsimd(w1_bf01, 0, 1, SCALAR_TO, LAST_FROM)
        round_on_gpsimd(w1_bf01, 0, 1, LAST_FROM, P)
        w1_operand(1, (0, 1))
        quantize_w1(1, slice(PASS, 2 * PASS), w1_bf11.rearrange("p t m j -> p (t m j)"))
        quantize_w1(1, slice(0, PASS), w1_bf01.rearrange("p t m j -> p (t m j)"))
        z_rows = tile_at([P, SIDE + PACK * MERGED], F32, "z_rows", W1_AT[1, 1])
        z_first = z_rows[:, SIDE:].rearrange("p (t c) -> p t c", t=PACK)
        z_pieces = [
            z_rows[:, PACK * PIECE * i : PACK * PIECE * (i + 1)].rearrange("p (t c) -> p t c", t=PACK) for i in range(2)
        ]
        for t in range(PACK):
            left(0, t)
            merge(z_first, 0, t, 0, MERGED)

        w3_codes = tile([P, PASSES, PACK * N], U8, "w3_codes", "picked00")
        nc.sync.dma_start(w3_codes.bitcast(I32), w3_words.rearrange("b p c i -> p b (c i)").bitcast(I32))
        w3_planes = tile([P, PASSES, N], U8, "w3_planes", "w2_codes1")
        nc.gpsimd.memset(w3_planes.rearrange("p b c -> p (b c)").bitcast(I32), 0)
        for quad in range(QUADRANTS):
            nc.sync.dma_start(
                w3_planes[32 * quad : 32 * quad + 4, :, :].bitcast(I32),
                w3_scales[:, 4 * quad : 4 * quad + 4, :].rearrange("b r c -> r b c").bitcast(I32),
            )
        bias_cols = tile([P, N // P], F32, "bias_cols", "picked01")
        with nc.allow_non_contiguous_dma("one bias value for each partition"):
            nc.sync.dma_start(bias_cols, bias.rearrange("(n p) -> p n", p=P))

        y = [tile([P, MERGED], F32, f"y{n}") for n in range(N // P)]
        z_codes = [tile([P, MERGED], U32, f"z_codes{b}") for b in range(PASSES)]
        z_planes = [tile([P, MERGED], U8, f"z_planes{b}") for b in range(PASSES)]

        def quantize_z(b, c0, c1, rounded):
            nc.vector.quantize_mx(
                out=z_codes[b][:, c0:c1].bitcast(E4M3), scales=z_planes[b][:, c0:c1],
                in_=rounded.rearrange("p c t -> p (c t)"),
            )

        def second_pass(acc, n, b, c0, c1, start, stop):
            nc.tensor.matmul_mx(
                out=acc[:, c0:c1], lhsT=w3_codes[:, b, PACK * P * n : PACK * P * (n + 1)].bitcast(E4M3),
                lhsT_scale=w3_planes[:, b, P * n : P * (n + 1)],
                rhs=z_codes[b][:, c0:c1].bitcast(E4M3), rhs_scale=z_planes[b][:, c0:c1], start=start, stop=stop,
            )

        def finish(acc, n, c0, c1):
            second_pass(acc, n, 1, c0, c1, False, True)
            nc.scalar.activation(y[n][:, c0:c1], acc[:, c0:c1], IDENTITY, bias=bias_cols[:, n : n + 1])

        def bank(index):
            return psum.tile([P, BANK], F32, name="acc", tag=f"bank{index}")[:]

        z_early = tile([P, PACK, SIDE], F32, "z_early")
        for t in range(PACK):
            left(1, t)
            merge(z_early, 1, t, 0, SIDE)
        z_bf0 = tile([P, 2, SIDE, PACK], BF16, "z_bf0", "w1_planes1")
        y_first = [bank(N // P + i) for i in range(len(RANGES))]
        y_second = [bank(1), bank(2 * N // P - 1)]
        y_rest = {n: bank(n) for n in range(2, N // P)}
        for t in range(2):
            merge(z_pieces[0], 1, t, *RANGES[1])
        for side in range(2):
            c0, c1 = SIDE * side, SIDE * (side + 1)
            round_z(nc.scalar.copy, z_bf0[:, side], z_first[:, :, c0:c1])
            quantize_z(0, c0, c1, z_bf0[:, side])
            for i in ((0,), (1, 2))[side]:
                second_pass(y_first[i], 0, 0, *RANGES[i], True, False)
            second_pass(y_second[side], 1, 0, c0, c1, True, False)
            for n in y_rest:
                second_pass(y_rest[n], n, 0, c0, c1, side == 0, False)
            for t in ((2, 3), (0, 1, 2, 3))[side]:
                merge(z_pieces[side], 1, t, *RANGES[1 + side])
        z_bf10 = tile([P, SIDE, PACK], BF16, "z_bf10")
        round_z(nc.scalar.copy, z_bf10, z_early)
        quantize_z(1, *RANGES[0], z_bf10)
        z_bf11 = tile([P, PIECE, PACK], BF16, "z_bf11")
        round_z(nc.scalar.copy, z_bf11, z_pieces[0])
        finish(y_first[0], 0, *RANGES[0])
        finish(y_second[0], 1, *RANGES[0])
        z_bf12 = tile([P, PIECE, PACK], BF16, "z_bf12", "z_early")
        round_z(nc.vector.tensor_copy, z_bf12, z_pieces[1])
        quantize_z(1, *RANGES[1], z_bf11)
        finish(y_first[1], 0, *RANGES[1])
        quantize_z(1, *RANGES[2], z_bf12)
        finish(y_first[2], 0, *RANGES[2])
        finish(y_second[1], 1, SIDE, MERGED)
        for n in y_rest:
            finish(y_rest[n], n, 0, MERGED)

        first = tile([P, N // P, TERMS], F32, "first")
        second = tile([P, N // P, TERMS], F32, "second")
        term = tile([P, N // P, TERMS], F32, "term")
        out_rows = out.rearrange("(n p) t -> p n t", p=P)
        for n in range(EARLY_ROWS):
            nc.vector.tensor_copy(second[:, n, :], y[n].indirect(p4[:]))
        above = tile([P, EARLY_ROWS, TERMS], F32, "above")
        for n in range(EARLY_ROWS):
            nc.vector.tensor_tensor(first[:, n, :], y[n].indirect(p3[:]), second[:, n, :], SUBTRACT)
            nc.scalar.activation(above[:, n, :], first[:, n, :], RELU)
            nc.gpsimd.tensor_tensor(term[:, n, :], above[:, n, :], second[:, n, :], ADD)
            nc.scalar.dma_start(out_rows[:, n, :], term[:, n, :])
        for n, c0, c1 in STORES:
            if c0 == 0:
                nc.vector.tensor_copy(first[:, n, :], y[n].indirect(p3[:]))
            nc.vector.tensor_copy(second[:, n, c0:c1], y[n].indirect(p4[:, c0 // PER_COLUMN : c1 // PER_COLUMN]))
            nc.vector.tensor_tensor(term[:, n, c0:c1], first[:, n, c0:c1], second[:, n, c0:c1], MAX)
            nc.sync.dma_start(out_rows[:, n, c0:c1], term[:, n, c0:c1])
